import numpy as np, ml_dtypes
CORES = [36,164,52,180,100,228,116,244]
N = 8
import mx_ref
BF = ml_dtypes.bfloat16
def gcols(t, e):
    v = np.concatenate([t.reshape(8, 16, -1, 4), np.zeros((8, 16, 1, 4), BF)], axis=2)
    return np.ascontiguousarray(np.stack([v[g][:, e[g]] for g in range(8)])).reshape(128, -1)
def tile(rs):
    return np.stack(rs, axis=2).reshape(128, -1).astype(BF)
def pick(q, e):
    c = np.concatenate([q[0].reshape(128, -1, 4), np.zeros((128, 1, 4), np.uint8)], axis=1); s = np.concatenate([q[1], np.ones((16, 1), np.uint8)], axis=1)
    return (np.ascontiguousarray(c[:, e].reshape(128, -1)), np.ascontiguousarray(s[:, e]))
def join(*qs):
    return (np.concatenate([q[0] for q in qs], axis=1), np.concatenate([q[1] for q in qs], axis=1))
def put(q, e, v):
    c, s = q[0].reshape(128, -1, 4).copy(), q[1].copy(); c[:, e] = v[0].reshape(128, -1, 4); s[:, e] = v[1]
    return (c.reshape(128, -1), s)
def pk(c, s):
    return (np.ascontiguousarray(c), mx_ref.live(s))
def emit(q):
    return q[0], q[1]
def packed(v, rng):
    q = [mx_ref.quantize(np.ascontiguousarray(v[r])) for r in range(N)]
    return np.stack([a for a, b in q]), np.stack([mx_ref.plane(b, rng) for a, b in q])
def values_of_codes():
    e, c = np.zeros((128, 128, 4), np.float32), np.zeros((128, 2, 4), np.uint8)
    e[np.arange(128), np.arange(128), 0] = 1
    c[:127, :, 0] = np.arange(256).reshape(2, 128).T[:127]
    return mx_ref.matmul(mx_ref.quantize(e.reshape(128, 512).astype(BF)), (c.reshape(128, 8), np.full((16, 2), 127, np.uint8))).T.reshape(-1).astype(np.float64)
CODE_VALUE, SCALE_VALUE = values_of_codes(), 2.0 ** (np.arange(256) - 127.0)
def decode(q):
    return (CODE_VALUE[q[0]].reshape(16, 8, -1, 4) * SCALE_VALUE[q[1]][:, None, :, None] + 0.0).reshape(128, -1).astype(np.float32)
def f(rng, *shape):
    return mx_ref.flush((rng.standard_normal(shape, dtype=np.float32) * np.exp2(rng.integers(-2, 3, shape[:-1] + (1,)))).astype(BF))
def wide(rng, *shape, cols=0):
    v = rng.standard_normal(shape, dtype=np.float32) * np.exp2(rng.integers(-12, 13, shape)).astype(np.float32)
    if cols: v *= np.repeat(np.exp2(rng.integers(-cols, cols + 1, shape[:-2] + (1, shape[-1] // 4))) * (rng.random(shape[:-2] + (1, shape[-1] // 4)) > 0.0625), 4, axis=-1).astype(np.float32)
    return mx_ref.flush(v.astype(BF))
C, L, R = 288, 96, 3
def big(v):
    v = v.astype(np.float32)
    v[np.abs(v) < np.float32(2.0 ** -16)] = 0
    return v.astype(BF)
def numbers_of(rng):
    return {"x": big(f(rng, N, 128, 4 * C)), "u": np.array(f(rng, N, 128, 512)), "v": np.array(f(rng, N, 128, 512))}
def layers(rng):
    return big(f(rng, N, 128, 2048)).reshape(N, 8, 16, 4, 8, 16, 4)
def weights(rng, w):
    c, p = packed(np.ascontiguousarray(w).reshape(N, 128, 2048), rng)
    return {"wc": c, "ws": p}
def setup_inputs(rng):
    return {**numbers_of(rng), **weights(rng, layers(rng))}
def setup_inputs_ties(rng):
    d = numbers_of(rng)
    x = d["x"].reshape(N, 8, 16, C, 4)
    x[:, :, 0] = 0
    x[:, :, 0, :, 0] = np.floor(rng.integers(2, 7, (N, 8, 1)) * rng.random((N, 8, C))).astype(np.float32).astype(BF)
    u = d["u"].reshape(N, 128, 128, 4)
    u[:, :, ::16] = 0
    o = rng.permutation(N)
    for r in range(N):
        for h in range(0, 128, 16): u[r, h, h, 0] = 0.0 if r == o[0] else -1.0 if r == o[1] else 1.0
    w = layers(rng)
    w[:, :, :, :, :, 0] = 0
    return {"x": x.reshape(N, 128, 4 * C), "u": u.reshape(N, 128, 512), "v": d["v"], **weights(rng, w)}
def setup_inputs_near(rng):
    d = numbers_of(rng)
    x = d["x"].astype(np.float32).reshape(N, 8, 16, C, 4)
    u = d["u"].reshape(N, 128, 128, 4)
    h = rng.permutation(8)
    o = rng.permutation(N)
    x[:, :, 0] = 0
    x[:, :, 8:] = 0
    u[:, :, ::16] = 0
    for r in range(N):
        k = -1.0 if o[r] % 4 == 3 else 1.0
        for g in h[:4]:
            x[r, g, 0, :, 0] = np.where(rng.random(C) < rng.uniform(0.2, 0.9), 1.0, -1.0)
            s = rng.integers(0, 16 if o[r] % 2 else 8, C)
            x[r, g, 8] = ((s[:, None] >> np.arange(4)) & 1) * np.exp2(np.arange(4) - 23.0)
            x[r, g, 11, :, 0] = 2.0 ** -10
            a, m = 16 * int(g), k if o[r] < N // 2 else k * 2.0 ** -30
            u[r, a, a, 0] = m
            u[r, a + 8, a] = m
            u[r, a + 11, a, 0] = m
        for g in h[4:]:
            x[r, g, 10, :, 0] = (1.0 + 0.125 * rng.integers(0, 8, C)) * 2.0 ** -30
            u[r, 16 * int(g) + 10, 16 * int(g), 0] = k * 2.0 ** -30
        for g in h[6:]: x[r, g, 10, rng.integers(C), 0] = 2.0 ** 29
    w = layers(rng)
    w[:, :, 8:] = 0
    w[:, :, :, :, :, 8:] = 0
    w[:, :, 0] = 0
    w[:, :, :, :, :, 0] = 0
    return {"x": x.reshape(N, 128, 4 * C).astype(BF), "u": u.reshape(N, 128, 512), "v": d["v"], **weights(rng, w)}
def setup_inputs_huge(rng):
    d = numbers_of(rng)
    h = rng.permutation(8)
    o = rng.permutation(N)
    c = rng.integers(0, 2, 8) * 2.0 - 1.0
    x = (0.9 + 0.1 * rng.random((N, 8, 1, C, 1))) * (0.95 + 0.05 * rng.random((N, 8, 16, C, 4))) * c[:, None, None, None]
    x[:, h[4:]] *= rng.choice([-1.0, 1.0], (N, 4, 1, C, 1))
    u = d["u"].reshape(N, 128, 128, 4)
    for r in range(N):
        for g in range(8):
            a = 2.0 ** 30 * (1.0 - 0.1 * rng.random((8, 16, 4))) * c[:, None, None]
            if o[r] % 4 == 0: a = -a
            if o[r] % 4 < 2: a[h[4:]] = 0
            else: a[h[:4]] = 0
            u[r, :, 16 * g] = a.reshape(128, 4).astype(np.float32).astype(BF)
    w = np.zeros((N, 128, 4, 128, 4), np.float32)
    i = np.arange(128)
    for b in range(4): w[:, i, b, i, b] = -1
    return {"x": (2.0 ** 30 * x).astype(np.float32).reshape(N, 128, 4 * C).astype(BF), "u": u.reshape(N, 128, 512), "v": d["v"], **weights(rng, w.astype(BF))}
def setup_inputs_ends(rng):
    d = numbers_of(rng)
    x = d["x"].astype(np.float32).reshape(N, 8, 16, C, 4)
    h = rng.permutation(8)
    e = int(rng.integers(N))
    x[:, :, 0] = 0
    for g in range(8):
        p = rng.permutation(N)
        if g in h[:4]: p[(e + np.arange(N)) % N] = np.concatenate([[0, 1, N - 1, N - 2], 2 + rng.permutation(N - 4)])
        x[:, g, 0, :, 0] = np.exp2(p)[:, None] * (1.0 + 0.125 * rng.integers(0, 8, (N, C)))
    m = int(h[7])
    k = np.repeat(np.arange(4.0), [L // 4, L - L // 4, L, C - 2 * L])
    for r in range(N):
        j = rng.permutation(C)
        x[r, m, 0, j] = -np.exp2(k)[:, None]
        x[r, m, 0, j, r % 4] = np.exp2(4.0 - k)
        x[r, m, 0, j[C - 1], r % 4] = -1.5
    s = (N, 8, 8, C, 4)
    x[:, :, 8:] = rng.choice([-1.0, 1.0], s) * (1.0 + (2 * rng.integers(0, 64, s) + 1) * 0.0078125) * np.exp2(rng.integers(-14, -7, s))
    x[:, :, 8, :, 0] = rng.choice([-1.96875, 1.96875], (N, 8, C))
    u = d["u"].reshape(N, 128, 128, 4)
    u[:, :, ::16] = 0
    for a in range(0, 128, 16): u[:, a, a, 0] = 1
    for r in range(N):
        u[r, 16 * m, 16 * m, 0] = 0
        u[r, 16 * m, 16 * m, r % 4] = 1
    w = layers(rng)
    w[:, :, 0] = 0
    w[:, :, :, :, :, 0] = 0
    return {"x": x.reshape(N, 128, 4 * C).astype(BF), "u": u.reshape(N, 128, 512), "v": d["v"], **weights(rng, w)}
def setup_inputs_spread(rng):
    d = setup_inputs(rng)
    d["x"] = big(wide(rng, N, 128, 4 * C, cols=6))
    return d
def check_inputs(d):
    b = []
    for k in ("x", "u", "v"):
        a = np.abs(d[k].astype(np.float32))
        if not (np.isfinite(a).all() and ((a == 0) | (a >= 2.0 ** -30) & (a <= 2.0 ** 30)).all()): b.append("a value of " + k)
    none, least, most = [emit(mx_ref.quantize(np.full((128, 16), k, np.float32).astype(BF)))[1][0, 0] for k in (0.0, 2.0 ** -30, 2.0 ** 30)]
    for r in range(N):
        if ((d["wc"][r] == 0x7F) | (d["wc"][r] == 0xFF)).any(): b.append("wc: a code that is no number")
        s = mx_ref.live(d["ws"][r])
        if ((s != none) & ((s < least) | (s > most))).any(): b.append("ws: a scale out of range")
    return b
def reference(x, u, v, wc, ws):
    qu = [mx_ref.quantize(u[r]) for r in range(N)]
    lay = [pk(wc[r], ws[r]) for r in range(N)]
    now = [x[r] for r in range(N)]
    ls = np.zeros((N, 8, C + 2 * L), np.float32)
    for t in range(R):
        order, kept, gone = [], [], []
        for r in range(N):
            s = mx_ref.matmul(qu[r], mx_ref.quantize(now[r]))[::16] + np.float32(0.0)
            o = np.argsort(-s, axis=1, kind="stable")
            order.append(o)
            kept.append(np.take_along_axis(s, o[:, L:], axis=1))
            gone.append(mx_ref.quantize(gcols(now[r], o[:, :L])))
        came = [decode(gone[r]).astype(BF) for r in range(N)]
        final = []
        for r in range(N):
            said = []
            for e in ((r + 1) % N, (r + 2) % N):
                a = mx_ref.matmul(qu[e], gone[r])[::16] + np.float32(0.0)
                said.append(np.count_nonzero(kept[e][:, None, :] > a[:, :, None], axis=2))
            final.append(np.maximum(said[0], said[1]))
        made = []
        for r in range(N):
            lo, hi = sorted([(r - 1) % N, (r - 2) % N])
            place = np.concatenate([order[r][:, L:], np.tile(C + np.arange(2 * L), (8, 1))], axis=1)
            key = np.concatenate([np.tile(np.arange(C - L), (8, 1)), final[lo], final[hi]], axis=1)
            l = np.take_along_axis(place, np.argsort(key, axis=1, kind="stable")[:, :C], axis=1)
            ls[r] = np.concatenate([l, final[lo], final[hi]], axis=1)
            a = np.concatenate([now[r], came[lo], came[hi]], axis=1)
            before = np.concatenate([l[:, :1], l[:, :-1]], axis=1)
            z = ((gcols(a, l).astype(np.float32) + gcols(a, before).astype(np.float32)) * np.float32(0.5)).astype(BF)
            q = mx_ref.quantize(z)
            made.append(tile([mx_ref.matmul(pick(lay[r], np.arange(128 * b, 128 * b + 128)), q) * np.float32(0.03125) + z[:, b::4].astype(np.float32) for b in range(4)]))
        now = made
    y = np.zeros((N, 128, C), np.float32)
    oc, osc = np.zeros((N, 128, 4 * C), np.uint8), np.zeros((N, 16, C), np.uint8)
    for r in range(N):
        q = mx_ref.quantize(now[r])
        y[r] = mx_ref.matmul(mx_ref.quantize(v[r]), q)
        oc[r], osc[r] = emit(q)
    return {"y": y, "ls": ls, "oc": oc, "osc": osc}

@@ -1,0 +1,511 @@
+from concourse.bass import DstId, RemoteDMATransfer
+from concourse.mybir import dt, AluOpType as Op, ActivationFunctionType as AF
+
+C, L, R = 288, 96, 3
+BIG = 1.0e29
+F8, U8, BF, F32, I32, U16 = "float8_e4m3fn_x4", "uint8", "bfloat16", "float32", "int32", "uint16"
+GW = 304
+EW = 520
+TW = [288, 224, 160, 128, 128]
+
+
+def _sb(n, d):
+    return ("sbuf", [128, n], d)
+
+
+SCRATCH = {
+    "xt": _sb(4 * C, BF), "ut": _sb(512, BF), "vt": _sb(512, BF), "xn": _sb(4 * C, BF),
+    "qx": _sb(C, F8), "sx": _sb(C, U8), "qu": _sb(128, F8), "su": _sb(128, U8), "qv": _sb(128, F8), "sv": _sb(128, U8),
+    "qw": _sb(512, F8), "sw": _sb(512, U8),
+    "qur": _sb(128, F8), "sur": _sb(128, U8), "quc": _sb(32, F8), "suc": _sb(32, U8),
+    "qul": _sb(64, F8), "sul": _sb(64, U8), "qu2": _sb(256, F8), "su2": _sb(256, U8),
+    "pi": _sb(2, I32), "ti": _sb(6, I32), "pf": _sb(8, F32), "li": _sb(64, I32), "lst": _sb(64, U16),
+    "la": _sb(8, U16), "lb": _sb(8, U16), "lc": _sb(2, U16),
+    "km": _sb(C, BF), "eqm": _sb(C, BF), "mb": _sb(C, BF), "mi": _sb(C, BF), "kk": _sb(C, BF), "kz": _sb(C, BF),
+    "c16": _sb(18, F32), "cc": _sb(18, F32), "ja": _sb(12, F32), "jv": _sb(C, F32), "idn": _sb(192, F32), "ngn": _sb(192, BF),
+    "obi": _sb(512, BF), "obt": _sb(512, BF), "qob": _sb(128, F8), "sob": _sb(128, U8),
+    "one": _sb(EW, BF), "et": _sb(2 * EW, BF), "qe": _sb(512, F8), "se": _sb(512, U8),
+    "mm": _sb(C, F32), "hh": _sb(C, F32), "sga": _sb(6 * 272, BF),
+    "rs": _sb(18 * 88, F32), "rsd": _sb(C, BF), "u1": _sb(18, F32), "rs2": _sb(18, F32), "ext": _sb(C, F32),
+    "rkf": _sb(18, F32), "rko": _sb(18, U16), "cm": _sb(384, F32), "ex2": _sb(C, F32), "oro": _sb(18, U16),
+    "xp": _sb(4 * C, BF), "at": _sb(512, BF), "vp": _sb(4 * 384, BF), "gp": _sb(4 * GW, BF),
+    "zt": _sb(4 * C, BF), "zp": _sb(4 * C, BF), "qz": _sb(C, F8), "sz": _sb(C, U8),
+    "ma": _sb(192, F32), "ha": _sb(192, F32), "rep": _sb(2 * C, F32), "pb": _sb(2 * C, BF), "sgp": _sb(2 * C, BF),
+    "jkp": _sb(4 * C, BF), "tt0": _sb(150, F32), "p1": _sb(6 * 144, BF), "f0": _sb(6, F32),
+    "ee": _sb(384, BF), "r2": _sb(384, BF), "kys": _sb(192, F32), "ka": _sb(12, F32), "b2": _sb(12, F32),
+    "kb": _sb(384, BF), "jkq": _sb(7 * 192, BF), "rk": _sb(12 * 96, F32), "plf": _sb(12, F32), "plo": _sb(12, U16),
+    "ww": _sb(384, BF), "flg": _sb(C, BF), "st": _sb(C, BF), "exw": _sb(C, F32), "exs": _sb(C, BF),
+    "wa": _sb(18, F32), "lf": _sb(18, F32), "lo": _sb(18, U16), "lsb": _sb(480, F32), "yb": _sb(C, F32),
+    "hs": _sb(20 * R, F32), "qa": _sb(128 * R, F8), "sa": _sb(128 * R, U8), "ql": _sb(192 * R, F8), "sl": _sb(192 * R, U8),
+    "fm": _sb(8 * R, BF), "fl": _sb(16 * R, BF), "sc": ("dram", [2 * R, 128, 18], F32),
+    "ps0": ("psum", [128, 512], F32), "ps1": ("psum", [128, 512], F32), "pc": ("psum", [128, 512], F32),
+    "pr": ("psum", [128, 2048], F32),
+}
+for _a in range(5):
+    SCRATCH["bt%d" % _a] = _sb(4 * TW[_a], BF)
+    SCRATCH["qb%d" % _a] = _sb(TW[_a], F8)
+    SCRATCH["sb%d" % _a] = _sb(TW[_a], U8)
+
+SEMAPHORES = ["cv", "ca", "cp", "cg", "ldx", "ldu", "ldw", "sent", "uarr", "sty", "stz", "sto", "stl"]
+for _r in range(R):
+    SEMAPHORES += ["%s%d" % (_n, _r) for _n in ("qarr", "farr", "sca", "scb", "rpa", "rpb")]
+
+
+def rank_program(g, core, T, topo):
+    rank = T.rank_of(core)
+    if rank is None:
+        return
+    N = len(T.cores)
+    Q = {"v": g.vector, "a": g.scalar, "p": g.tensor, "g": g, "s": g.sync}
+    own = {"v": "cv", "a": "ca", "p": "cp", "g": "cg"}
+    clock = {e: {} for e in Q}
+    count = {}
+    waited = {}
+    wr, rd = {}, {}
+
+    def need(e, rec):
+        sem, val, snap = rec[0], rec[1], rec[2]
+        if clock[e].get(sem, 0) < val:
+            Q[e].wait_ge(T.sem[sem], val)
+            waited[sem] = max(waited.get(sem, 0), val)
+            clock[e][sem] = val
+        for k, x in snap.items():
+            if clock[e].get(k, 0) < x:
+                clock[e][k] = x
+
+    def before(e, reads, writes):
+        recs = []
+        for k in reads:
+            if k in wr:
+                recs.append(wr[k])
+            if k.startswith("P:"):
+                recs += [x for x in rd.get(k, []) if x[3] != e]
+        for k in writes:
+            if k in wr and not (e == "p" and wr[k][3] == "p"):
+                recs.append(wr[k])
+            recs += rd.get(k, [])
+        recs.sort(key=lambda x: -x[1])
+        for x in recs:
+            need(e, x)
+
+    def after(rec, reads, writes):
+        for k in reads:
+            rd.setdefault(k, []).append(rec)
+        for k in writes:
+            wr[k] = rec
+            rd[k] = []
+
+    def op(e, fn, reads, writes):
+        before(e, reads, writes)
+        s = own[e]
+        count[s] = count.get(s, 0) + 1
+        fn().then_inc(T.sem[s], 1)
+        after((s, count[s], dict(clock[e]), e), reads, writes)
+
+    def dmas(e, sem, pairs, reads, writes):
+        before(e, reads, writes)
+        for o, i in pairs:
+            count[sem] = count.get(sem, 0) + 16
+            Q[e].dma_start(o, i).then_inc(T.sem[sem], 16)
+        after((sem, count[sem], dict(clock[e]), "d"), reads, writes)
+
+    def arrives(sem, n, writes):
+        count[sem] = n
+        after((sem, n, {}, "r"), [], writes)
+
+    def send(items, reads):
+        before("g", reads, [])
+        tr = []
+        for k, (d, src, dst, sem) in enumerate(items):
+            c = T.cores[d]
+            eng = topo.engines(core, c)
+            w = len(eng) // len(items)
+            rid, pid = topo.addr(c, core)
+            tr.append(RemoteDMATransfer(dst_ids=[DstId(rid=rid, pnc=pid)], dma_engine_mask=sum(1 << x for x in eng[k * w:(k + 1) * w]),
+                                        remote_sem=T.sem[sem], src=src, dst=dst))
+            count["sent"] = count.get("sent", 0) + w
+        g.remote_dma_fused(tr, local_sem=T.sem.sent)
+
+    def share(s, n):
+        return len(topo.engines(T.cores[s], core)) // n
+
+    V, A, PE = g.vector, g.scalar, g.tensor
+
+    def ts(out, in0, s1, s2, o0, o1, reads, writes):
+        if s2 is None:
+            op("v", lambda: V.tensor_scalar(out, in0, s1, None, o0), reads, writes)
+        else:
+            op("v", lambda: V.tensor_scalar(out, in0, s1, s2, o0, o1), reads, writes)
+
+    def tt(out, a, b, o, reads, writes):
+        op("v", lambda: V.tensor_tensor(out, a, b, o), reads, writes)
+
+    def cp(out, a, reads, writes):
+        op("v", lambda: V.tensor_copy(out, a), reads, writes)
+
+    def ms(ap, val, writes):
+        op("v", lambda: V.memset(ap, val), [], writes)
+
+    def scan(out, d0, d1, init, o0, o1, reads, writes):
+        op("v", lambda: V.tensor_tensor_scan(out, d0, d1, init, o0, o1), reads, writes)
+
+    def qz(q, s, t, reads, writes):
+        op("v", lambda: V.quantize_mx(q, s, t), reads, writes)
+
+    def mx(out, wq, ws_, xq, xs, start, stop, reads, writes):
+        op("p", lambda: PE.matmul_mx(out, wq, ws_, xq, xs, start, stop), reads, writes)
+
+    def act(out, in_, f, reads, writes, **kw):
+        op("a", lambda: A.activation(out, in_, f, **kw), reads, writes)
+
+    def iota(out, pat, cmul, writes, flt=False):
+        if flt:
+            op("g", lambda: g.iota(out, pat, 0, cmul, allow_small_or_imprecise_dtypes=True), [], writes)
+        else:
+            op("g", lambda: g.iota(out, pat, 0, cmul), [], writes)
+
+    rcv = [(rank + 1) % N, (rank + 2) % N]
+    snd = [(rank - 1) % N, (rank - 2) % N]
+
+    def slot_at(d):
+        return 0 if rank == min((d - 1) % N, (d - 2) % N) else 1
+
+    def xplane(t):
+        act(T.xp[:, C * t:C * t + C], T.xt[:, t:4 * C:4], AF.Copy, ["xt"], ["xp.%d" % t], scale=32.0)
+
+    dmas("a", "ldu", [(T.ut[:], T.u[:])], [], ["ut"])
+    dmas("s", "ldx", [(T.xt[:], T.x[:])], [], ["xt"])
+    dmas("s", "ldw", [(T.qw[:].bitcast(dt.uint8), T.wc[:]), (T.sw[:], T.ws[:]), (T.vt[:], T.v[:])], ["xt"], ["qw", "vt"])
+    iota(T.li[:, 0:8], [[16, 8]], 0, ["li.a"])
+    iota(T.pi[:], [[0, 2]], 1, ["pi"])
+    iota(T.km[:], [[0, 18], [1, 16]], 0, ["km"], True)
+    iota(T.c16[:], [[16, 18]], 0, ["c16"], True)
+    iota(T.obi[:], [[1, 8], [0, 64]], 0, ["obi"], True)
+    ms(T.kk[:], BIG, ["kk"])
+    ms(T.kz[:], 1.0, ["kz"])
+    ms(T.bt0[:, 4 * 240:], 0.0, ["bt0.0", "bt0.1", "bt0.2", "bt0.3"])
+    ms(T.kk[:, 0:C:16], -BIG, ["kk"])
+    ms(T.kz[:, 0:C:16], 0.0, ["kz"])
+    cp(T.la[:], T.li[:, 0:8], ["li.a"], ["la"])
+    ts(T.ti[:, 0:1], T.pi[:, 0:1], 15, None, Op.bitwise_and, None, ["pi"], ["ti.0"])
+    ts(T.ti[:, 1:2], T.pi[:, 0:1], 31, None, Op.bitwise_and, None, ["pi"], ["ti.1"])
+    ts(T.ti[:, 2:3], T.pi[:, 0:1], 4, None, Op.logical_shift_right, None, ["pi"], ["ti.2"])
+    ts(T.ti[:, 4:6], T.pi[:], 7, None, Op.bitwise_and, None, ["pi"], ["ti.3"])
+    for a, lo_ in ((1, 176), (2, 112)):
+        ms(T["bt%d" % a][:, 4 * lo_:], 0.0, ["bt%d.%d" % (a, t) for t in range(4)])
+    cp(T.pf[:, 0:3], T.ti[:, 0:3], ["ti.0", "ti.1", "ti.2"], ["pf"])
+    ts(T.lc[:], T.ti[:, 4:6], 16.0, None, Op.mult, None, ["ti.3"], ["lc"])
+    for a, lo_ in ((3, 48), (4, 0)):
+        ms(T["bt%d" % a][:, 4 * lo_:], 0.0, ["bt%d.%d" % (a, t) for t in range(4)])
+    ts(T.eqm[:], T.km[:], T.pf[:, 0:1], None, Op.is_equal, None, ["km", "pf"], ["eqm"])
+    ts(T.pf[:, 4:5], T.pf[:, 0:1], -1024.0, 15360.0, Op.mult, Op.add, ["pf"], ["pf.q"])
+    ts(T.pf[:, 5:6], T.pf[:, 0:1], -1025.0, 15375.0, Op.mult, Op.add, ["pf"], ["pf.q2"])
+    ms(T.rs[:, 87:88], 0.0, ["rs.0"])
+    ts(T.mb[:], T.eqm[:], 2.0 * BIG, -BIG, Op.mult, Op.add, ["eqm"], ["mb"])
+    ms(T.at[:, 4 * L:], 0.0, ["at.z"])
+    qz(T.qu[:], T.su[:], T.ut[:], ["ut"], ["qu"])
+    ts(T.cc[:], T.c16[:], T.pf[:, 5:6], None, Op.add, None, ["c16", "pf.q2"], ["cc"])
+    act(T.suc[:], T.su[:].indirect(T.lc[:]), AF.Copy, ["qu", "lc"], ["suc"])
+    act(T.sur[:], T.su[:].indirect(T.la[:]), AF.Copy, ["qu", "la"], ["sur"])
+    cp(T.quc[:].bitcast(dt.uint32), T.qu[:].bitcast(dt.uint32).indirect(T.lc[:]), ["qu", "lc"], ["quc"])
+    cp(T.qur[:].bitcast(dt.uint32), T.qu[:].bitcast(dt.uint32).indirect(T.la[:]), ["qu", "la"], ["qur"])
+    items = []
+    for e in range(2):
+        items.append((snd[e], T.quc[:, 0:8].bitcast(dt.uint8), T.qul[:, 32 * e:32 * e + 8].bitcast(dt.uint8), "uarr"))
+        items.append((snd[e], T.suc[:], T.sul[:, 32 * e:32 * e + 32], "uarr"))
+    send(items, ["quc", "suc"])
+    arrives("uarr", 2 * share(rcv[0], 4) + 2 * share(rcv[1], 4), ["qul"])
+    qz(T.qx[:], T.sx[:], T.xt[:], ["xt"], ["qx"])
+    ts(T.obt[:], T.obi[:], T.pf[:, 2:3], None, Op.is_equal, None, ["obi", "pf"], ["obt"])
+    for t in range(3):
+        xplane(t)
+
+    for r in range(R):
+        first, last = r == 0, r == R - 1
+        hs, fm, fl = T.hs[:, 20 * r:20 * r + 18], T.fm[:, 8 * r:8 * r + 6], T.fl[:, 16 * r:16 * r + 12]
+        qa, sa = T.qa[:, 128 * r:128 * r + 128], T.sa[:, 128 * r:128 * r + 128]
+        ql, sl = T.ql[:, 192 * r:192 * r + 192], T.sl[:, 192 * r:192 * r + 192]
+        mx(T.ps0[:, 0:C], T.qur[:], T.sur[:], T.qx[:], T.sx[:], True, True, ["qur", "sur", "qx"], ["P:0"])
+        mx(T.ps1[:, 0:C], T.qur[:], T.sur[:], T.qx[:], T.sx[:], True, True, ["qur", "sur", "qx"], ["P:1"])
+        S0, S1 = T.ps0, T.ps1
+        tt(T.mm[:, 192:C], S0[:, 192:C], T.mb[:, 192:C], Op.min, ["P:0", "mb"], ["mm.b"])
+        tt(T.mm[:, 0:192], S0[:, 0:192], T.mb[:, 0:192], Op.min, ["P:0", "mb"], ["mm.a"])
+        scan(T.hh[:, 192:C], T.kk[:, 192:C], T.mm[:, 192:C], 0.0, Op.min, Op.max, ["kk", "mm.b"], ["hh.b"])
+        scan(T.hh[:, 0:192], T.kk[:, 0:192], T.mm[:, 0:192], 0.0, Op.min, Op.max, ["kk", "mm.a"], ["hh.a"])
+        if first:
+            qz(T.qob[:], T.sob[:], T.obt[:], ["obt"], ["qob"])
+        cp(hs, T.hh[:, 15:C:16], ["hh.a", "hh.b"], ["hs%d" % r])
+        send([(snd[e], hs, T.sc[2 * r + e], "%s%d" % (("sca", "scb")[e], r)) for e in range(2)], ["hs%d" % r])
+
+        def spread(e, q):
+            arrives("%s%d" % (("sca", "scb")[e], r), share(rcv[e], 2), ["sc%d.%d" % (r, e)])
+            dmas(q, "%s%d" % (("rpa", "rpb")[e], r), [(T.rep[i:128:16, C * e:C * e + C], T.sc[2 * r + e]) for i in range(16)],
+                 ["sc%d.%d" % (r, e)], ["rep.%d" % e])
+
+        spread(0, "s")
+        if first:
+            iota(T.jv[:], [[1, C]], 0, ["jv"], True)
+            iota(T.li[:, 10:18], [[1, 8]], 0, ["li.b"])
+            iota(T.li[:, 26:50], [[1, 12], [0, 2]], 0, ["li.d"])
+            iota(T.li[:, 50:62], [[32, 12]], 0, ["li.e"])
+
+        def lane(c):
+            n = 18 - c
+            return n // 4, n % 4
+
+        def lview(c, a, b):
+            t, k = lane(c)
+            return T["bt%d" % t][:, 4 * a + k:4 * b:4]
+
+        def lname(c):
+            return "bt%d.%d" % lane(c)
+
+        def quant(t):
+            qz(T["qb%d" % t][:], T["sb%d" % t][:], T["bt%d" % t][:], ["bt%d.%d" % (t, k) for k in range(4)], ["qb%d" % t])
+
+        def sums(t, start, stop):
+            mx(T.pc[:, 0:TW[t]], T.qob[:], T.sob[:], T["qb%d" % t][:], T["sb%d" % t][:], start, stop, ["qob", "qb%d" % t], ["P:c"])
+
+        def p1(c):
+            o = 272 * (17 - c)
+            act(T.sga[:, o:o + 16 * c], S1[:, 0:16 * c], AF.Sign, ["P:1", "hh.b"], ["sga.%d" % c], bias=T.hh[:, 16 * c + 15:16 * c + 16], scale=-1.0)
+
+        def p2(c):
+            o = 272 * (17 - c)
+            act(lview(c, 0, 16 * c), T.sga[:, o:o + 16 * c], AF.Relu, ["sga.%d" % c], [lname(c), "rs.%d" % c],
+                accum_out=T.rs[:, 88 * c + 87:88 * c + 88])
+
+        p1(17)
+        for c in range(16, 11, -1):
+            p1(c)
+            p2(c + 1)
+        p2(12)
+        if first:
+            xplane(3)
+        spread(1, "a")
+
+        def bits(c):
+            ts(lview(c, 0, 16 * c), S0[:, 0:16 * c], T.hh[:, 16 * c + 15:16 * c + 16], None, Op.is_lt, None, ["P:0", "hh.a"], [lname(c)])
+
+        def rsum(c):
+            scan(T.rs[:, 88 * c + 88 - 8 * c:88 * c + 88], lview(c, 0, 8 * c), lview(c, 8 * c, 16 * c), 0.0, Op.add, Op.add,
+                 [lname(c)], ["rs.%d" % c])
+
+        tt(T.bt0[:, 0:4 * C:4], S0[:, 0:C], T.hh[:], Op.is_le, ["P:0", "hh.a", "hh.b"], ["bt0.0"])
+        for c in (10, 9, 8, 7, 6):
+            bits(c)
+        quant(2)
+        for c in (5, 4, 3, 2):
+            bits(c)
+        quant(3)
+        bits(1)
+        bits(11)
+        scan(T.rsd[:], T.kz[:], T.bt0[:, 0:4 * C:4], 0.0, Op.mult, Op.add, ["kz", "bt0.0"], ["rsd"])
+        quant(4)
+        quant(0)
+        sums(0, True, False)
+        sums(2, False, False)
+        sums(3, False, False)
+        sums(4, False, False)
+        if first:
+            ts(T.mi[:], T.eqm[:], 1049600.0, -1024.0, Op.mult, Op.add, ["eqm"], ["mi"])
+            ms(T.one[:], 1.0, ["one"])
+            for h in range(2):
+                op("g", lambda: g.affine_select(T.et[:, EW * h:EW * h + EW], T.one[:], [[1, EW]], Op.is_equal, 0.0, -2 - h, -4), ["one"], ["et.%d" % h])
+        for c in (11, 10, 9, 8, 7):
+            rsum(c)
+        tt(T.u1[:], T.rsd[:, 15:C:16], T.cc[:], Op.subtract, ["rsd", "cc"], ["u1"])
+        for c in (6, 5, 4):
+            rsum(c)
+        quant(1)
+        sums(1, False, True)
+        for c in (3, 2, 1):
+            rsum(c)
+        if first:
+            cp(T.lb[:], T.li[:, 10:18], ["li.b"], ["lb"])
+        tt(T.rs2[:], T.rs[:, 87:18 * 88:88], T.u1[:], Op.add, ["rs.%d" % c for c in range(18)] + ["u1"], ["rs2"])
+        scan(T.ext[:], T.mi[:], T.pc[:, 0:C], 0.0, Op.add, Op.min, ["mi", "P:c"], ["ext"])
+        tt(T.rkf[:], T.ext[:, 15:C:16], T.rs2[:], Op.subtract, ["ext", "rs2"], ["rkf"])
+        cp(T.rko[:], T.rkf[:], ["rkf"], ["rko"])
+        cp(T.cm[:, 96:384].indirect(T.rko[:]), T.jv[:], ["rko", "jv"], ["cm"])
+        scan(T.ex2[:, 0:L], T.mi[:, 0:L], T.cm[:, 96:192], 0.0, Op.add, Op.min, ["mi", "cm"], ["ex2.a"])
+        ts(T.oro[:, 0:6], T.ex2[:, 15:L:16], T.pf[:, 4:5], None, Op.add, None, ["ex2.a", "pf.q"], ["oro.a"])
+        for t in range(4):
+            win = T.xp[:, C * t:C * t + C].indirect(T.oro[:, 0:6])
+            if t < 2:
+                ts(T.at[:, t:4 * L:4], win, 2.0 ** -5, None, Op.mult, None, ["xp.%d" % t, "oro.a"], ["at.%d" % t])
+            else:
+                act(T.at[:, t:4 * L:4], win, AF.Copy, ["xp.%d" % t, "oro.a"], ["at.%d" % t], scale=2.0 ** -5)
+        qz(qa, sa, T.at[:], ["at.z", "at.0", "at.1", "at.2", "at.3"], ["qa%d" % r])
+        at_ = {d: 192 * r + L * slot_at(d) for d in rcv}
+        send([(d, T.qa[:, 128 * r:128 * r + L].bitcast(dt.uint8), T.ql[:, at_[d]:at_[d] + L].bitcast(dt.uint8), "qarr%d" % r) for d in rcv], ["qa%d" % r])
+        send([(d, T.sa[:, 128 * r:128 * r + L], T.sl[:, at_[d]:at_[d] + L], "qarr%d" % r) for d in rcv], ["qa%d" % r])
+        arrives("qarr%d" % r, 2 * share(snd[0], 2) + 2 * share(snd[1], 2), ["ql%d" % r])
+        for e in range(2):
+            o = 128 * e
+            if first:
+                act(T.su2[:, o:o + 128], T.sul[:, 32 * e:32 * e + 8].indirect(T.lb[:]), AF.Copy, ["qul", "lb"], ["su2.%d" % e])
+                cp(T.qu2[:, o:o + 128].bitcast(dt.uint32), T.qul[:, 32 * e:32 * e + 8].bitcast(dt.uint32).indirect(T.lb[:]), ["qul", "lb"], ["qu2.%d" % e])
+            mx((T.ps0, T.ps1)[e][:, 0:128], T.qu2[:, o:o + 128], T.su2[:, o:o + 128], qa, sa, True, True,
+               ["qu2.%d" % e, "su2.%d" % e, "qa%d" % r], ["P:%d" % e])
+        scan(T.ex2[:, L:C], T.mi[:, L:C], T.cm[:, 192:384], 0.0, Op.add, Op.min, ["mi", "cm"], ["ex2.b"])
+        for e in range(2):
+            tt(T.ma[:, L * e:L * e + L], (T.ps0, T.ps1)[e][:, 0:L], T.mb[:, 0:L], Op.min, ["P:%d" % e, "mb"], ["ma.%d" % e])
+        for e in range(2):
+            scan(T.ha[:, L * e:L * e + L], T.kk[:, 0:L], T.ma[:, L * e:L * e + L], 0.0, Op.min, Op.max, ["kk", "ma.%d" % e], ["ha.%d" % e])
+
+        def a1(c):
+            o = C * (c % 2)
+            act(T.sgp[:, o:o + C], T.rep[:, 0:C], AF.Sign, ["rep.0", "ha.0"], ["sgp.%d" % (c % 2)], bias=T.ha[:, 16 * c + 15:16 * c + 16], scale=-1.0)
+
+        def a2(c):
+            o = C * (c % 2)
+            act(T.jkp[:, C * (c - 2):C * (c - 1)], T.sgp[:, o:o + C], AF.Relu, ["sgp.%d" % (c % 2)], ["tt0.%d" % c], scale=-1.0,
+                accum_out=T.tt0[:, 143 + c:144 + c])
+
+        a1(2)
+        for c in range(3, 6):
+            a1(c)
+            a2(c - 1)
+        a2(5)
+        cols = [(0, 1), (0, 0)] + [(1, c) for c in range(6)]
+
+        def vb(k):
+            e, c = cols[k]
+            o = C * (k % 2)
+            ts(T.pb[:, o:o + C], T.rep[:, C * e:C * e + C], T.ha[:, L * e + 16 * c + 15:L * e + 16 * c + 16], None, Op.is_gt, None,
+               ["rep.%d" % e, "ha.%d" % e], ["pb.%d" % (k % 2)])
+
+        def vs(k):
+            e, c = cols[k]
+            o = C * (k % 2)
+            if e == 0:
+                scan(T.tt0[:, c:144 + c], T.pb[:, o:o + 144], T.pb[:, o + 144:o + C], 0.0, Op.add, Op.add, ["pb.%d" % (k % 2)],
+                     ["tt0.0", "tt0.1"][:c + 1])
+            else:
+                scan(T.p1[:, 144 * c:144 * c + 144], T.pb[:, o:o + 144], T.pb[:, o + 144:o + C], -96.0, Op.add, Op.add,
+                     ["pb.%d" % (k % 2)], ["p1.%d" % c])
+
+        vb(0)
+        for k in range(1, 8):
+            vb(k)
+            vs(k - 1)
+        ts(T.f0[:], T.tt0[:, 143:149], -96.0, 0.0, Op.add, Op.max, ["tt0.%d" % c for c in range(6)], ["f0"])
+        vs(7)
+        tt(fm, T.f0[:], T.p1[:, 143:6 * 144:144], Op.max, ["f0"] + ["p1.%d" % c for c in range(6)], ["fm%d" % r])
+        send([(d, fm, T.fl[:, 16 * r + 6 * slot_at(d):16 * r + 6 * slot_at(d) + 6], "farr%d" % r) for d in rcv], ["fm%d" % r])
+        arrives("farr%d" % r, share(snd[0], 2) + share(snd[1], 2), ["fl%d" % r])
+
+        ts(T.oro[:, 6:18], T.ex2[:, L + 15:C:16], T.pf[:, 4:5], None, Op.add, None, ["ex2.b", "pf.q"], ["oro.b"])
+        if first:
+            for b in range(4):
+                o = EW * (b % 2) + 2 - 2 * (b // 2)
+                qz(T.qe[:, 128 * b:128 * b + 128], T.se[:, 128 * b:128 * b + 128], T.et[:, o:o + 512], ["et.%d" % (b % 2)], ["qe.%d" % b])
+            cp(T.lst[:, 26:50], T.li[:, 26:50], ["li.d"], ["lst.d"])
+            ts(T.lst[:, 50:62], T.li[:, 50:62], T.pf[:, 1:2], None, Op.add, None, ["li.e", "pf"], ["lst.e"])
+            ts(T.ja[:], T.c16[:, 0:12], T.pf[:, 0:1], 1.0 / 256, Op.add, Op.mult, ["c16", "pf"], ["ja"])
+            ts(T.idn[:], T.jv[:, 0:192], 1.0 / 256, None, Op.mult, None, ["jv"], ["idn"])
+            ts(T.ngn[:], T.jv[:, 0:192], -191.0, None, Op.add, None, ["jv"], ["ngn"])
+        for t in range(4):
+            win = T.xp[:, C * t:C * t + C].indirect(T.oro[:, 6:18])
+            o = T.vp[:, 384 * t + 192:384 * t + 384]
+            if t < (1 if first else 2):
+                ts(o, win, 2.0 ** -6, None, Op.mult, None, ["xp.%d" % t, "oro.b"], ["vp.s%d" % t])
+            else:
+                act(o, win, AF.Copy, ["xp.%d" % t, "oro.b"], ["vp.s%d" % t], scale=2.0 ** -6)
+        ms(T.ww[:], 256.0, ["ww"])
+        if last:
+            ts(T.cm[:, 0:192], T.jv[:, 0:192], 288.0, None, Op.add, None, ["jv"], ["cm"])
+            qz(T.qv[:], T.sv[:], T.vt[:], ["vt"], ["qv"])
+        cp(T.gp[:, 0:4 * GW:GW], T.vp[:, 192:4 * 384:384], ["vp.s%d" % t for t in range(4)], ["gp.z"])
+        for b in range(4):
+            mx(T.pr[:, 512 * b:512 * b + 192], T.qe[:, 128 * b:128 * b + 128], T.se[:, 128 * b:128 * b + 128], ql, sl, True, True,
+               ["qe.%d" % b, "ql%d" % r], ["P:r%d" % b])
+        for b in range(4):
+            o, i = T.vp[:, 384 * b:384 * b + 192], T.pr[:, 512 * b:512 * b + 192]
+            if b % 2:
+                ts(o, i, 0.5, None, Op.mult, None, ["P:r%d" % b], ["vp.d%d" % b])
+            else:
+                act(o, i, AF.Copy, ["P:r%d" % b], ["vp.d%d" % b], scale=0.5)
+
+        fn_ = "fl%d" % r
+        act(T.ee[:, 192:384], fl.indirect(T.lst[:, 38:50]), AF.Copy, [fn_, "lst.d"], ["ee.1"])
+        cp(T.ee[:, 0:192], fl.indirect(T.lst[:, 26:38]), [fn_, "lst.d"], ["ee.0"])
+        tt(T.ka[:], fl, T.ja[:], Op.add, [fn_, "ja"], ["ka"])
+        op("v", lambda: V.transpose(T.r2[:], T.ee[:]), ["ee.0", "ee.1"], ["r2"])
+        ts(T.b2[:], fl, 191.0, 2.0, Op.min, Op.mult, [fn_], ["b2"])
+        tt(T.kys[:], T.r2[:].indirect(T.lst[:, 50:62]), T.idn[:], Op.add, ["r2", "lst.e", "idn"], ["kys"])
+        for c in range(5, 12):
+            act(T.jkq[:, 192 * (c - 5):192 * (c - 4)], T.kys[:], AF.Sign, ["kys", "ka"], ["rk.%d" % c], bias=T.ka[:, c:c + 1], scale=-1.0,
+                accum_out=T.rk[:, 96 * c + 95:96 * c + 96])
+        if last:
+            act(T.lsb[:, C:480], T.r2[:].indirect(T.lst[:, 50:62]), AF.Copy, ["r2", "lst.e"], ["lsb.b"])
+
+        def kb(c):
+            o = 192 * (c % 2)
+            ts(T.kb[:, o:o + 192], T.kys[:], T.ka[:, c:c + 1], 2.0, Op.is_lt, Op.mult, ["kys", "ka"], ["kb.%d" % (c % 2)])
+
+        def ks(c):
+            o = 192 * (c % 2)
+            scan(T.rk[:, 96 * c:96 * c + 96], T.kb[:, o:o + 96], T.kb[:, o + 96:o + 192], -191.0, Op.add, Op.add, ["kb.%d" % (c % 2)], ["rk.%d" % c])
+
+        kb(0)
+        for c in range(1, 5):
+            kb(c)
+            ks(c - 1)
+        ks(4)
+        tt(T.plf[:], T.rk[:, 95:12 * 96:96], T.b2[:], Op.add, ["rk.%d" % c for c in range(12)] + ["b2"], ["plf"])
+        ts(T.plo[:], T.plf[:], 193.0, 0.5, Op.add, Op.mult, ["plf"], ["plo"])
+        cp(T.ww[:].indirect(T.plo[:]), T.ngn[:], ["plo", "ngn"], ["ww"])
+        ts(T.flg[:], T.ww[:, 0:C], 0.0, None, Op.is_gt, None, ["ww"], ["flg"])
+        scan(T.exw[:], T.mi[:], T.ww[:, 0:C], 0.0, Op.add, Op.min, ["mi", "ww"], ["exw"])
+        scan(T.st[:], T.flg[:], T.flg[:], 0.0, Op.add, Op.max, ["flg"], ["st"])
+        ts(T.wa[:], T.exw[:, 15:C:16], T.pf[:, 4:5], None, Op.add, None, ["exw", "pf.q"], ["wa"])
+        scan(T.exs[:], T.mb[:], T.st[:], 0.0, Op.max, Op.min, ["mb", "st"], ["exs"])
+        tt(T.lf[:], T.wa[:], T.exs[:, 15:C:16], Op.min, ["wa", "exs"], ["lf"])
+        ts(T.lo[:], T.lf[:], 191.0, None, Op.add, None, ["lf"], ["lo"])
+        for t in (1, 2, 3, 0):
+            win = T.vp[:, 384 * t:384 * t + 384].indirect(T.lo[:])
+            o = T.gp[:, GW * t + 1:GW * t + 1 + C]
+            if t:
+                act(o, win, AF.Copy, ["vp.s%d" % t, "vp.d%d" % t, "lo"], ["gp.%d" % t])
+            else:
+                cp(o, win, ["vp.s%d" % t, "vp.d%d" % t, "lo"], ["gp.%d" % t])
+        for t in range(4):
+            tt(T.zt[:, t:4 * C:4], T.gp[:, GW * t + 1:GW * t + 1 + C], T.gp[:, GW * t:GW * t + C], Op.add, ["gp.%d" % t, "gp.z"], ["zt.%d" % t])
+        qz(T.qz[:], T.sz[:], T.zt[:], ["zt.%d" % t for t in range(4)], ["qz"])
+        for b in range(4):
+            mx(T.pr[:, 512 * b:512 * b + C], T.qw[:, 128 * b:128 * b + 128], T.sw[:, 128 * b:128 * b + 128], T.qz[:], T.sz[:], True, True,
+               ["qw", "qz"], ["P:r%d" % b])
+        for t in range(4):
+            o, i = T.zp[:, C * t:C * t + C], T.zt[:, t:4 * C:4]
+            if t < 2:
+                act(o, i, AF.Copy, ["zt.%d" % t], ["zp.%d" % t], scale=32.0)
+            else:
+                ts(o, i, 32.0, None, Op.mult, None, ["zt.%d" % t], ["zp.%d" % t])
+        if last:
+            act(T.lsb[:, 0:C], T.cm[:].indirect(T.lo[:]), AF.Copy, ["cm", "lo"], ["lsb.a"])
+            dmas("s", "stl", [(T.ls[:], T.lsb[0:128:16, :])], ["lsb.a", "lsb.b"], [])
+        for b in range(4):
+            tt(T.xp[:, C * b:C * b + C], T.pr[:, 512 * b:512 * b + C], T.zp[:, C * b:C * b + C], Op.add, ["P:r%d" % b, "zp.%d" % b], ["xp.%d" % b])
+            o, i = T.xn[:, b:4 * C:4], T.xp[:, C * b:C * b + C]
+            if b < 3:
+                act(o, i, AF.Copy, ["xp.%d" % b], ["xn.%d" % b], scale=2.0 ** -5)
+            else:
+                ts(o, i, 2.0 ** -5, None, Op.mult, None, ["xp.%d" % b], ["xn.%d" % b])
+        qz(T.qx[:], T.sx[:], T.xn[:], ["xn.%d" % b for b in range(4)], ["qx"])
+
+    H = C // 2
+    mx(T.ps1[:, 0:H], T.qv[:], T.sv[:], T.qx[:, H:C], T.sx[:, H:C], True, True, ["qv", "qx"], ["P:1"])
+    mx(T.pc[:, 0:H], T.qv[:], T.sv[:], T.qx[:, 0:H], T.sx[:, 0:H], True, True, ["qv", "qx"], ["P:c"])
+    dmas("s", "sto", [(T.oc[:], T.qx[:].bitcast(dt.uint8))] + [(T.osc[4 * k:4 * k + 4, :], T.sx[32 * k:32 * k + 4, :]) for k in range(4)], ["qx"], [])
+    act(T.yb[:, H:C], T.ps1[:, 0:H], AF.Copy, ["P:1"], ["yb.1"])
+    dmas("a", "stz", [(T.y[:, H:C], T.yb[:, H:C])], ["yb.1"], [])
+    cp(T.yb[:, 0:H], T.pc[:, 0:H], ["P:c"], ["yb.0"])
+    dmas("s", "sty", [(T.y[:, 0:H], T.yb[:, 0:H])], ["yb.0"], [])
+    stores = ("stl", "sto", "stz", "sty")
+    for s in SEMAPHORES:
+        if count.get(s, 0) > waited.get(s, 0) and s not in stores:
+            g.wait_ge(T.sem[s], count[s])
+    for s in stores:
+        g.wait_ge(T.sem[s], count[s])

@@ -25,21 +25,21 @@ SCRATCH = {
     "c16": _sb(18, F32), "cc": _sb(18, F32), "ja": _sb(12, F32), "jv": _sb(C, F32), "idn": _sb(192, F32), "ngn": _sb(192, BF),
     "obi": _sb(512, BF), "obt": _sb(512, BF), "qob": _sb(128, F8), "sob": _sb(128, U8),
     "one": _sb(EW, BF), "et": _sb(2 * EW, BF), "qe": _sb(512, F8), "se": _sb(512, U8),
-    "mm": _sb(C, F32), "hh": _sb(C, F32), "sga": _sb(6 * 272, BF),
+    "mm": _sb(C, F32), "hh": _sb(C, F32), "sga": _sb(6 * 272, BF), "jka": _sb(6 * 96, BF),
     "rs": _sb(18 * 88, F32), "rsd": _sb(C, BF), "u1": _sb(18, F32), "rs2": _sb(18, F32), "ext": _sb(C, F32),
     "rkf": _sb(18, F32), "rko": _sb(18, U16), "cm": _sb(384, F32), "ex2": _sb(C, F32), "oro": _sb(18, U16),
     "xp": _sb(4 * C, BF), "at": _sb(512, BF), "vp": _sb(4 * 384, BF), "gp": _sb(4 * GW, BF),
     "zt": _sb(4 * C, BF), "zp": _sb(4 * C, BF), "qz": _sb(C, F8), "sz": _sb(C, U8),
-    "ma": _sb(192, F32), "ha": _sb(192, F32), "rep": _sb(2 * C, F32), "pb": _sb(2 * C, BF), "sgp": _sb(2 * C, BF),
+    "ma": _sb(192, F32), "ha": _sb(192, F32), "rep": _sb(2 * C, F32), "pb": _sb(8 * C, BF), "sgp": _sb(4 * C, BF),
     "jkp": _sb(4 * C, BF), "tt0": _sb(150, F32), "p1": _sb(6 * 144, BF), "f0": _sb(6, F32),
     "ee": _sb(384, BF), "r2": _sb(384, BF), "kys": _sb(192, F32), "ka": _sb(12, F32), "b2": _sb(12, F32),
-    "kb": _sb(384, BF), "jkq": _sb(7 * 192, BF), "rk": _sb(12 * 96, F32), "plf": _sb(12, F32), "plo": _sb(12, U16),
+    "kb": _sb(5 * 192, BF), "jkq": _sb(7 * 192, BF), "rk": _sb(12 * 96, F32), "plf": _sb(12, F32), "plo": _sb(12, U16),
     "ww": _sb(384, BF), "flg": _sb(C, BF), "st": _sb(C, BF), "exw": _sb(C, F32), "exs": _sb(C, BF),
     "wa": _sb(18, F32), "lf": _sb(18, F32), "lo": _sb(18, U16), "lsb": _sb(480, F32), "yb": _sb(C, F32),
     "hs": _sb(20 * R, F32), "qa": _sb(128 * R, F8), "sa": _sb(128 * R, U8), "ql": _sb(192 * R, F8), "sl": _sb(192 * R, U8),
     "fm": _sb(8 * R, BF), "fl": _sb(16 * R, BF), "sc": ("dram", [2 * R, 128, 18], F32),
-    "ps0": ("psum", [128, 512], F32), "ps1": ("psum", [128, 512], F32), "pc": ("psum", [128, 512], F32),
-    "pr": ("psum", [128, 2048], F32),
+    "ps0": ("psum", [128, 512], F32), "ps1": ("psum", [128, 512], F32), "ps2": ("psum", [128, 512], F32),
+    "pc": ("psum", [128, 512], F32), "pr": ("psum", [128, 2048], F32),
 }
 for _a in range(5):
     SCRATCH["bt%d" % _a] = _sb(4 * TW[_a], BF)
@@ -173,6 +173,10 @@ def rank_program(g, core, T, topo):
     def xplane(t):
         act(T.xp[:, C * t:C * t + C], T.xt[:, t:4 * C:4], AF.Copy, ["xt"], ["xp.%d" % t], scale=32.0)
 
+    def qx_of(t, reads):
+        qz(T.qx[:, 160:C], T.sx[:, 160:C], t[:, 640:4 * C], reads, ["qx.b"])
+        qz(T.qx[:, 0:160], T.sx[:, 0:160], t[:, 0:640], reads, ["qx.a"])
+
     dmas("a", "ldu", [(T.ut[:], T.u[:])], [], ["ut"])
     dmas("s", "ldx", [(T.xt[:], T.x[:])], [], ["xt"])
     dmas("s", "ldw", [(T.qw[:].bitcast(dt.uint8), T.wc[:]), (T.sw[:], T.ws[:]), (T.vt[:], T.v[:])], ["xt"], ["qw", "vt"])
@@ -181,9 +185,10 @@ def rank_program(g, core, T, topo):
     iota(T.km[:], [[0, 18], [1, 16]], 0, ["km"], True)
     iota(T.c16[:], [[16, 18]], 0, ["c16"], True)
     iota(T.obi[:], [[1, 8], [0, 64]], 0, ["obi"], True)
+    iota(T.li[:, 10:18], [[1, 8]], 0, ["li.b"])
     ms(T.kk[:], BIG, ["kk"])
     ms(T.kz[:], 1.0, ["kz"])
-    ms(T.bt0[:, 4 * 240:], 0.0, ["bt0.0", "bt0.1", "bt0.2", "bt0.3"])
+    ms(T.bt0[:, 4 * 240:], 0.0, ["bt0.0", "bt0.1", "bt0.2", "bt0.3", "bt0.d"])
     ms(T.kk[:, 0:C:16], -BIG, ["kk"])
     ms(T.kz[:, 0:C:16], 0.0, ["kz"])
     cp(T.la[:], T.li[:, 0:8], ["li.a"], ["la"])
@@ -203,6 +208,7 @@ def rank_program(g, core, T, topo):
     ms(T.rs[:, 87:88], 0.0, ["rs.0"])
     ts(T.mb[:], T.eqm[:], 2.0 * BIG, -BIG, Op.mult, Op.add, ["eqm"], ["mb"])
     ms(T.at[:, 4 * L:], 0.0, ["at.z"])
+    ts(T.mi[:], T.eqm[:], 1049600.0, -1024.0, Op.mult, Op.add, ["eqm"], ["mi"])
     qz(T.qu[:], T.su[:], T.ut[:], ["ut"], ["qu"])
     ts(T.cc[:], T.c16[:], T.pf[:, 5:6], None, Op.add, None, ["c16", "pf.q2"], ["cc"])
     act(T.suc[:], T.su[:].indirect(T.lc[:]), AF.Copy, ["qu", "lc"], ["suc"])
@@ -215,7 +221,8 @@ def rank_program(g, core, T, topo):
         items.append((snd[e], T.suc[:], T.sul[:, 32 * e:32 * e + 32], "uarr"))
     send(items, ["quc", "suc"])
     arrives("uarr", 2 * share(rcv[0], 4) + 2 * share(rcv[1], 4), ["qul"])
-    qz(T.qx[:], T.sx[:], T.xt[:], ["xt"], ["qx"])
+    ms(T.one[:], 1.0, ["one"])
+    qx_of(T.xt, ["xt"])
     ts(T.obt[:], T.obi[:], T.pf[:, 2:3], None, Op.is_equal, None, ["obi", "pf"], ["obt"])
     for t in range(3):
         xplane(t)
@@ -225,12 +232,14 @@ def rank_program(g, core, T, topo):
         hs, fm, fl = T.hs[:, 20 * r:20 * r + 18], T.fm[:, 8 * r:8 * r + 6], T.fl[:, 16 * r:16 * r + 12]
         qa, sa = T.qa[:, 128 * r:128 * r + 128], T.sa[:, 128 * r:128 * r + 128]
         ql, sl = T.ql[:, 192 * r:192 * r + 192], T.sl[:, 192 * r:192 * r + 192]
-        mx(T.ps0[:, 0:C], T.qur[:], T.sur[:], T.qx[:], T.sx[:], True, True, ["qur", "sur", "qx"], ["P:0"])
-        mx(T.ps1[:, 0:C], T.qur[:], T.sur[:], T.qx[:], T.sx[:], True, True, ["qur", "sur", "qx"], ["P:1"])
+        mx(T.ps2[:, 0:128], T.qur[:], T.sur[:], T.qx[:, 160:C], T.sx[:, 160:C], True, True, ["qur", "sur", "qx.b"], ["P:2"])
+        mx(T.ps0[:, 0:C], T.qur[:], T.sur[:], T.qx[:], T.sx[:], True, True, ["qur", "sur", "qx.a", "qx.b"], ["P:0"])
+        mx(T.ps1[:, 0:C], T.qur[:], T.sur[:], T.qx[:], T.sx[:], True, True, ["qur", "sur", "qx.a", "qx.b"], ["P:1"])
         S0, S1 = T.ps0, T.ps1
-        tt(T.mm[:, 192:C], S0[:, 192:C], T.mb[:, 192:C], Op.min, ["P:0", "mb"], ["mm.b"])
-        tt(T.mm[:, 0:192], S0[:, 0:192], T.mb[:, 0:192], Op.min, ["P:0", "mb"], ["mm.a"])
+        tt(T.mm[:, 192:C], T.ps2[:, 32:128], T.mb[:, 192:C], Op.min, ["P:2", "mb"], ["mm.b"])
         scan(T.hh[:, 192:C], T.kk[:, 192:C], T.mm[:, 192:C], 0.0, Op.min, Op.max, ["kk", "mm.b"], ["hh.b"])
+        tt(T.mm[:, 0:192], S0[:, 0:192], T.mb[:, 0:192], Op.min, ["P:0", "mb"], ["mm.a"])
+        tt(T.bt0[:, 4 * 192:4 * C:4], S0[:, 192:C], T.hh[:, 192:C], Op.is_le, ["P:0", "hh.b"], ["bt0.d"])
         scan(T.hh[:, 0:192], T.kk[:, 0:192], T.mm[:, 0:192], 0.0, Op.min, Op.max, ["kk", "mm.a"], ["hh.a"])
         if first:
             qz(T.qob[:], T.sob[:], T.obt[:], ["obt"], ["qob"])
@@ -245,9 +254,10 @@ def rank_program(g, core, T, topo):
         spread(0, "s")
         if first:
             iota(T.jv[:], [[1, C]], 0, ["jv"], True)
-            iota(T.li[:, 10:18], [[1, 8]], 0, ["li.b"])
             iota(T.li[:, 26:50], [[1, 12], [0, 2]], 0, ["li.d"])
             iota(T.li[:, 50:62], [[32, 12]], 0, ["li.e"])
+            for h in range(2):
+                op("g", lambda: g.affine_select(T.et[:, EW * h:EW * h + EW], T.one[:], [[1, EW]], Op.is_equal, 0.0, -2 - h, -4), ["one"], ["et.%d" % h])
 
         def lane(c):
             n = 18 - c
@@ -261,7 +271,7 @@ def rank_program(g, core, T, topo):
             return "bt%d.%d" % lane(c)
 
         def quant(t):
-            qz(T["qb%d" % t][:], T["sb%d" % t][:], T["bt%d" % t][:], ["bt%d.%d" % (t, k) for k in range(4)], ["qb%d" % t])
+            qz(T["qb%d" % t][:], T["sb%d" % t][:], T["bt%d" % t][:], ["bt%d.%d" % (t, k) for k in range(4)] + ["bt%d.d" % t], ["qb%d" % t])
 
         def sums(t, start, stop):
             mx(T.pc[:, 0:TW[t]], T.qob[:], T.sob[:], T["qb%d" % t][:], T["sb%d" % t][:], start, stop, ["qob", "qb%d" % t], ["P:c"])
@@ -280,9 +290,6 @@ def rank_program(g, core, T, topo):
             p1(c)
             p2(c + 1)
         p2(12)
-        if first:
-            xplane(3)
-        spread(1, "a")
 
         def bits(c):
             ts(lview(c, 0, 16 * c), S0[:, 0:16 * c], T.hh[:, 16 * c + 15:16 * c + 16], None, Op.is_lt, None, ["P:0", "hh.a"], [lname(c)])
@@ -291,40 +298,40 @@ def rank_program(g, core, T, topo):
             scan(T.rs[:, 88 * c + 88 - 8 * c:88 * c + 88], lview(c, 0, 8 * c), lview(c, 8 * c, 16 * c), 0.0, Op.add, Op.add,
                  [lname(c)], ["rs.%d" % c])
 
-        tt(T.bt0[:, 0:4 * C:4], S0[:, 0:C], T.hh[:], Op.is_le, ["P:0", "hh.a", "hh.b"], ["bt0.0"])
+        tt(T.bt0[:, 0:4 * 192:4], S0[:, 0:192], T.hh[:, 0:192], Op.is_le, ["P:0", "hh.a"], ["bt0.0"])
         for c in (10, 9, 8, 7, 6):
             bits(c)
         quant(2)
         for c in (5, 4, 3, 2):
             bits(c)
-        quant(3)
         bits(1)
+        quant(3)
         bits(11)
-        scan(T.rsd[:], T.kz[:], T.bt0[:, 0:4 * C:4], 0.0, Op.mult, Op.add, ["kz", "bt0.0"], ["rsd"])
+        scan(T.rsd[:], T.kz[:], T.bt0[:, 0:4 * C:4], 0.0, Op.mult, Op.add, ["kz", "bt0.0", "bt0.d"], ["rsd"])
         quant(4)
         quant(0)
         sums(0, True, False)
         sums(2, False, False)
         sums(3, False, False)
         sums(4, False, False)
+        for c in range(6, 0, -1):
+            act(T.jka[:, 96 * c - 96:96 * c - 96 + 16 * c], lview(c, 0, 16 * c), AF.Copy, [lname(c)], ["rs.%d" % c],
+                accum_out=T.rs[:, 88 * c + 87:88 * c + 88])
         if first:
-            ts(T.mi[:], T.eqm[:], 1049600.0, -1024.0, Op.mult, Op.add, ["eqm"], ["mi"])
-            ms(T.one[:], 1.0, ["one"])
-            for h in range(2):
-                op("g", lambda: g.affine_select(T.et[:, EW * h:EW * h + EW], T.one[:], [[1, EW]], Op.is_equal, 0.0, -2 - h, -4), ["one"], ["et.%d" % h])
-        for c in (11, 10, 9, 8, 7):
-            rsum(c)
-        tt(T.u1[:], T.rsd[:, 15:C:16], T.cc[:], Op.subtract, ["rsd", "cc"], ["u1"])
-        for c in (6, 5, 4):
+            xplane(3)
+            cp(T.lb[:], T.li[:, 10:18], ["li.b"], ["lb"])
+            for e in range(2):
+                act(T.su2[:, 128 * e:128 * e + 128], T.sul[:, 32 * e:32 * e + 8].indirect(T.lb[:]), AF.Copy, ["qul", "lb"], ["su2.%d" % e])
+        spread(1, "a")
+        for c in (11, 10):
             rsum(c)
         quant(1)
         sums(1, False, True)
-        for c in (3, 2, 1):
+        for c in (9, 8, 7):
             rsum(c)
-        if first:
-            cp(T.lb[:], T.li[:, 10:18], ["li.b"], ["lb"])
-        tt(T.rs2[:], T.rs[:, 87:18 * 88:88], T.u1[:], Op.add, ["rs.%d" % c for c in range(18)] + ["u1"], ["rs2"])
+        tt(T.u1[:], T.rsd[:, 15:C:16], T.cc[:], Op.subtract, ["rsd", "cc"], ["u1"])
         scan(T.ext[:], T.mi[:], T.pc[:, 0:C], 0.0, Op.add, Op.min, ["mi", "P:c"], ["ext"])
+        tt(T.rs2[:], T.rs[:, 87:18 * 88:88], T.u1[:], Op.add, ["rs.%d" % c for c in range(18)] + ["u1"], ["rs2"])
         tt(T.rkf[:], T.ext[:, 15:C:16], T.rs2[:], Op.subtract, ["ext", "rs2"], ["rkf"])
         cp(T.rko[:], T.rkf[:], ["rkf"], ["rko"])
         cp(T.cm[:, 96:384].indirect(T.rko[:]), T.jv[:], ["rko", "jv"], ["cm"])
@@ -344,7 +351,6 @@ def rank_program(g, core, T, topo):
         for e in range(2):
             o = 128 * e
             if first:
-                act(T.su2[:, o:o + 128], T.sul[:, 32 * e:32 * e + 8].indirect(T.lb[:]), AF.Copy, ["qul", "lb"], ["su2.%d" % e])
                 cp(T.qu2[:, o:o + 128].bitcast(dt.uint32), T.qul[:, 32 * e:32 * e + 8].bitcast(dt.uint32).indirect(T.lb[:]), ["qul", "lb"], ["qu2.%d" % e])
             mx((T.ps0, T.ps1)[e][:, 0:128], T.qu2[:, o:o + 128], T.su2[:, o:o + 128], qa, sa, True, True,
                ["qu2.%d" % e, "su2.%d" % e, "qa%d" % r], ["P:%d" % e])
@@ -355,12 +361,12 @@ def rank_program(g, core, T, topo):
             scan(T.ha[:, L * e:L * e + L], T.kk[:, 0:L], T.ma[:, L * e:L * e + L], 0.0, Op.min, Op.max, ["kk", "ma.%d" % e], ["ha.%d" % e])
 
         def a1(c):
-            o = C * (c % 2)
-            act(T.sgp[:, o:o + C], T.rep[:, 0:C], AF.Sign, ["rep.0", "ha.0"], ["sgp.%d" % (c % 2)], bias=T.ha[:, 16 * c + 15:16 * c + 16], scale=-1.0)
+            o = C * (c - 2)
+            act(T.sgp[:, o:o + C], T.rep[:, 0:C], AF.Sign, ["rep.0", "ha.0"], ["sgp.%d" % c], bias=T.ha[:, 16 * c + 15:16 * c + 16], scale=-1.0)
 
         def a2(c):
-            o = C * (c % 2)
-            act(T.jkp[:, C * (c - 2):C * (c - 1)], T.sgp[:, o:o + C], AF.Relu, ["sgp.%d" % (c % 2)], ["tt0.%d" % c], scale=-1.0,
+            o = C * (c - 2)
+            act(T.jkp[:, o:o + C], T.sgp[:, o:o + C], AF.Relu, ["sgp.%d" % c], ["tt0.%d" % c], scale=-1.0,
                 accum_out=T.tt0[:, 143 + c:144 + c])
 
         a1(2)
@@ -372,31 +378,31 @@ def rank_program(g, core, T, topo):
 
         def vb(k):
             e, c = cols[k]
-            o = C * (k % 2)
+            o = C * k
             ts(T.pb[:, o:o + C], T.rep[:, C * e:C * e + C], T.ha[:, L * e + 16 * c + 15:L * e + 16 * c + 16], None, Op.is_gt, None,
-               ["rep.%d" % e, "ha.%d" % e], ["pb.%d" % (k % 2)])
+               ["rep.%d" % e, "ha.%d" % e], ["pb.%d" % k])
 
         def vs(k):
             e, c = cols[k]
-            o = C * (k % 2)
+            o = C * k
             if e == 0:
-                scan(T.tt0[:, c:144 + c], T.pb[:, o:o + 144], T.pb[:, o + 144:o + C], 0.0, Op.add, Op.add, ["pb.%d" % (k % 2)],
+                scan(T.tt0[:, c:144 + c], T.pb[:, o:o + 144], T.pb[:, o + 144:o + C], 0.0, Op.add, Op.add, ["pb.%d" % k],
                      ["tt0.0", "tt0.1"][:c + 1])
             else:
                 scan(T.p1[:, 144 * c:144 * c + 144], T.pb[:, o:o + 144], T.pb[:, o + 144:o + C], -96.0, Op.add, Op.add,
-                     ["pb.%d" % (k % 2)], ["p1.%d" % c])
+                     ["pb.%d" % k], ["p1.%d" % c])
 
         vb(0)
         for k in range(1, 8):
             vb(k)
             vs(k - 1)
-        ts(T.f0[:], T.tt0[:, 143:149], -96.0, 0.0, Op.add, Op.max, ["tt0.%d" % c for c in range(6)], ["f0"])
         vs(7)
+        ts(T.f0[:], T.tt0[:, 143:149], -96.0, 0.0, Op.add, Op.max, ["tt0.%d" % c for c in range(6)], ["f0"])
+        ts(T.oro[:, 6:18], T.ex2[:, L + 15:C:16], T.pf[:, 4:5], None, Op.add, None, ["ex2.b", "pf.q"], ["oro.b"])
         tt(fm, T.f0[:], T.p1[:, 143:6 * 144:144], Op.max, ["f0"] + ["p1.%d" % c for c in range(6)], ["fm%d" % r])
         send([(d, fm, T.fl[:, 16 * r + 6 * slot_at(d):16 * r + 6 * slot_at(d) + 6], "farr%d" % r) for d in rcv], ["fm%d" % r])
         arrives("farr%d" % r, share(snd[0], 2) + share(snd[1], 2), ["fl%d" % r])
 
-        ts(T.oro[:, 6:18], T.ex2[:, L + 15:C:16], T.pf[:, 4:5], None, Op.add, None, ["ex2.b", "pf.q"], ["oro.b"])
         if first:
             for b in range(4):
                 o = EW * (b % 2) + 2 - 2 * (b // 2)
@@ -442,12 +448,12 @@ def rank_program(g, core, T, topo):
             act(T.lsb[:, C:480], T.r2[:].indirect(T.lst[:, 50:62]), AF.Copy, ["r2", "lst.e"], ["lsb.b"])
 
         def kb(c):
-            o = 192 * (c % 2)
-            ts(T.kb[:, o:o + 192], T.kys[:], T.ka[:, c:c + 1], 2.0, Op.is_lt, Op.mult, ["kys", "ka"], ["kb.%d" % (c % 2)])
+            o = 192 * c
+            ts(T.kb[:, o:o + 192], T.kys[:], T.ka[:, c:c + 1], 2.0, Op.is_lt, Op.mult, ["kys", "ka"], ["kb.%d" % c])
 
         def ks(c):
-            o = 192 * (c % 2)
-            scan(T.rk[:, 96 * c:96 * c + 96], T.kb[:, o:o + 96], T.kb[:, o + 96:o + 192], -191.0, Op.add, Op.add, ["kb.%d" % (c % 2)], ["rk.%d" % c])
+            o = 192 * c
+            scan(T.rk[:, 96 * c:96 * c + 96], T.kb[:, o:o + 96], T.kb[:, o + 96:o + 192], -191.0, Op.add, Op.add, ["kb.%d" % c], ["rk.%d" % c])
 
         kb(0)
         for c in range(1, 5):
@@ -464,15 +470,13 @@ def rank_program(g, core, T, topo):
         scan(T.exs[:], T.mb[:], T.st[:], 0.0, Op.max, Op.min, ["mb", "st"], ["exs"])
         tt(T.lf[:], T.wa[:], T.exs[:, 15:C:16], Op.min, ["wa", "exs"], ["lf"])
         ts(T.lo[:], T.lf[:], 191.0, None, Op.add, None, ["lf"], ["lo"])
-        for t in (1, 2, 3, 0):
-            win = T.vp[:, 384 * t:384 * t + 384].indirect(T.lo[:])
-            o = T.gp[:, GW * t + 1:GW * t + 1 + C]
-            if t:
-                act(o, win, AF.Copy, ["vp.s%d" % t, "vp.d%d" % t, "lo"], ["gp.%d" % t])
-            else:
-                cp(o, win, ["vp.s%d" % t, "vp.d%d" % t, "lo"], ["gp.%d" % t])
+        act(T.gp[:, 161:1 + C], T.vp[:, 0:384].indirect(T.lo[:, 10:18]), AF.Copy, ["vp.s0", "vp.d0", "lo"], ["gp.h"])
+        cp(T.gp[:, 1:161], T.vp[:, 0:384].indirect(T.lo[:, 0:10]), ["vp.s0", "vp.d0", "lo"], ["gp.0"])
+        for t in (1, 2, 3):
+            act(T.gp[:, GW * t + 1:GW * t + 1 + C], T.vp[:, 384 * t:384 * t + 384].indirect(T.lo[:]), AF.Copy,
+                ["vp.s%d" % t, "vp.d%d" % t, "lo"], ["gp.%d" % t])
         for t in range(4):
-            tt(T.zt[:, t:4 * C:4], T.gp[:, GW * t + 1:GW * t + 1 + C], T.gp[:, GW * t:GW * t + C], Op.add, ["gp.%d" % t, "gp.z"], ["zt.%d" % t])
+            tt(T.zt[:, t:4 * C:4], T.gp[:, GW * t + 1:GW * t + 1 + C], T.gp[:, GW * t:GW * t + C], Op.add, ["gp.%d" % t, "gp.z", "gp.h"], ["zt.%d" % t])
         qz(T.qz[:], T.sz[:], T.zt[:], ["zt.%d" % t for t in range(4)], ["qz"])
         for b in range(4):
             mx(T.pr[:, 512 * b:512 * b + C], T.qw[:, 128 * b:128 * b + 128], T.sw[:, 128 * b:128 * b + 128], T.qz[:], T.sz[:], True, True,
@@ -493,16 +497,17 @@ def rank_program(g, core, T, topo):
                 act(o, i, AF.Copy, ["xp.%d" % b], ["xn.%d" % b], scale=2.0 ** -5)
             else:
                 ts(o, i, 2.0 ** -5, None, Op.mult, None, ["xp.%d" % b], ["xn.%d" % b])
-        qz(T.qx[:], T.sx[:], T.xn[:], ["xn.%d" % b for b in range(4)], ["qx"])
+        qx_of(T.xn, ["xn.%d" % b for b in range(4)])
 
-    H = C // 2
-    mx(T.ps1[:, 0:H], T.qv[:], T.sv[:], T.qx[:, H:C], T.sx[:, H:C], True, True, ["qv", "qx"], ["P:1"])
-    mx(T.pc[:, 0:H], T.qv[:], T.sv[:], T.qx[:, 0:H], T.sx[:, 0:H], True, True, ["qv", "qx"], ["P:c"])
-    dmas("s", "sto", [(T.oc[:], T.qx[:].bitcast(dt.uint8))] + [(T.osc[4 * k:4 * k + 4, :], T.sx[32 * k:32 * k + 4, :]) for k in range(4)], ["qx"], [])
-    act(T.yb[:, H:C], T.ps1[:, 0:H], AF.Copy, ["P:1"], ["yb.1"])
+    H = 160
+    mx(T.ps1[:, 0:C - H], T.qv[:], T.sv[:], T.qx[:, H:C], T.sx[:, H:C], True, True, ["qv", "qx.b"], ["P:1"])
+    mx(T.pc[:, 0:H], T.qv[:], T.sv[:], T.qx[:, 0:H], T.sx[:, 0:H], True, True, ["qv", "qx.a"], ["P:c"])
+    dmas("s", "sto", [(T.oc[:], T.qx[:].bitcast(dt.uint8))] + [(T.osc[4 * k:4 * k + 4, :], T.sx[32 * k:32 * k + 4, :]) for k in range(4)],
+         ["qx.a", "qx.b"], [])
+    act(T.yb[:, H:C], T.ps1[:, 0:C - H], AF.Copy, ["P:1"], ["yb.1"])
     dmas("a", "stz", [(T.y[:, H:C], T.yb[:, H:C])], ["yb.1"], [])
     cp(T.yb[:, 0:H], T.pc[:, 0:H], ["P:c"], ["yb.0"])
-    dmas("s", "sty", [(T.y[:, 0:H], T.yb[:, 0:H])], ["yb.0"], [])
+    dmas("a", "sty", [(T.y[:, 0:H], T.yb[:, 0:H])], ["yb.0"], [])
     stores = ("stl", "sto", "stz", "sty")
     for s in SEMAPHORES:
         if count.get(s, 0) > waited.get(s, 0) and s not in stores:

@@ -2,11 +2,18 @@ from concourse.bass import DstId, RemoteDMATransfer
 from concourse.mybir import dt, AluOpType as Op, ActivationFunctionType as AF
 
 C, L, R = 288, 96, 3
+H = 160
 BIG = 1.0e29
 F8, U8, BF, F32, I32, U16 = "float8_e4m3fn_x4", "uint8", "bfloat16", "float32", "int32", "uint16"
 GW = 304
 EW = 520
 TW = [288, 224, 160, 128, 128]
+RP = 112
+VTOP = 14
+AEARLY = [9, 8, 7]
+ALATE = [17, 16, 15]
+VC = [(0, 5), (0, 2)] + [(1, _c) for _c in range(6)]
+SP = 160
 
 
 def _sb(n, d):
@@ -19,41 +26,65 @@ SCRATCH = {
     "qw": _sb(512, F8), "sw": _sb(512, U8),
     "qur": _sb(128, F8), "sur": _sb(128, U8), "quc": _sb(32, F8), "suc": _sb(32, U8),
     "qul": _sb(64, F8), "sul": _sb(64, U8), "qu2": _sb(256, F8), "su2": _sb(256, U8),
-    "pi": _sb(2, I32), "ti": _sb(6, I32), "pf": _sb(8, F32), "li": _sb(64, I32), "lst": _sb(64, U16),
-    "la": _sb(8, U16), "lb": _sb(8, U16), "lc": _sb(2, U16),
+    "pi": _sb(2, I32), "ti": _sb(6, I32), "pf": _sb(8, F32), "li": _sb(80, I32), "lst": _sb(80, U16),
+    "la": _sb(8, U16), "lb": _sb(8, U16), "qh": _sb(L * R, F8), "sh": _sb(128 * R, U8),
     "km": _sb(C, BF), "eqm": _sb(C, BF), "mb": _sb(C, BF), "mi": _sb(C, BF), "kk": _sb(C, BF), "kz": _sb(C, BF),
-    "c16": _sb(18, F32), "cc": _sb(18, F32), "ja": _sb(12, F32), "jv": _sb(C, F32), "idn": _sb(192, F32), "ngn": _sb(192, BF),
+    "m16": _sb(C, BF), "pw": _sb(48, F32),
+    "c16": _sb(18, F32), "ja": _sb(12, F32), "jv": _sb(C, F32), "idn": _sb(192, F32), "ngn": _sb(192, BF),
     "obi": _sb(512, BF), "obt": _sb(512, BF), "qob": _sb(128, F8), "sob": _sb(128, U8),
     "one": _sb(EW, BF), "et": _sb(2 * EW, BF), "qe": _sb(512, F8), "se": _sb(512, U8),
-    "mm": _sb(C, F32), "hh": _sb(C, F32), "sga": _sb(6 * 272, BF), "jka": _sb(6 * 96, BF),
-    "rs": _sb(18 * 88, F32), "rsd": _sb(C, BF), "u1": _sb(18, F32), "rs2": _sb(18, F32), "ext": _sb(C, F32),
+    "mm": _sb(C, F32), "hh": _sb(C, F32), "sga": _sb(8 * 18 * 17, BF), "jka": _sb(8 * 10 * 11, BF),
+    "rs": _sb(18 * RP, F32), "rsd": _sb(C, BF), "rs2": _sb(18, F32), "ext": _sb(C, F32),
     "rkf": _sb(18, F32), "rko": _sb(18, U16), "cm": _sb(384, F32), "ex2": _sb(C, F32), "oro": _sb(18, U16),
     "xp": _sb(4 * C, BF), "at": _sb(512, BF), "vp": _sb(4 * 384, BF), "gp": _sb(4 * GW, BF),
     "zt": _sb(4 * C, BF), "zp": _sb(4 * C, BF), "qz": _sb(C, F8), "sz": _sb(C, U8),
-    "ma": _sb(192, F32), "ha": _sb(192, F32), "rep": _sb(2 * C, F32), "pb": _sb(8 * C, BF), "sgp": _sb(4 * C, BF),
-    "jkp": _sb(4 * C, BF), "tt0": _sb(150, F32), "p1": _sb(6 * 144, BF), "f0": _sb(6, F32),
-    "ee": _sb(384, BF), "r2": _sb(384, BF), "kys": _sb(192, F32), "ka": _sb(12, F32), "b2": _sb(12, F32),
-    "kb": _sb(5 * 192, BF), "jkq": _sb(7 * 192, BF), "rk": _sb(12 * 96, F32), "plf": _sb(12, F32), "plo": _sb(12, U16),
-    "ww": _sb(384, BF), "flg": _sb(C, BF), "st": _sb(C, BF), "exw": _sb(C, F32), "exs": _sb(C, BF),
+    "ma": _sb(192, F32), "ha": _sb(192, F32), "rep": _sb(2 * C, F32), "pb": _sb(8 * C, BF), "sgp": _sb(6 * C, BF),
+    "jkp": _sb(6 * C, BF), "yh": _sb(2, F32), "y0": _sb(6 * 144, F32), "y1": _sb(6 * 144, BF),
+    "ee": _sb(384, BF), "r2": _sb(384, BF), "kys": _sb(192, F32), "f2": _sb(12, F32), "ka": _sb(12, F32), "b2": _sb(12, F32),
+    "kb": _sb(384 + 6 * 98, BF), "jkq": _sb(12 * 192, BF), "rk": _sb(12, F32), "rh": _sb(6 * 96, F32), "ini": _sb(8, F32),
+    "plf": _sb(12 * 96, F32), "plo": _sb(12, U16),
+    "ww": _sb(384, BF), "flg": _sb(C, BF), "st": _sb(C, BF), "exw": _sb(C, BF), "exs": _sb(C, BF),
     "wa": _sb(18, F32), "lf": _sb(18, F32), "lo": _sb(18, U16), "lsb": _sb(480, F32), "yb": _sb(C, F32),
     "hs": _sb(20 * R, F32), "qa": _sb(128 * R, F8), "sa": _sb(128 * R, U8), "ql": _sb(192 * R, F8), "sl": _sb(192 * R, U8),
-    "fm": _sb(8 * R, BF), "fl": _sb(16 * R, BF), "sc": ("dram", [2 * R, 128, 18], F32),
-    "ps0": ("psum", [128, 512], F32), "ps1": ("psum", [128, 512], F32), "ps2": ("psum", [128, 512], F32),
-    "pc": ("psum", [128, 512], F32), "pr": ("psum", [128, 2048], F32),
+    "fm": _sb(32 * R, BF), "fl": _sb(32 * R, BF), "sc": ("dram", [2 * R, 128, 18], F32),
+    "ps": ("psum", [128, 4096], F32),
 }
 for _a in range(5):
-    SCRATCH["bt%d" % _a] = _sb(4 * TW[_a], BF)
-    SCRATCH["qb%d" % _a] = _sb(TW[_a], F8)
-    SCRATCH["sb%d" % _a] = _sb(TW[_a], U8)
+    _w = C if _a == 4 else TW[_a]
+    SCRATCH["bt%d" % _a] = _sb(4 * _w, BF)
+    SCRATCH["qb%d" % _a] = _sb(_w, F8)
+    SCRATCH["sb%d" % _a] = _sb(_w, U8)
 
-SEMAPHORES = ["cv", "ca", "cp", "cg", "ldx", "ldu", "ldw", "sent", "uarr", "sty", "stz", "sto", "stl"]
+SEMAPHORES = ["cv", "ca", "cp", "cg", "ldx", "ldy", "ldu", "ldw", "sent", "uarr", "sty", "stz", "sto", "stp", "stl"]
 for _r in range(R):
-    SEMAPHORES += ["%s%d" % (_n, _r) for _n in ("qarr", "farr", "sca", "scb", "rpa", "rpb")]
+    SEMAPHORES += ["%s%d" % (_n, _r) for _n in ("qarr", "harr", "sca", "scb", "rpa", "rpb")]
+    SEMAPHORES += ["farr%d0" % _r, "farr%d1" % _r]
+
+
+def helpers(c, T, topo):
+    return [x for x in topo.cores_of(c) if x not in T.cores and topo.die(x) == topo.die(c)][:2]
+
+
+def helper_program(g, core, rank, e, T, topo):
+    N = len(T.cores)
+    d = (rank + 1 + e) % N
+    rid, pid = topo.addr(T.cores[d], core)
+    mask = topo.mask(core, T.cores[d])
+    came = len(topo.engines(T.cores[rank], core)) // 2
+    for r in range(R):
+        a = 192 * r + (0 if rank == min((d - 1) % N, (d - 2) % N) else L)
+        g.wait_ge(T.sem["harr%d" % r], 2 * came)
+        g.remote_dma(T.ql[:, a:a + L].bitcast(dt.uint8), T.qh[:, L * r:L * r + L].bitcast(dt.uint8), T.sem["qarr%d" % r], T.sem.sent, pid, rid, mask)
+        g.remote_dma(T.sl[:, a:a + L], T.sh[:, L * r:L * r + L], T.sem["qarr%d" % r], T.sem.sent, pid, rid, mask)
+    g.wait_ge(T.sem.sent, 2 * R * len(topo.engines(core, T.cores[d])))
 
 
 def rank_program(g, core, T, topo):
     rank = T.rank_of(core)
     if rank is None:
+        for k, c in enumerate(T.cores):
+            if core in helpers(c, T, topo):
+                helper_program(g, core, k, helpers(c, T, topo).index(core), T, topo)
         return
     N = len(T.cores)
     Q = {"v": g.vector, "a": g.scalar, "p": g.tensor, "g": g, "s": g.sync}
@@ -116,8 +147,7 @@ def rank_program(g, core, T, topo):
     def send(items, reads):
         before("g", reads, [])
         tr = []
-        for k, (d, src, dst, sem) in enumerate(items):
-            c = T.cores[d]
+        for k, (c, src, dst, sem) in enumerate(items):
             eng = topo.engines(core, c)
             w = len(eng) // len(items)
             rid, pid = topo.addr(c, core)
@@ -158,93 +188,198 @@ def rank_program(g, core, T, topo):
     def act(out, in_, f, reads, writes, **kw):
         op("a", lambda: A.activation(out, in_, f, **kw), reads, writes)
 
-    def iota(out, pat, cmul, writes, flt=False):
+    def iota(out, pat, base, cmul, writes, flt=False):
         if flt:
-            op("g", lambda: g.iota(out, pat, 0, cmul, allow_small_or_imprecise_dtypes=True), [], writes)
+            op("g", lambda: g.iota(out, pat, base, cmul, allow_small_or_imprecise_dtypes=True), [], writes)
         else:
-            op("g", lambda: g.iota(out, pat, 0, cmul), [], writes)
+            op("g", lambda: g.iota(out, pat, base, cmul), [], writes)
+
+    def scale(e, out, in_, c, reads, writes):
+        if e == "v":
+            ts(out, in_, c, None, Op.mult, None, reads, writes)
+        else:
+            act(out, in_, AF.Copy, reads, writes, scale=c)
+
+    def move(e, out, in_, reads, writes):
+        if e == "v":
+            cp(out, in_, reads, writes)
+        else:
+            act(out, in_, AF.Copy, reads, writes)
+
+    def fill(out, n, c, writes):
+        act(out, T.one[:, 0:n], AF.Copy, ["one"], writes, scale=c)
+
+    def bank(k, a, b):
+        return T.ps[:, 512 * k + a:512 * k + b]
 
     rcv = [(rank + 1) % N, (rank + 2) % N]
     snd = [(rank - 1) % N, (rank - 2) % N]
+    run = {"a": (0, H), "b": (H, C)}
 
     def slot_at(d):
         return 0 if rank == min((d - 1) % N, (d - 2) % N) else 1
 
-    def xplane(t):
-        act(T.xp[:, C * t:C * t + C], T.xt[:, t:4 * C:4], AF.Copy, ["xt"], ["xp.%d" % t], scale=32.0)
+    def xps(t):
+        return ["xp.a%d" % t, "xp.b%d" % t]
 
-    def qx_of(t, reads):
-        qz(T.qx[:, 160:C], T.sx[:, 160:C], t[:, 640:4 * C], reads, ["qx.b"])
-        qz(T.qx[:, 0:160], T.sx[:, 0:160], t[:, 0:640], reads, ["qx.a"])
+    def xplane(t):
+        act(T.xp[:, C * t:C * t + C], T.xt[:, t:4 * C:4], AF.Copy, ["xt.a", "xt.b"], xps(t), scale=32.0)
+
+    def qx_of(t, h, reads):
+        a, b = run[h]
+        qz(T.qx[:, a:b], T.sx[:, a:b], t[:, 4 * a:4 * b], reads, ["qx." + h])
+
+    AV, AA, BV, SV, SA, CS = 0, 1, 4, 2, 3, 5
+
+    def scores(k, a, b, names):
+        mx(bank(k, 0, b - a), T.qur[:], T.sur[:], T.qx[:, a:b], T.sx[:, a:b], True, True, ["qur", "sur"] + names, ["P:%d" % k])
+
+    def scores_a():
+        scores(AV, 0, H, ["qx.a"])
+        scores(AA, 0, H, ["qx.a"])
+
+    def scores_b():
+        scores(BV, H, C, ["qx.b"])
+        scores(SA, 0, C - 16, ["qx.a", "qx.b"])
+        scores(SV, 0, 16 * VTOP, ["qx.a", "qx.b"])
+
+    def src_of(h):
+        return (bank(AV, 0, H), "P:%d" % AV) if h == "a" else (bank(BV, 0, C - H), "P:%d" % BV)
+
+    def hold1(h):
+        a, b = run[h]
+        tt(T.mm[:, a:b], src_of(h)[0], T.mb[:, a:b], Op.min, [src_of(h)[1], "mb"], ["mm." + h])
+
+    def hold2(h):
+        a, b = run[h]
+        scan(T.hh[:, a:b], T.kk[:, a:b], T.mm[:, a:b], 0.0, Op.min, Op.max, ["kk", "mm." + h], ["hh." + h])
+
+    def diag(h):
+        a, b = run[h]
+        tt(T.bt0[:, 4 * a:4 * b:4], src_of(h)[0], T.hh[:, a:b], Op.is_le, [src_of(h)[1], "hh." + h], ["bt0." + h])
+
+    def lane(c):
+        n = 18 - c
+        return n // 4, n % 4
+
+    def lview(c, a, b):
+        t, k = lane(c)
+        return T["bt%d" % t][:, 4 * a + k:4 * b:4]
+
+    def lname(c):
+        return "bt%d.%d" % lane(c)
+
+    def hname(c):
+        return "hh.a" if 16 * c < H else "hh.b"
+
+    def pad(a, lo_):
+        fill(T["bt%d" % a][:, 4 * lo_:4 * TW[a]], 4 * (TW[a] - lo_), 0.0, ["bt%d.%s" % (a, t) for t in "0123b"])
+
+    def quant(t):
+        w = TW[t]
+        qz(T["qb%d" % t][:, 0:w], T["sb%d" % t][:, 0:w], T["bt%d" % t][:, 0:4 * w], ["bt%d.%s" % (t, k) for k in "0123ab"], ["qb%d" % t])
+
+    def sums(t, start, stop):
+        w = C if start else TW[t]
+        mx(bank(CS, 0, w), T.qob[:], T.sob[:], T["qb%d" % t][:, 0:w], T["sb%d" % t][:, 0:w], start, stop, ["qob", "qb%d" % t], ["P:%d" % CS])
+
+    def p1(c):
+        o, k = 8 * c * (c - 1), AA if 16 * c < H else SA
+        act(T.sga[:, o:o + 16 * c], bank(k, 0, 16 * c), AF.Sign, ["P:%d" % k, hname(c)], ["sga.%d" % c], bias=T.hh[:, 16 * c + 15:16 * c + 16], scale=-1.0)
+
+    def p2(c):
+        o = 8 * c * (c - 1)
+        act(lview(c, 0, 16 * c), T.sga[:, o:o + 16 * c], AF.Relu, ["sga.%d" % c], [lname(c), "rs.%d" % c],
+            accum_out=T.rs[:, RP * c + RP - 1:RP * c + RP])
+
+    def rows(cs):
+        p1(cs[0])
+        for c, d in zip(cs[1:], cs):
+            p1(c)
+            p2(d)
+        p2(cs[-1])
+
+    def bits(c):
+        k = AV if 16 * c <= H else SV
+        ts(lview(c, 0, 16 * c), bank(k, 0, 16 * c), T.hh[:, 16 * c + 15:16 * c + 16], None, Op.is_lt, None, ["P:%d" % k, hname(c)], [lname(c)])
+
+    def rsum(c):
+        scan(T.rs[:, RP * c + RP - 8 * c:RP * c + RP], lview(c, 0, 8 * c), lview(c, 8 * c, 16 * c), 0.0, Op.add, Op.add, [lname(c)], ["rs.%d" % c])
+
+    def asum(c):
+        act(T.jka[:, 8 * c * (c - 1):8 * c * (c + 1)], lview(c, 0, 16 * c), AF.Copy, [lname(c)], ["rs.%d" % c],
+            accum_out=T.rs[:, RP * c + RP - 1:RP * c + RP])
 
     dmas("a", "ldu", [(T.ut[:], T.u[:])], [], ["ut"])
-    dmas("s", "ldx", [(T.xt[:], T.x[:])], [], ["xt"])
-    dmas("s", "ldw", [(T.qw[:].bitcast(dt.uint8), T.wc[:]), (T.sw[:], T.ws[:]), (T.vt[:], T.v[:])], ["xt"], ["qw", "vt"])
-    iota(T.li[:, 0:8], [[16, 8]], 0, ["li.a"])
-    iota(T.pi[:], [[0, 2]], 1, ["pi"])
-    iota(T.km[:], [[0, 18], [1, 16]], 0, ["km"], True)
-    iota(T.c16[:], [[16, 18]], 0, ["c16"], True)
-    iota(T.obi[:], [[1, 8], [0, 64]], 0, ["obi"], True)
-    iota(T.li[:, 10:18], [[1, 8]], 0, ["li.b"])
+    dmas("s", "ldx", [(T.xt[:, 0:4 * H], T.x[:, 0:4 * H])], [], ["xt.a"])
+    dmas("s", "ldy", [(T.xt[:, 4 * H:], T.x[:, 4 * H:])], [], ["xt.b"])
+    dmas("s", "ldw", [(T.qw[:].bitcast(dt.uint8), T.wc[:]), (T.sw[:], T.ws[:]), (T.vt[:], T.v[:])], ["xt.a", "xt.b"], ["qw", "vt"])
+    iota(T.li[:, 0:8], [[16, 8]], 0, 0, ["li.a"])
+    iota(T.pi[:], [[0, 2]], 0, 1, ["pi"])
+    iota(T.km[:], [[0, 18], [1, 16]], 0, 0, ["km"], True)
+    iota(T.c16[:], [[16, 18]], 0, 0, ["c16"], True)
+    iota(T.obi[:], [[1, 8], [0, 64]], 0, 0, ["obi"], True)
+    iota(T.li[:, 10:18], [[1, 8]], 0, 0, ["li.b"])
+    ms(T.one[:], 1.0, ["one"])
     ms(T.kk[:], BIG, ["kk"])
-    ms(T.kz[:], 1.0, ["kz"])
-    ms(T.bt0[:, 4 * 240:], 0.0, ["bt0.0", "bt0.1", "bt0.2", "bt0.3", "bt0.d"])
-    ms(T.kk[:, 0:C:16], -BIG, ["kk"])
-    ms(T.kz[:, 0:C:16], 0.0, ["kz"])
     cp(T.la[:], T.li[:, 0:8], ["li.a"], ["la"])
+    ts(T.ti[:, 4:6], T.pi[:], 7, None, Op.bitwise_and, None, ["pi"], ["ti.3"])
     ts(T.ti[:, 0:1], T.pi[:, 0:1], 15, None, Op.bitwise_and, None, ["pi"], ["ti.0"])
     ts(T.ti[:, 1:2], T.pi[:, 0:1], 31, None, Op.bitwise_and, None, ["pi"], ["ti.1"])
     ts(T.ti[:, 2:3], T.pi[:, 0:1], 4, None, Op.logical_shift_right, None, ["pi"], ["ti.2"])
-    ts(T.ti[:, 4:6], T.pi[:], 7, None, Op.bitwise_and, None, ["pi"], ["ti.3"])
-    for a, lo_ in ((1, 176), (2, 112)):
-        ms(T["bt%d" % a][:, 4 * lo_:], 0.0, ["bt%d.%d" % (a, t) for t in range(4)])
+    ts(T.lst[:, 0:2], T.ti[:, 4:6], 16.0, None, Op.mult, None, ["ti.3"], ["lc"])
+    ms(T.kk[:, 0:C:16], -BIG, ["kk"])
     cp(T.pf[:, 0:3], T.ti[:, 0:3], ["ti.0", "ti.1", "ti.2"], ["pf"])
-    ts(T.lc[:], T.ti[:, 4:6], 16.0, None, Op.mult, None, ["ti.3"], ["lc"])
-    for a, lo_ in ((3, 48), (4, 0)):
-        ms(T["bt%d" % a][:, 4 * lo_:], 0.0, ["bt%d.%d" % (a, t) for t in range(4)])
     ts(T.eqm[:], T.km[:], T.pf[:, 0:1], None, Op.is_equal, None, ["km", "pf"], ["eqm"])
-    ts(T.pf[:, 4:5], T.pf[:, 0:1], -1024.0, 15360.0, Op.mult, Op.add, ["pf"], ["pf.q"])
-    ts(T.pf[:, 5:6], T.pf[:, 0:1], -1025.0, 15375.0, Op.mult, Op.add, ["pf"], ["pf.q2"])
-    ms(T.rs[:, 87:88], 0.0, ["rs.0"])
+    for a, lo_ in ((2, 112), (3, 48), (4, 0), (0, 240)):
+        pad(a, lo_)
+    ms(T.bt4[:, 512:], 0.0, ["bt4.z"])
     ts(T.mb[:], T.eqm[:], 2.0 * BIG, -BIG, Op.mult, Op.add, ["eqm"], ["mb"])
-    ms(T.at[:, 4 * L:], 0.0, ["at.z"])
-    ts(T.mi[:], T.eqm[:], 1049600.0, -1024.0, Op.mult, Op.add, ["eqm"], ["mi"])
     qz(T.qu[:], T.su[:], T.ut[:], ["ut"], ["qu"])
-    ts(T.cc[:], T.c16[:], T.pf[:, 5:6], None, Op.add, None, ["c16", "pf.q2"], ["cc"])
-    act(T.suc[:], T.su[:].indirect(T.lc[:]), AF.Copy, ["qu", "lc"], ["suc"])
+    qx_of(T.xt, "a", ["xt.a"])
     act(T.sur[:], T.su[:].indirect(T.la[:]), AF.Copy, ["qu", "la"], ["sur"])
-    cp(T.quc[:].bitcast(dt.uint32), T.qu[:].bitcast(dt.uint32).indirect(T.lc[:]), ["qu", "lc"], ["quc"])
+    act(T.suc[:], T.su[:].indirect(T.lst[:, 0:2]), AF.Copy, ["qu", "lc"], ["suc"])
     cp(T.qur[:].bitcast(dt.uint32), T.qu[:].bitcast(dt.uint32).indirect(T.la[:]), ["qu", "la"], ["qur"])
+    scores_a()
+    cp(T.quc[:].bitcast(dt.uint32), T.qu[:].bitcast(dt.uint32).indirect(T.lst[:, 0:2]), ["qu", "lc"], ["quc"])
+    pad(1, 176)
+    fill(T.kz[:], C, 512.0, ["kz"])
+    fill(T.rs[:, RP - 1:RP], 1, 0.0, ["rs.0"])
+    act(T.kz[:, 0:C:16], T.c16[:], AF.Identity, ["c16"], ["kz"], scale=-1.0, bias=128.0)
     items = []
     for e in range(2):
-        items.append((snd[e], T.quc[:, 0:8].bitcast(dt.uint8), T.qul[:, 32 * e:32 * e + 8].bitcast(dt.uint8), "uarr"))
-        items.append((snd[e], T.suc[:], T.sul[:, 32 * e:32 * e + 32], "uarr"))
+        items.append((T.cores[snd[e]], T.quc[:, 0:8].bitcast(dt.uint8), T.qul[:, 32 * e:32 * e + 8].bitcast(dt.uint8), "uarr"))
+        items.append((T.cores[snd[e]], T.suc[:], T.sul[:, 32 * e:32 * e + 32], "uarr"))
     send(items, ["quc", "suc"])
-    arrives("uarr", 2 * share(rcv[0], 4) + 2 * share(rcv[1], 4), ["qul"])
-    ms(T.one[:], 1.0, ["one"])
-    qx_of(T.xt, ["xt"])
+    arrives("uarr", 2 * share(rcv[0], 4) + 2 * share(rcv[1], 4), ["qul.0", "qul.1"])
+    qx_of(T.xt, "b", ["xt.b"])
+    hold1("a")
+    scores_b()
+    cp(T.lb[:], T.li[:, 10:18], ["li.b"], ["lb"])
+    hold2("a")
     ts(T.obt[:], T.obi[:], T.pf[:, 2:3], None, Op.is_equal, None, ["obi", "pf"], ["obt"])
-    for t in range(3):
-        xplane(t)
+    rows(AEARLY)
+    diag("a")
 
     for r in range(R):
         first, last = r == 0, r == R - 1
-        hs, fm, fl = T.hs[:, 20 * r:20 * r + 18], T.fm[:, 8 * r:8 * r + 6], T.fl[:, 16 * r:16 * r + 12]
+        hs = T.hs[:, 20 * r:20 * r + 18]
         qa, sa = T.qa[:, 128 * r:128 * r + 128], T.sa[:, 128 * r:128 * r + 128]
         ql, sl = T.ql[:, 192 * r:192 * r + 192], T.sl[:, 192 * r:192 * r + 192]
-        mx(T.ps2[:, 0:128], T.qur[:], T.sur[:], T.qx[:, 160:C], T.sx[:, 160:C], True, True, ["qur", "sur", "qx.b"], ["P:2"])
-        mx(T.ps0[:, 0:C], T.qur[:], T.sur[:], T.qx[:], T.sx[:], True, True, ["qur", "sur", "qx.a", "qx.b"], ["P:0"])
-        mx(T.ps1[:, 0:C], T.qur[:], T.sur[:], T.qx[:], T.sx[:], True, True, ["qur", "sur", "qx.a", "qx.b"], ["P:1"])
-        S0, S1 = T.ps0, T.ps1
-        tt(T.mm[:, 192:C], T.ps2[:, 32:128], T.mb[:, 192:C], Op.min, ["P:2", "mb"], ["mm.b"])
-        scan(T.hh[:, 192:C], T.kk[:, 192:C], T.mm[:, 192:C], 0.0, Op.min, Op.max, ["kk", "mm.b"], ["hh.b"])
-        tt(T.mm[:, 0:192], S0[:, 0:192], T.mb[:, 0:192], Op.min, ["P:0", "mb"], ["mm.a"])
-        tt(T.bt0[:, 4 * 192:4 * C:4], S0[:, 192:C], T.hh[:, 192:C], Op.is_le, ["P:0", "hh.b"], ["bt0.d"])
-        scan(T.hh[:, 0:192], T.kk[:, 0:192], T.mm[:, 0:192], 0.0, Op.min, Op.max, ["kk", "mm.a"], ["hh.a"])
+
+        low = [c for c in range(9, 0, -1) if c not in AEARLY + ALATE]
+        bits(low[0])
+        hold1("b")
+        for c in low[-2:]:
+            bits(c)
+        hold2("b")
+        rows(ALATE)
         if first:
             qz(T.qob[:], T.sob[:], T.obt[:], ["obt"], ["qob"])
+        else:
+            quant(4)
         cp(hs, T.hh[:, 15:C:16], ["hh.a", "hh.b"], ["hs%d" % r])
-        send([(snd[e], hs, T.sc[2 * r + e], "%s%d" % (("sca", "scb")[e], r)) for e in range(2)], ["hs%d" % r])
+        send([(T.cores[snd[e]], hs, T.sc[2 * r + e], "%s%d" % (("sca", "scb")[e], r)) for e in range(2)], ["hs%d" % r])
 
         def spread(e, q):
             arrives("%s%d" % (("sca", "scb")[e], r), share(rcv[e], 2), ["sc%d.%d" % (r, e)])
@@ -253,262 +388,330 @@ def rank_program(g, core, T, topo):
 
         spread(0, "s")
         if first:
-            iota(T.jv[:], [[1, C]], 0, ["jv"], True)
-            iota(T.li[:, 26:50], [[1, 12], [0, 2]], 0, ["li.d"])
-            iota(T.li[:, 50:62], [[32, 12]], 0, ["li.e"])
+            qz(T.qb4[:, 0:C], T.sb4[:, 0:C], T.bt4[:, 0:4 * C], ["bt4.z"] + ["bt4.%d" % k for k in range(4)], ["qb4"])
+            iota(T.jv[:], [[1, C]], 0, 0, ["jv"], True)
+            iota(T.li[:, 26:38], [[1, 6], [0, 2]], 0, 0, ["li.d"])
+            iota(T.li[:, 50:56], [[32, 6]], 0, 0, ["li.e"])
+            iota(T.li[:, 56:68], [[96, 2], [192, 2], [32, 3]], 0, 0, ["li.f"])
+            iota(T.ja[:], [[48, 2], [96, 2], [16, 3]], 0, 0, ["ja"], True)
+            iota(T.idn[:], [[48, 2], [96, 2], [1, 48]], 0, 0, ["idn"], True)
+        diag("b")
+        for c in low[1:-2] + list(range(10, VTOP + 1)):
+            bits(c)
+        quant(2)
+        scan(T.rsd[:], T.kz[:], T.bt0[:, 0:4 * C:4], 512.0, Op.min, Op.add, ["kz", "bt0.a", "bt0.b"], ["rsd"])
+        for c in low + [10]:
+            asum(c)
+        sums(4, True, False)
+        sums(2, False, False)
+        quant(1)
+        sums(1, False, False)
+        quant(0)
+        sums(0, False, False)
+        if first:
+            act(T.mi[:], T.eqm[:], AF.Identity, ["eqm"], ["mi"], scale=1049600.0, bias=-1024.0)
+            act(T.pf[:, 5:6], T.pf[:, 0:1], AF.Identity, ["pf"], ["pf.q2"], scale=-1025.0, bias=15503.0)
+            act(T.pf[:, 4:5], T.pf[:, 0:1], AF.Identity, ["pf"], ["pf.q"], scale=-1024.0, bias=15360.0)
+            for t in range(4):
+                xplane(t)
+            fill(T.at[:, 4 * L:], 128, 0.0, ["at.z"])
+        spread(1, "s" if first else "a")
+        quant(3)
+        sums(3, False, True)
+        for c in range(11, VTOP + 1):
+            rsum(c)
+        scan(T.ext[:], T.mi[:], bank(CS, 0, C), 0.0, Op.add, Op.min, ["mi", "P:%d" % CS], ["ext"])
+        tt(T.rs2[:], T.rs[:, RP - 1:18 * RP:RP], T.rsd[:, 15:C:16], Op.add, ["rs.%d" % c for c in range(18)] + ["rsd"], ["rs2"])
+        if first:
+            cp(T.lst[:, 26:33], T.li[:, 26:33], ["li.d"], ["lst.c"])
+        tt(T.rkf[:], T.ext[:, 15:C:16], T.rs2[:], Op.subtract, ["ext", "rs2"], ["rkf"])
+        if first:
+            cp(T.lst[:, 40:45], T.li[:, 33:38], ["li.d"], ["lst.d"])
+            act(T.ngn[:], T.idn[:], AF.Identity, ["idn"], ["ngn"], scale=-1.0, bias=-64.0)
+            fill(T.pw[:, 0:16], 16, 1.0 / 16, ["pw.a"])
+            act(T.pw[:, 16:32], T.eqm[:, 0:16], AF.Copy, ["eqm"], ["pw.b"], scale=-1.0)
+            act(T.idn[:], T.idn[:], AF.Copy, ["idn"], ["idn"], scale=1.0 / 128)
             for h in range(2):
                 op("g", lambda: g.affine_select(T.et[:, EW * h:EW * h + EW], T.one[:], [[1, EW]], Op.is_equal, 0.0, -2 - h, -4), ["one"], ["et.%d" % h])
 
-        def lane(c):
-            n = 18 - c
-            return n // 4, n % 4
-
-        def lview(c, a, b):
-            t, k = lane(c)
-            return T["bt%d" % t][:, 4 * a + k:4 * b:4]
-
-        def lname(c):
-            return "bt%d.%d" % lane(c)
-
-        def quant(t):
-            qz(T["qb%d" % t][:], T["sb%d" % t][:], T["bt%d" % t][:], ["bt%d.%d" % (t, k) for k in range(4)] + ["bt%d.d" % t], ["qb%d" % t])
-
-        def sums(t, start, stop):
-            mx(T.pc[:, 0:TW[t]], T.qob[:], T.sob[:], T["qb%d" % t][:], T["sb%d" % t][:], start, stop, ["qob", "qb%d" % t], ["P:c"])
-
-        def p1(c):
-            o = 272 * (17 - c)
-            act(T.sga[:, o:o + 16 * c], S1[:, 0:16 * c], AF.Sign, ["P:1", "hh.b"], ["sga.%d" % c], bias=T.hh[:, 16 * c + 15:16 * c + 16], scale=-1.0)
-
-        def p2(c):
-            o = 272 * (17 - c)
-            act(lview(c, 0, 16 * c), T.sga[:, o:o + 16 * c], AF.Relu, ["sga.%d" % c], [lname(c), "rs.%d" % c],
-                accum_out=T.rs[:, 88 * c + 87:88 * c + 88])
-
-        p1(17)
-        for c in range(16, 11, -1):
-            p1(c)
-            p2(c + 1)
-        p2(12)
-
-        def bits(c):
-            ts(lview(c, 0, 16 * c), S0[:, 0:16 * c], T.hh[:, 16 * c + 15:16 * c + 16], None, Op.is_lt, None, ["P:0", "hh.a"], [lname(c)])
-
-        def rsum(c):
-            scan(T.rs[:, 88 * c + 88 - 8 * c:88 * c + 88], lview(c, 0, 8 * c), lview(c, 8 * c, 16 * c), 0.0, Op.add, Op.add,
-                 [lname(c)], ["rs.%d" % c])
-
-        tt(T.bt0[:, 0:4 * 192:4], S0[:, 0:192], T.hh[:, 0:192], Op.is_le, ["P:0", "hh.a"], ["bt0.0"])
-        for c in (10, 9, 8, 7, 6):
-            bits(c)
-        quant(2)
-        for c in (5, 4, 3, 2):
-            bits(c)
-        bits(1)
-        quant(3)
-        bits(11)
-        scan(T.rsd[:], T.kz[:], T.bt0[:, 0:4 * C:4], 0.0, Op.mult, Op.add, ["kz", "bt0.0", "bt0.d"], ["rsd"])
-        quant(4)
-        quant(0)
-        sums(0, True, False)
-        sums(2, False, False)
-        sums(3, False, False)
-        sums(4, False, False)
-        for c in range(6, 0, -1):
-            act(T.jka[:, 96 * c - 96:96 * c - 96 + 16 * c], lview(c, 0, 16 * c), AF.Copy, [lname(c)], ["rs.%d" % c],
-                accum_out=T.rs[:, 88 * c + 87:88 * c + 88])
-        if first:
-            xplane(3)
-            cp(T.lb[:], T.li[:, 10:18], ["li.b"], ["lb"])
-            for e in range(2):
-                act(T.su2[:, 128 * e:128 * e + 128], T.sul[:, 32 * e:32 * e + 8].indirect(T.lb[:]), AF.Copy, ["qul", "lb"], ["su2.%d" % e])
-        spread(1, "a")
-        for c in (11, 10):
-            rsum(c)
-        quant(1)
-        sums(1, False, True)
-        for c in (9, 8, 7):
-            rsum(c)
-        tt(T.u1[:], T.rsd[:, 15:C:16], T.cc[:], Op.subtract, ["rsd", "cc"], ["u1"])
-        scan(T.ext[:], T.mi[:], T.pc[:, 0:C], 0.0, Op.add, Op.min, ["mi", "P:c"], ["ext"])
-        tt(T.rs2[:], T.rs[:, 87:18 * 88:88], T.u1[:], Op.add, ["rs.%d" % c for c in range(18)] + ["u1"], ["rs2"])
-        tt(T.rkf[:], T.ext[:, 15:C:16], T.rs2[:], Op.subtract, ["ext", "rs2"], ["rkf"])
-        cp(T.rko[:], T.rkf[:], ["rkf"], ["rko"])
-        cp(T.cm[:, 96:384].indirect(T.rko[:]), T.jv[:], ["rko", "jv"], ["cm"])
-        scan(T.ex2[:, 0:L], T.mi[:, 0:L], T.cm[:, 96:192], 0.0, Op.add, Op.min, ["mi", "cm"], ["ex2.a"])
-        ts(T.oro[:, 0:6], T.ex2[:, 15:L:16], T.pf[:, 4:5], None, Op.add, None, ["ex2.a", "pf.q"], ["oro.a"])
-        for t in range(4):
-            win = T.xp[:, C * t:C * t + C].indirect(T.oro[:, 0:6])
-            if t < 2:
-                ts(T.at[:, t:4 * L:4], win, 2.0 ** -5, None, Op.mult, None, ["xp.%d" % t, "oro.a"], ["at.%d" % t])
-            else:
-                act(T.at[:, t:4 * L:4], win, AF.Copy, ["xp.%d" % t, "oro.a"], ["at.%d" % t], scale=2.0 ** -5)
-        qz(qa, sa, T.at[:], ["at.z", "at.0", "at.1", "at.2", "at.3"], ["qa%d" % r])
-        at_ = {d: 192 * r + L * slot_at(d) for d in rcv}
-        send([(d, T.qa[:, 128 * r:128 * r + L].bitcast(dt.uint8), T.ql[:, at_[d]:at_[d] + L].bitcast(dt.uint8), "qarr%d" % r) for d in rcv], ["qa%d" % r])
-        send([(d, T.sa[:, 128 * r:128 * r + L], T.sl[:, at_[d]:at_[d] + L], "qarr%d" % r) for d in rcv], ["qa%d" % r])
-        arrives("qarr%d" % r, 2 * share(snd[0], 2) + 2 * share(snd[1], 2), ["ql%d" % r])
-        for e in range(2):
+        def theirs(e):
             o = 128 * e
             if first:
-                cp(T.qu2[:, o:o + 128].bitcast(dt.uint32), T.qul[:, 32 * e:32 * e + 8].bitcast(dt.uint32).indirect(T.lb[:]), ["qul", "lb"], ["qu2.%d" % e])
-            mx((T.ps0, T.ps1)[e][:, 0:128], T.qu2[:, o:o + 128], T.su2[:, o:o + 128], qa, sa, True, True,
-               ["qu2.%d" % e, "su2.%d" % e, "qa%d" % r], ["P:%d" % e])
+                act(T.su2[:, o:o + 128], T.sul[:, 32 * e:32 * e + 8].indirect(T.lb[:]), AF.Copy, ["qul.%d" % e, "lb"], ["su2.%d" % e])
+                cp(T.qu2[:, o:o + 128].bitcast(dt.uint32), T.qul[:, 32 * e:32 * e + 8].bitcast(dt.uint32).indirect(T.lb[:]),
+                   ["qul.%d" % e, "lb"], ["qu2.%d" % e])
+
+        ts(T.rko[:], T.rkf[:], T.pf[:, 5:6], None, Op.add, None, ["rkf", "pf.q2"], ["rko"])
+        if first:
+            ts(T.lst[:, 50:68], T.li[:, 50:68], T.pf[:, 1:2], None, Op.add, None, ["li.e", "li.f", "pf"], ["lst.e"])
+        cp(T.cm[:, 96:384].indirect(T.rko[:]), T.jv[:], ["rko", "jv"], ["cm"])
+        theirs(0)
+        scan(T.ex2[:, 0:L], T.mi[:, 0:L], T.cm[:, 96:192], 0.0, Op.add, Op.min, ["mi", "cm"], ["ex2.a"])
+        theirs(1)
+        ts(T.oro[:, 0:6], T.ex2[:, 15:L:16], T.pf[:, 4:5], None, Op.add, None, ["ex2.a", "pf.q"], ["oro.a"])
+        if first:
+            ts(T.ja[:], T.ja[:], T.pf[:, 0:1], 1.0 / 128, Op.add, Op.mult, ["ja", "pf"], ["ja"])
+        for t in range(4):
+            scale("vvaa"[t], T.at[:, t:4 * L:4], T.xp[:, C * t:C * t + C].indirect(T.oro[:, 0:6]), 2.0 ** -5, xps(t) + ["oro.a"], ["at.%d" % t])
+        if first:
+            scan(T.pw[:, 32:48], T.pw[:, 0:16], T.pw[:, 16:32], 0.0, Op.mult, Op.min, ["pw.a", "pw.b"], ["pw"])
+        qz(qa, sa, T.at[:], ["at.z", "at.0", "at.1", "at.2", "at.3"], ["qa%d" % r])
+        hands = helpers(core, T, topo)
+        send([(c, T.qa[:, 128 * r:128 * r + L].bitcast(dt.uint8), T.qh[:, L * r:L * r + L].bitcast(dt.uint8), "harr%d" % r) for c in hands], ["qa%d" % r])
+        send([(c, T.sa[:, 128 * r:128 * r + L], T.sh[:, L * r:L * r + L], "harr%d" % r) for c in hands], ["qa%d" % r])
+        arrives("qarr%d" % r, sum(2 * len(topo.engines(helpers(T.cores[snd[e]], T, topo)[e], core)) for e in range(2)), ["ql%d" % r])
+        for e in range(2):
+            o = 128 * e
+            mx(bank(4 + e, 0, 128), T.qu2[:, o:o + 128], T.su2[:, o:o + 128], qa, sa, True, True,
+               ["qu2.%d" % e, "su2.%d" % e, "qa%d" % r], ["P:%d" % (4 + e)])
+        if first:
+            fill(T.kb[:, 384:384 + 6 * 98:98], 6, -96.0, ["kb.y"])
+            fill(T.kb[:, 384 + 97:384 + 6 * 98:98], 6, 0.0, ["kb.z"])
+            fill(T.pb[:, 0:1], 1, -288.0, ["pb.z"])
+            fill(T.pb[:, C - SP + 1:C - SP + 2], 1, 0.0, ["pb.y"])
         scan(T.ex2[:, L:C], T.mi[:, L:C], T.cm[:, 192:384], 0.0, Op.add, Op.min, ["mi", "cm"], ["ex2.b"])
         for e in range(2):
-            tt(T.ma[:, L * e:L * e + L], (T.ps0, T.ps1)[e][:, 0:L], T.mb[:, 0:L], Op.min, ["P:%d" % e, "mb"], ["ma.%d" % e])
+            tt(T.ma[:, L * e:L * e + L], bank(4 + e, 0, L), T.mb[:, 0:L], Op.min, ["P:%d" % (4 + e), "mb"], ["ma.%d" % e])
         for e in range(2):
             scan(T.ha[:, L * e:L * e + L], T.kk[:, 0:L], T.ma[:, L * e:L * e + L], 0.0, Op.min, Op.max, ["kk", "ma.%d" % e], ["ha.%d" % e])
+        END = 6 * 143
 
-        def a1(c):
-            o = C * (c - 2)
-            act(T.sgp[:, o:o + C], T.rep[:, 0:C], AF.Sign, ["rep.0", "ha.0"], ["sgp.%d" % c], bias=T.ha[:, 16 * c + 15:16 * c + 16], scale=-1.0)
+        def a1(c, n):
+            act(T.sgp[:, C * c:C * c + n], T.rep[:, 0:n], AF.Sign, ["rep.0", "ha.0"], ["sgp.%d" % c],
+                bias=T.ha[:, 16 * c + 15:16 * c + 16], scale=-1.0)
 
         def a2(c):
-            o = C * (c - 2)
-            act(T.jkp[:, o:o + C], T.sgp[:, o:o + C], AF.Relu, ["sgp.%d" % c], ["tt0.%d" % c], scale=-1.0,
-                accum_out=T.tt0[:, 143 + c:144 + c])
+            act(T.jkp[:, C * c:C * c + C], T.sgp[:, C * c:C * c + C], AF.Sign, ["sgp.%d" % c], ["y0.%d" % c], scale=-1.0, bias=-0.5,
+                accum_out=T.y0[:, END + c:END + c + 1])
 
-        a1(2)
-        for c in range(3, 6):
-            a1(c)
-            a2(c - 1)
-        a2(5)
-        cols = [(0, 1), (0, 0)] + [(1, c) for c in range(6)]
-
-        def vb(k):
-            e, c = cols[k]
-            o = C * k
-            ts(T.pb[:, o:o + C], T.rep[:, C * e:C * e + C], T.ha[:, L * e + 16 * c + 15:L * e + 16 * c + 16], None, Op.is_gt, None,
+        def vb(e, c):
+            k = VC.index((e, c))
+            o, a = (1, SP) if k == 0 else (C * k, 0)
+            ts(T.pb[:, o:o + C - a], T.rep[:, C * e + a:C * e + C], T.ha[:, L * e + 16 * c + 15:L * e + 16 * c + 16], 2.0, Op.is_gt, Op.mult,
                ["rep.%d" % e, "ha.%d" % e], ["pb.%d" % k])
 
-        def vs(k):
-            e, c = cols[k]
+        def vs(e, c):
+            k = VC.index((e, c))
             o = C * k
-            if e == 0:
-                scan(T.tt0[:, c:144 + c], T.pb[:, o:o + 144], T.pb[:, o + 144:o + C], 0.0, Op.add, Op.add, ["pb.%d" % k],
-                     ["tt0.0", "tt0.1"][:c + 1])
+            if k == 0:
+                w = (C - SP) // 2 + 1
+                scan(T.y0[:, END + c - 6 * (w - 1):END + c + 1:6], T.pb[:, 0:w], T.pb[:, w:2 * w], T.yh[:, 0:1], Op.add, Op.add,
+                     ["pb.0", "pb.z", "pb.y", "yh"], ["y0.%d" % c])
             else:
-                scan(T.p1[:, 144 * c:144 * c + 144], T.pb[:, o:o + 144], T.pb[:, o + 144:o + C], -96.0, Op.add, Op.add,
-                     ["pb.%d" % k], ["p1.%d" % c])
+                scan((T.y0, T.y1)[e][:, c:6 * 144:6], T.pb[:, o:o + 144], T.pb[:, o + 144:o + C], -288.0, Op.add, Op.add, ["pb.%d" % k], ["y%d.%d" % (e, c)])
 
-        vb(0)
-        for k in range(1, 8):
-            vb(k)
-            vs(k - 1)
-        vs(7)
-        ts(T.f0[:], T.tt0[:, 143:149], -96.0, 0.0, Op.add, Op.max, ["tt0.%d" % c for c in range(6)], ["f0"])
+        def final(h):
+            o, n = 16 * (2 * r + h), "%d%d" % (r, h)
+            fm = T.fm[:, o:o + 3]
+            tt(fm, T.y0[:, END + 3 * h:END + 3 * h + 3], T.y1[:, END + 3 * h:END + 3 * h + 3], Op.max,
+               ["y%d.%d" % (e, c) for e in range(2) for c in range(3 * h, 3 * h + 3)], ["fm" + n])
+            send([(T.cores[d], fm, T.fl[:, o + 3 * slot_at(d):o + 3 * slot_at(d) + 3], "farr" + n) for d in rcv], ["fm" + n])
+            arrives("farr" + n, share(snd[0], 2) + share(snd[1], 2), ["fl" + n])
+
+        a1(0, C)
+        a1(1, C)
+        a2(0)
+        a1(5, SP)
+        a2(1)
+        a1(3, C)
+        act(T.jkp[:, C * 5:C * 5 + SP], T.sgp[:, C * 5:C * 5 + SP], AF.Relu, ["sgp.5"], ["yh"], scale=-2.0, accum_out=T.yh[:, 0:1])
+        a1(4, C)
+        a2(3)
+        a2(4)
+        seq = [(0, 2), (1, 0), (1, 1), (1, 2)]
+        vb(*seq[0])
+        for x, y in zip(seq[1:] + [(0, 5)], seq):
+            vb(*x)
+            vs(*y)
         ts(T.oro[:, 6:18], T.ex2[:, L + 15:C:16], T.pf[:, 4:5], None, Op.add, None, ["ex2.b", "pf.q"], ["oro.b"])
-        tt(fm, T.f0[:], T.p1[:, 143:6 * 144:144], Op.max, ["f0"] + ["p1.%d" % c for c in range(6)], ["fm%d" % r])
-        send([(d, fm, T.fl[:, 16 * r + 6 * slot_at(d):16 * r + 6 * slot_at(d) + 6], "farr%d" % r) for d in rcv], ["fm%d" % r])
-        arrives("farr%d" % r, share(snd[0], 2) + share(snd[1], 2), ["fl%d" % r])
+        final(0)
+        vb(1, 3)
+        for c in (4, 5):
+            vb(1, c)
+            vs(1, c - 1)
+        vs(0, 5)
+        vs(1, 5)
+        final(1)
 
-        if first:
-            for b in range(4):
-                o = EW * (b % 2) + 2 - 2 * (b // 2)
+        def unpacker(b):
+            o = EW * (b % 2) + 2 - 2 * (b // 2)
+            if first:
                 qz(T.qe[:, 128 * b:128 * b + 128], T.se[:, 128 * b:128 * b + 128], T.et[:, o:o + 512], ["et.%d" % (b % 2)], ["qe.%d" % b])
-            cp(T.lst[:, 26:50], T.li[:, 26:50], ["li.d"], ["lst.d"])
-            ts(T.lst[:, 50:62], T.li[:, 50:62], T.pf[:, 1:2], None, Op.add, None, ["li.e", "pf"], ["lst.e"])
-            ts(T.ja[:], T.c16[:, 0:12], T.pf[:, 0:1], 1.0 / 256, Op.add, Op.mult, ["c16", "pf"], ["ja"])
-            ts(T.idn[:], T.jv[:, 0:192], 1.0 / 256, None, Op.mult, None, ["jv"], ["idn"])
-            ts(T.ngn[:], T.jv[:, 0:192], -191.0, None, Op.add, None, ["jv"], ["ngn"])
-        for t in range(4):
-            win = T.xp[:, C * t:C * t + C].indirect(T.oro[:, 6:18])
-            o = T.vp[:, 384 * t + 192:384 * t + 384]
-            if t < (1 if first else 2):
-                ts(o, win, 2.0 ** -6, None, Op.mult, None, ["xp.%d" % t, "oro.b"], ["vp.s%d" % t])
-            else:
-                act(o, win, AF.Copy, ["xp.%d" % t, "oro.b"], ["vp.s%d" % t], scale=2.0 ** -6)
-        ms(T.ww[:], 256.0, ["ww"])
+
+        def stayers(e, t):
+            scale(e, T.vp[:, 384 * t + 192:384 * t + 384], T.xp[:, C * t:C * t + C].indirect(T.oro[:, 6:18]), 2.0 ** -6, xps(t) + ["oro.b"], ["vp.s%d" % t])
+
+        for t in range(2):
+            stayers("a", t)
         if last:
-            ts(T.cm[:, 0:192], T.jv[:, 0:192], 288.0, None, Op.add, None, ["jv"], ["cm"])
             qz(T.qv[:], T.sv[:], T.vt[:], ["vt"], ["qv"])
-        cp(T.gp[:, 0:4 * GW:GW], T.vp[:, 192:4 * 384:384], ["vp.s%d" % t for t in range(4)], ["gp.z"])
-        for b in range(4):
-            mx(T.pr[:, 512 * b:512 * b + 192], T.qe[:, 128 * b:128 * b + 128], T.se[:, 128 * b:128 * b + 128], ql, sl, True, True,
-               ["qe.%d" % b, "ql%d" % r], ["P:r%d" % b])
-        for b in range(4):
-            o, i = T.vp[:, 384 * b:384 * b + 192], T.pr[:, 512 * b:512 * b + 192]
-            if b % 2:
-                ts(o, i, 0.5, None, Op.mult, None, ["P:r%d" % b], ["vp.d%d" % b])
+
+        def keys(h, between):
+            n, o = "%d%d" % (r, h), 16 * (2 * r + h)
+            fl, w, c = T.fl[:, o:o + 6], 192 * h, slice(6 * h, 6 * h + 6)
+            act(T.ee[:, w + 112:w + 192], fl.indirect(T.lst[:, 40:45]), AF.Relu, ["fl" + n, "lst.d"], ["ee.1%d" % h], bias=96.0)
+            act(T.f2[:, c], fl, AF.Relu, ["fl" + n], ["f2.%d" % h], bias=96.0)
+            act(T.b2[:, c], T.f2[:, c], AF.Relu, ["f2.%d" % h], ["b2.%d" % h], scale=-1.0, bias=382.0)
+            ts(T.ee[:, w:w + 112], fl.indirect(T.lst[:, 26:33]), 96.0, 0.0, Op.add, Op.max, ["fl" + n, "lst.c"], ["ee.0%d" % h])
+            between()
+            op("v", lambda: V.transpose(T.r2[:, w:w + 192], T.ee[:, w:w + 192]), ["ee.0%d" % h, "ee.1%d" % h], ["r2.%d" % h])
+            tt(T.ka[:, c], T.f2[:, c], T.ja[:, c], Op.add, ["f2.%d" % h, "ja"], ["ka.%d" % h])
+            tt(T.kys[:, L * h:L * h + L], T.r2[:, w:w + 192].indirect(T.lst[:, 50:56]), T.idn[:, L * h:L * h + L], Op.add,
+               ["r2.%d" % h, "lst.e", "idn"], ["kys.%d" % h])
+
+        def ka(c, a, b, out, name):
+            act(T.jkq[:, 192 * c + a:192 * c + b], T.kys[:, a:b], AF.Sign, ["kys.%d" % (a // L), "kys.%d" % ((b - 1) // L), "ka.%d" % (c // 6)], [name],
+                bias=T.ka[:, c:c + 1], scale=-1.0, accum_out=out)
+
+        def kb(c, a, o):
+            ts(T.kb[:, o:o + L], T.kys[:, a:a + L], T.ka[:, c:c + 1], 2.0, Op.is_lt, Op.mult, ["kys.%d" % (a // L), "ka.%d" % (c // 6)], ["kb.%d" % o])
+
+        def ks(c, o, m, out, init, reads, name):
+            scan(out[:, 96 * c + 96 - m:96 * c + 96], T.kb[:, o:o + m], T.kb[:, o + m:o + 2 * m], init, Op.add, Op.add, reads, [name])
+
+        def old(c):
+            return 384 + 98 * c
+
+        unpacker(0)
+        ms(T.ww[:], -512.0, ["ww"])
+        keys(0, lambda: None)
+        for c in range(2, 6):
+            ka(c, 0, L, T.rh[:, 96 * c + 95:96 * c + 96], "rh.%d" % c)
+        kb(0, 0, 0)
+        kb(1, 0, L)
+        ks(0, 0, 48, T.rh, -95.0, ["kb.0"], "rh.0")
+        ks(1, L, 48, T.rh, -95.0, ["kb.96"], "rh.1")
+        keys(1, lambda: tt(T.ini[:, 0:6], T.rh[:, 95:6 * 96:96], T.b2[:, 0:6], Op.subtract, ["rh.%d" % c for c in range(6)] + ["b2.0"], ["ini.0"]))
+        act(T.ini[:, 6:7], T.b2[:, 6:7], AF.Identity, ["b2.1"], ["ini.1"], scale=-1.0, bias=-191.0)
+        for c in range(7, 12):
+            ka(c, 0, 2 * L, T.rk[:, c:c + 1], "rk.%d" % c)
+        kb(6, 0, 192)
+        kb(6, L, 288)
+        kb(0, L, old(0) + 1)
+        ks(6, 192, L, T.plf, T.ini[:, 6:7], ["kb.192", "kb.288", "ini.1"], "plf.6")
+        for c in range(1, 7):
+            if c < 6:
+                kb(c, L, old(c) + 1)
             else:
-                act(o, i, AF.Copy, ["P:r%d" % b], ["vp.d%d" % b], scale=0.5)
-
-        fn_ = "fl%d" % r
-        act(T.ee[:, 192:384], fl.indirect(T.lst[:, 38:50]), AF.Copy, [fn_, "lst.d"], ["ee.1"])
-        cp(T.ee[:, 0:192], fl.indirect(T.lst[:, 26:38]), [fn_, "lst.d"], ["ee.0"])
-        tt(T.ka[:], fl, T.ja[:], Op.add, [fn_, "ja"], ["ka"])
-        op("v", lambda: V.transpose(T.r2[:], T.ee[:]), ["ee.0", "ee.1"], ["r2"])
-        ts(T.b2[:], fl, 191.0, 2.0, Op.min, Op.mult, [fn_], ["b2"])
-        tt(T.kys[:], T.r2[:].indirect(T.lst[:, 50:62]), T.idn[:], Op.add, ["r2", "lst.e", "idn"], ["kys"])
-        for c in range(5, 12):
-            act(T.jkq[:, 192 * (c - 5):192 * (c - 4)], T.kys[:], AF.Sign, ["kys", "ka"], ["rk.%d" % c], bias=T.ka[:, c:c + 1], scale=-1.0,
-                accum_out=T.rk[:, 96 * c + 95:96 * c + 96])
-        if last:
-            act(T.lsb[:, C:480], T.r2[:].indirect(T.lst[:, 50:62]), AF.Copy, ["r2", "lst.e"], ["lsb.b"])
-
-        def kb(c):
-            o = 192 * c
-            ts(T.kb[:, o:o + 192], T.kys[:], T.ka[:, c:c + 1], 2.0, Op.is_lt, Op.mult, ["kys", "ka"], ["kb.%d" % c])
-
-        def ks(c):
-            o = 192 * c
-            scan(T.rk[:, 96 * c:96 * c + 96], T.kb[:, o:o + 96], T.kb[:, o + 96:o + 192], -191.0, Op.add, Op.add, ["kb.%d" % c], ["rk.%d" % c])
-
-        kb(0)
-        for c in range(1, 5):
-            kb(c)
-            ks(c - 1)
-        ks(4)
-        tt(T.plf[:], T.rk[:, 95:12 * 96:96], T.b2[:], Op.add, ["rk.%d" % c for c in range(12)] + ["b2"], ["plf"])
-        ts(T.plo[:], T.plf[:], 193.0, 0.5, Op.add, Op.mult, ["plf"], ["plo"])
+                tt(T.plf[:, 96 * 7 + 95:96 * 12:96], T.rk[:, 7:12], T.b2[:, 7:12], Op.subtract, ["rk.%d" % c for c in range(7, 12)] + ["b2.1"], ["plf.7"])
+            ks(c - 1, old(c - 1), 49, T.plf, T.ini[:, c - 1:c], ["kb.%d" % (old(c - 1) + 1), "kb.y", "kb.z", "ini.0"], "plf.%d" % (c - 1))
+        unpacker(1)
+        ts(T.plo[:], T.plf[:, 95:12 * 96:96], 575.0, 0.5, Op.add, Op.mult, ["plf.%d" % c for c in range(8)], ["plo"])
+        if first:
+            act(T.m16[:], T.eqm[:], AF.Identity, ["eqm"], ["m16"], scale=-16.0, bias=16.0)
+        unpacker(2)
         cp(T.ww[:].indirect(T.plo[:]), T.ngn[:], ["plo", "ngn"], ["ww"])
-        ts(T.flg[:], T.ww[:, 0:C], 0.0, None, Op.is_gt, None, ["ww"], ["flg"])
-        scan(T.exw[:], T.mi[:], T.ww[:, 0:C], 0.0, Op.add, Op.min, ["mi", "ww"], ["exw"])
+        unpacker(3)
+        for t in (2, 3):
+            stayers("a", t)
+        for b in range(4):
+            mx(bank(b, 0, 192), T.qe[:, 128 * b:128 * b + 128], T.se[:, 128 * b:128 * b + 128], ql, sl, True, True,
+               ["qe.%d" % b, "ql%d" % r], ["P:%d" % b])
+        for b in range(4):
+            scale("a", T.vp[:, 384 * b:384 * b + 192], bank(b, 0, 192), 0.5, ["P:%d" % b], ["vp.d%d" % b])
+        act(T.gp[:, 0:4 * GW:GW], T.vp[:, 192:4 * 384:384], AF.Copy, ["vp.s%d" % t for t in range(4)], ["gp.z"])
+        ts(T.flg[:], T.ww[:, 0:C], -300.0, None, Op.is_lt, None, ["ww"], ["flg"])
+        scan(T.exw[:], T.m16[:], T.ww[:, 0:C], 0.0, Op.mult, Op.min, ["m16", "ww"], ["exw"])
         scan(T.st[:], T.flg[:], T.flg[:], 0.0, Op.add, Op.max, ["flg"], ["st"])
-        ts(T.wa[:], T.exw[:, 15:C:16], T.pf[:, 4:5], None, Op.add, None, ["exw", "pf.q"], ["wa"])
+        ts(T.wa[:], T.exw[:, 15:C:16], T.pw[:, 47:48], -255.0, Op.mult, Op.add, ["exw", "pw"], ["wa"])
         scan(T.exs[:], T.mb[:], T.st[:], 0.0, Op.max, Op.min, ["mb", "st"], ["exs"])
         tt(T.lf[:], T.wa[:], T.exs[:, 15:C:16], Op.min, ["wa", "exs"], ["lf"])
-        ts(T.lo[:], T.lf[:], 191.0, None, Op.add, None, ["lf"], ["lo"])
-        act(T.gp[:, 161:1 + C], T.vp[:, 0:384].indirect(T.lo[:, 10:18]), AF.Copy, ["vp.s0", "vp.d0", "lo"], ["gp.h"])
-        cp(T.gp[:, 1:161], T.vp[:, 0:384].indirect(T.lo[:, 0:10]), ["vp.s0", "vp.d0", "lo"], ["gp.0"])
-        for t in (1, 2, 3):
-            act(T.gp[:, GW * t + 1:GW * t + 1 + C], T.vp[:, 384 * t:384 * t + 384].indirect(T.lo[:]), AF.Copy,
-                ["vp.s%d" % t, "vp.d%d" % t, "lo"], ["gp.%d" % t])
-        for t in range(4):
-            tt(T.zt[:, t:4 * C:4], T.gp[:, GW * t + 1:GW * t + 1 + C], T.gp[:, GW * t:GW * t + C], Op.add, ["gp.%d" % t, "gp.z", "gp.h"], ["zt.%d" % t])
-        qz(T.qz[:], T.sz[:], T.zt[:], ["zt.%d" % t for t in range(4)], ["qz"])
-        for b in range(4):
-            mx(T.pr[:, 512 * b:512 * b + C], T.qw[:, 128 * b:128 * b + 128], T.sw[:, 128 * b:128 * b + 128], T.qz[:], T.sz[:], True, True,
-               ["qw", "qz"], ["P:r%d" % b])
-        for t in range(4):
-            o, i = T.zp[:, C * t:C * t + C], T.zt[:, t:4 * C:4]
-            if t < 2:
-                act(o, i, AF.Copy, ["zt.%d" % t], ["zp.%d" % t], scale=32.0)
-            else:
-                ts(o, i, 32.0, None, Op.mult, None, ["zt.%d" % t], ["zp.%d" % t])
         if last:
-            act(T.lsb[:, 0:C], T.cm[:].indirect(T.lo[:]), AF.Copy, ["cm", "lo"], ["lsb.a"])
-            dmas("s", "stl", [(T.ls[:], T.lsb[0:128:16, :])], ["lsb.a", "lsb.b"], [])
-        for b in range(4):
-            tt(T.xp[:, C * b:C * b + C], T.pr[:, 512 * b:512 * b + C], T.zp[:, C * b:C * b + C], Op.add, ["P:r%d" % b, "zp.%d" % b], ["xp.%d" % b])
-            o, i = T.xn[:, b:4 * C:4], T.xp[:, C * b:C * b + C]
-            if b < 3:
-                act(o, i, AF.Copy, ["xp.%d" % b], ["xn.%d" % b], scale=2.0 ** -5)
-            else:
-                ts(o, i, 2.0 ** -5, None, Op.mult, None, ["xp.%d" % b], ["xn.%d" % b])
-        qx_of(T.xn, ["xn.%d" % b for b in range(4)])
+            act(T.lsb[:, C:480], T.r2[:].indirect(T.lst[:, 56:68]), AF.Copy, ["r2.0", "r2.1", "lst.e"], ["lsb.b"], scale=0.5)
+            act(T.cm[:, 0:192], T.jv[:, 0:192], AF.Identity, ["jv"], ["cm"], bias=288.0)
+        ts(T.lo[:], T.lf[:], 191.0, None, Op.add, None, ["lf"], ["lo"])
 
-    H = 160
-    mx(T.ps1[:, 0:C - H], T.qv[:], T.sv[:], T.qx[:, H:C], T.sx[:, H:C], True, True, ["qv", "qx.b"], ["P:1"])
-    mx(T.pc[:, 0:H], T.qv[:], T.sv[:], T.qx[:, 0:H], T.sx[:, 0:H], True, True, ["qv", "qx.a"], ["P:c"])
-    dmas("s", "sto", [(T.oc[:], T.qx[:].bitcast(dt.uint8))] + [(T.osc[4 * k:4 * k + 4, :], T.sx[32 * k:32 * k + 4, :]) for k in range(4)],
+        def gather(e, t, h):
+            a, b = run[h]
+            move(e, T.gp[:, GW * t + 1 + a:GW * t + 1 + b], T.vp[:, 384 * t:384 * t + 384].indirect(T.lo[:, a // 16:b // 16]),
+                 ["vp.s%d" % t, "vp.d%d" % t, "lo"], ["gp.%s%d" % (h, t)])
+
+        def blend(t, h):
+            a, b = run[h]
+            o = GW * t
+            tt(T.zt[:, 4 * a + t:4 * b:4], T.gp[:, o + 1 + a:o + 1 + b], T.gp[:, o + a:o + b], Op.add,
+               ["gp.a%d" % t, "gp.z" if h == "a" else "gp.b%d" % t], ["zt.%s%d" % (h, t)])
+
+        def pb_(h, t):
+            return t if h == "a" else 4 + t
+
+        def layer(h):
+            a, b = run[h]
+            qz(T.qz[:, a:b], T.sz[:, a:b], T.zt[:, 4 * a:4 * b], ["zt.%s%d" % (h, t) for t in range(4)], ["qz." + h])
+            for t in range(4):
+                mx(bank(pb_(h, t), 0, b - a), T.qw[:, 128 * t:128 * t + 128], T.sw[:, 128 * t:128 * t + 128], T.qz[:, a:b], T.sz[:, a:b], True, True,
+                   ["qw", "qz." + h], ["P:%d" % pb_(h, t)])
+
+        def z32(h):
+            a, b = run[h]
+            for t in range(4):
+                scale("a", T.zp[:, 4 * a + t:4 * b:4], T.zt[:, 4 * a + t:4 * b:4], 32.0, ["zt.%s%d" % (h, t)], ["zp.%s%d" % (h, t)])
+
+        def state(t, h):
+            a, b = run[h]
+            tt(T.xp[:, C * t + a:C * t + b], bank(pb_(h, t), 0, b - a), T.zp[:, 4 * a + t:4 * b:4], Op.add,
+               ["P:%d" % pb_(h, t), "zp.%s%d" % (h, t)], ["xp.%s%d" % (h, t)])
+
+        def back(e, t, h):
+            a, b = run[h]
+            scale(e, T.xn[:, 4 * a + t:4 * b:4], T.xp[:, C * t + a:C * t + b], 2.0 ** -5, ["xp.%s%d" % (h, t)], ["xn.%s%d" % (h, t)])
+
+        def xns(h):
+            return ["xn.%s%d" % (h, t) for t in range(4)]
+
+        for t in (2, 3):
+            gather("a", t, "a")
+        for t in (0, 1):
+            gather("v", t, "a")
+        for t in range(4):
+            gather("a", t, "b")
+        for t in (0, 2, 1, 3):
+            blend(t, "a")
+        blend(0, "b")
+        layer("a")
+        z32("a")
+        for t in (1, 2, 3):
+            blend(t, "b")
+        state(0, "a")
+        layer("b")
+        z32("b")
+        for t in range(1, 4):
+            state(t, "a")
+        for t in range(4):
+            back("aavv"[t], t, "a")
+        state(0, "b")
+        qx_of(T.xn, "a", xns("a"))
+        if last:
+            mx(bank(0, 0, H), T.qv[:], T.sv[:], T.qx[:, 0:H], T.sx[:, 0:H], True, True, ["qv", "qx.a"], ["P:0"])
+            dmas("s", "stp", [(T.oc[:, 0:4 * H], T.qx[:, 0:H].bitcast(dt.uint8))], ["qx.a"], [])
+        else:
+            scores_a()
+        for t in range(1, 4):
+            state(t, "b")
+        for t in range(3):
+            back("a", t, "b")
+        if last:
+            act(T.yb[:, 0:H], bank(0, 0, H), AF.Copy, ["P:0"], ["yb.0"])
+            dmas("a", "stz", [(T.y[:, 0:H], T.yb[:, 0:H])], ["yb.0"], [])
+            act(T.lsb[:, 0:C], T.cm[:].indirect(T.lo[:]), AF.Copy, ["cm", "lo"], ["lsb.a"])
+            dmas("a", "stl", [(T.ls[:], T.lsb[0:128:16, :])], ["lsb.a", "lsb.b"], [])
+            back("v", 3, "b")
+            qx_of(T.xn, "b", xns("b"))
+        else:
+            hold1("a")
+            back("v", 3, "b")
+            hold2("a")
+            rows(AEARLY)
+            qx_of(T.xn, "b", xns("b"))
+            scores_b()
+            diag("a")
+
+    mx(bank(1, 0, C - H), T.qv[:], T.sv[:], T.qx[:, H:C], T.sx[:, H:C], True, True, ["qv", "qx.b"], ["P:1"])
+    dmas("s", "sto", [(T.oc[:, 4 * H:], T.qx[:, H:C].bitcast(dt.uint8))] + [(T.osc[4 * k:4 * k + 4, :], T.sx[32 * k:32 * k + 4, :]) for k in range(4)],
          ["qx.a", "qx.b"], [])
-    act(T.yb[:, H:C], T.ps1[:, 0:C - H], AF.Copy, ["P:1"], ["yb.1"])
-    dmas("a", "stz", [(T.y[:, H:C], T.yb[:, H:C])], ["yb.1"], [])
-    cp(T.yb[:, 0:H], T.pc[:, 0:H], ["P:c"], ["yb.0"])
-    dmas("a", "sty", [(T.y[:, 0:H], T.yb[:, 0:H])], ["yb.0"], [])
-    stores = ("stl", "sto", "stz", "sty")
+    cp(T.yb[:, H:C], bank(1, 0, C - H), ["P:1"], ["yb.1"])
+    dmas("s", "sty", [(T.y[:, H:C], T.yb[:, H:C])], ["yb.1"], [])
+    stores = ("stl", "stp", "sto", "stz", "sty")
     for s in SEMAPHORES:
         if count.get(s, 0) > waited.get(s, 0) and s not in stores:
             g.wait_ge(T.sem[s], count[s])

@@ -5,15 +5,19 @@ C, L, R = 288, 96, 3
 H = 160
 BIG = 1.0e29
 F8, U8, BF, F32, I32, U16 = "float8_e4m3fn_x4", "uint8", "bfloat16", "float32", "int32", "uint16"
-GW = 304
 EW = 520
 TW = [288, 224, 160, 128, 128]
-RP = 112
-VTOP = 14
-AEARLY = [9, 8, 7]
-ALATE = [17, 16, 15]
-VC = [(0, 5), (0, 2)] + [(1, _c) for _c in range(6)]
-SP = 160
+RP = 136
+FIRST = 96
+QUEUE = ("g0 g2 G0 g1 G2 g3 G1 G3 b4 b6 b8 b10 B4 B6 B8 b5 B10 b7 F0 b9 b11 B5 B7 B9 B11 nf0 Ov006 F1 nt0 Ov104 Oa146 nf1 ny0 nt1 nk na nv ny1 "
+         "Ev0 r0 r1 r2 r3 r4 r5 Ea2 t0 w0 w1 w2 s0 nj P Ea3 Ev1 t2 xv0 t3 t1 s1 xa2 xv3 xa1 U0 U1 "
+         "ca11 ca10 ca9 ca8 ca7 cv5 cv4 cv3 cv2 cv1 cv0 cv6 d5 d4 d3 d2 d1 d6 d0 U2 J U3")
+ORDER = ("Gv0-24 Ga48-96 Gv24-48 Ga96-160 Ga160-224 Ga224-288 B0-24 B24-48 B48-96 B96-160 B160-224 La Za0-160 B224-288 Za160-288 Sa0 Lb Sa1 Sa2 Kaa1 Kaa0 Sa3 Kva2 "
+         "Sb0 Kva3 Sb2 Kab2 Xa Sb1 Kab1 Sb3 Kvb0 Kvb3 ha Xb Ha p9 p8 P9 P8 b7 hb b3 Da b4 a7 Hb b1 b5 b2 p12 p11 p10 p13 P12 P10 P13 P11 "
+         "e Db b15 b6 d b16 b17 s15 b14 j0-1 q4 q0 q2 q3 q1 a5 a6 a4 s16 s2 s1 s3 s14 s17 j4-14 x")
+LAST = ("Gv0-24 Ga48-96 Gv24-48 Ga96-160 Ga160-224 Ga224-288 lw B0-24 B24-48 B48-96 B96-160 lf B160-224 La Za0-160 B224-288 lo Za160-288 o0 Sa0 Lb Sa1 Sa2 Kaa0 Kaa1 "
+        "Sa3 Kva2 Sb0 o1 o2 Sb1 Sb2 Kva3 Sb3 Kvb0 Kvb1 Kvb2 Xa Kvb3 y Xb")
+MASKS = ["eqm", "mb", "mi", "kk", "kz", "m16", "km", "eq4", "mi4", "m4", "mb8", "(mb8 is twice as long)"]
 
 
 def _sb(n, d):
@@ -26,39 +30,37 @@ SCRATCH = {
     "qw": _sb(512, F8), "sw": _sb(512, U8),
     "qur": _sb(128, F8), "sur": _sb(128, U8), "quc": _sb(32, F8), "suc": _sb(32, U8),
     "qul": _sb(64, F8), "sul": _sb(64, U8), "qu2": _sb(256, F8), "su2": _sb(256, U8),
-    "pi": _sb(2, I32), "ti": _sb(6, I32), "pf": _sb(8, F32), "li": _sb(80, I32), "lst": _sb(80, U16),
+    "pi": _sb(2, I32), "ti": _sb(8, I32), "pf": _sb(12, F32), "li": _sb(80, I32), "lst": _sb(80, U16),
     "la": _sb(8, U16), "lb": _sb(8, U16), "qh": _sb(L * R, F8), "sh": _sb(128 * R, U8),
-    "km": _sb(C, BF), "eqm": _sb(C, BF), "mb": _sb(C, BF), "mi": _sb(C, BF), "kk": _sb(C, BF), "kz": _sb(C, BF),
-    "m16": _sb(C, BF), "pw": _sb(48, F32),
-    "c16": _sb(18, F32), "ja": _sb(12, F32), "jv": _sb(C, F32), "idn": _sb(192, F32), "ngn": _sb(192, BF),
-    "obi": _sb(512, BF), "obt": _sb(512, BF), "qob": _sb(128, F8), "sob": _sb(128, U8),
+    "mk": _sb(C * len(MASKS), BF), "pw": _sb(56, F32),
+    "c16": _sb(18, F32), "ja": _sb(6, F32), "jv": _sb(C, F32), "idn": _sb(L, F32), "ngn": _sb(192, BF),
+    "obt": _sb(512, BF), "qob": _sb(128, F8), "sob": _sb(128, U8),
     "one": _sb(EW, BF), "et": _sb(2 * EW, BF), "qe": _sb(512, F8), "se": _sb(512, U8),
-    "mm": _sb(C, F32), "hh": _sb(C, F32), "sga": _sb(8 * 18 * 17, BF), "jka": _sb(8 * 10 * 11, BF),
-    "rs": _sb(18 * RP, F32), "rsd": _sb(C, BF), "rs2": _sb(18, F32), "ext": _sb(C, F32),
-    "rkf": _sb(18, F32), "rko": _sb(18, U16), "cm": _sb(384, F32), "ex2": _sb(C, F32), "oro": _sb(18, U16),
-    "xp": _sb(4 * C, BF), "at": _sb(512, BF), "vp": _sb(4 * 384, BF), "gp": _sb(4 * GW, BF),
+    "mm": _sb(C, F32), "hh": _sb(C, F32), "sga": _sb(8 * 18 * 17, BF), "jka": _sb(8 * 18 * 17, BF),
+    "rs": _sb(18, F32), "rb": _sb(18 * RP, BF), "rsd": _sb(C, BF), "ext": _sb(C, F32),
+    "rkf": _sb(18, F32), "rko": _sb(18, U16), "cm": _sb(384, F32), "ex2": _sb(C, F32), "oro": _sb(72, U16),
+    "xp": _sb(4 * C, BF), "at": _sb(512, BF), "vp": _sb(4 * 384, BF), "gp": _sb(4 * C + 4, BF),
     "zt": _sb(4 * C, BF), "zp": _sb(4 * C, BF), "qz": _sb(C, F8), "sz": _sb(C, U8),
-    "ma": _sb(192, F32), "ha": _sb(192, F32), "rep": _sb(2 * C, F32), "pb": _sb(8 * C, BF), "sgp": _sb(6 * C, BF),
-    "jkp": _sb(6 * C, BF), "yh": _sb(2, F32), "y0": _sb(6 * 144, F32), "y1": _sb(6 * 144, BF),
-    "ee": _sb(384, BF), "r2": _sb(384, BF), "kys": _sb(192, F32), "f2": _sb(12, F32), "ka": _sb(12, F32), "b2": _sb(12, F32),
-    "kb": _sb(384 + 6 * 98, BF), "jkq": _sb(12 * 192, BF), "rk": _sb(12, F32), "rh": _sb(6 * 96, F32), "ini": _sb(8, F32),
-    "plf": _sb(12 * 96, F32), "plo": _sb(12, U16),
-    "ww": _sb(384, BF), "flg": _sb(C, BF), "st": _sb(C, BF), "exw": _sb(C, BF), "exs": _sb(C, BF),
-    "wa": _sb(18, F32), "lf": _sb(18, F32), "lo": _sb(18, U16), "lsb": _sb(480, F32), "yb": _sb(C, F32),
+    "ma": _sb(192, F32), "ha": _sb(192, F32), "rep": _sb(2 * C, F32), "pb": _sb(12 * C, BF), "sgp": _sb(6 * C, BF),
+    "jkp": _sb(6 * C, BF), "y0": _sb(6 * 144, F32), "y1": _sb(6 * 144, BF),
+    "eo": _sb(192, BF), "ro": _sb(192, BF), "kyo": _sb(L, F32), "so": _sb(24, F32), "kb": _sb(18 * L, BF), "jkq": _sb(18 * L, BF),
+    "rh": _sb(6, F32), "ee": _sb(384, BF), "r2": _sb(384, BF), "xr": _sb(192, BF), "sc2": _sb(12, BF),
+    "rk": _sb(12 * 48, F32), "plf": _sb(12 * 49, BF), "kt": _sb(98, BF), "plo": _sb(12, U16),
+    "ww": _sb(384, BF), "flg": _sb(C, BF), "st": _sb(2 * C, BF), "exw": _sb(2 * C, BF), "exs": _sb(3 * C, BF),
+    "wa": _sb(18, F32), "lf": _sb(18, F32), "lo": _sb(90, U16), "lsb": _sb(480, F32), "yb": _sb(C, F32),
     "hs": _sb(20 * R, F32), "qa": _sb(128 * R, F8), "sa": _sb(128 * R, U8), "ql": _sb(192 * R, F8), "sl": _sb(192 * R, U8),
-    "fm": _sb(32 * R, BF), "fl": _sb(32 * R, BF), "sc": ("dram", [2 * R, 128, 18], F32),
+    "fm": _sb(32 * R, BF), "fl": _sb(32 * R, BF), "pm": _sb(C * R, BF), "pl": _sb(16 * R, BF), "sc": ("dram", [2 * R, 128, 18], F32),
     "ps": ("psum", [128, 4096], F32),
 }
 for _a in range(5):
     _w = C if _a == 4 else TW[_a]
-    SCRATCH["bt%d" % _a] = _sb(4 * _w, BF)
+    SCRATCH["bt%d" % _a] = _sb(4 * TW[_a], BF)
     SCRATCH["qb%d" % _a] = _sb(_w, F8)
     SCRATCH["sb%d" % _a] = _sb(_w, U8)
 
 SEMAPHORES = ["cv", "ca", "cp", "cg", "ldx", "ldy", "ldu", "ldw", "sent", "uarr", "sty", "stz", "sto", "stp", "stl"]
 for _r in range(R):
-    SEMAPHORES += ["%s%d" % (_n, _r) for _n in ("qarr", "harr", "sca", "scb", "rpa", "rpb")]
-    SEMAPHORES += ["farr%d0" % _r, "farr%d1" % _r]
+    SEMAPHORES += ["%s%d" % (_n, _r) for _n in ("qarr", "harr", "sca", "scb", "rpa", "rpb", "parr")] + ["farr%d%d" % (_r, _h) for _h in range(2)]
 
 
 def helpers(c, T, topo):
@@ -179,6 +181,9 @@ def rank_program(g, core, T, topo):
     def scan(out, d0, d1, init, o0, o1, reads, writes):
         op("v", lambda: V.tensor_tensor_scan(out, d0, d1, init, o0, o1), reads, writes)
 
+    def turn(out, in_, reads, writes):
+        op("v", lambda: V.transpose(out, in_), reads, writes)
+
     def qz(q, s, t, reads, writes):
         op("v", lambda: V.quantize_mx(q, s, t), reads, writes)
 
@@ -212,18 +217,17 @@ def rank_program(g, core, T, topo):
     def bank(k, a, b):
         return T.ps[:, 512 * k + a:512 * k + b]
 
+    def mk(name, a=0, b=C, step=1):
+        o = C * MASKS.index(name)
+        return T.mk[:, o + a:o + b:step]
+
     rcv = [(rank + 1) % N, (rank + 2) % N]
     snd = [(rank - 1) % N, (rank - 2) % N]
     run = {"a": (0, H), "b": (H, C)}
+    top = {k: max(int(w[1:]) for w in ORDER.split() if w[0] == k) for k in "pb"}
 
     def slot_at(d):
         return 0 if rank == min((d - 1) % N, (d - 2) % N) else 1
-
-    def xps(t):
-        return ["xp.a%d" % t, "xp.b%d" % t]
-
-    def xplane(t):
-        act(T.xp[:, C * t:C * t + C], T.xt[:, t:4 * C:4], AF.Copy, ["xt.a", "xt.b"], xps(t), scale=32.0)
 
     def qx_of(t, h, reads):
         a, b = run[h]
@@ -240,19 +244,20 @@ def rank_program(g, core, T, topo):
 
     def scores_b():
         scores(BV, H, C, ["qx.b"])
-        scores(SA, 0, C - 16, ["qx.a", "qx.b"])
-        scores(SV, 0, 16 * VTOP, ["qx.a", "qx.b"])
+        for k, e in ((SV, "b"), (SA, "p")):
+            if 16 * top[e] > H:
+                scores(k, 0, 16 * top[e], ["qx.a", "qx.b"])
 
     def src_of(h):
         return (bank(AV, 0, H), "P:%d" % AV) if h == "a" else (bank(BV, 0, C - H), "P:%d" % BV)
 
     def hold1(h):
         a, b = run[h]
-        tt(T.mm[:, a:b], src_of(h)[0], T.mb[:, a:b], Op.min, [src_of(h)[1], "mb"], ["mm." + h])
+        tt(T.mm[:, a:b], src_of(h)[0], mk("mb", a, b), Op.min, [src_of(h)[1], "mb"], ["mm." + h])
 
     def hold2(h):
         a, b = run[h]
-        scan(T.hh[:, a:b], T.kk[:, a:b], T.mm[:, a:b], 0.0, Op.min, Op.max, ["kk", "mm." + h], ["hh." + h])
+        scan(T.hh[:, a:b], mk("kk", a, b), T.mm[:, a:b], 0.0, Op.min, Op.max, ["kk", "mm." + h], ["hh." + h])
 
     def diag(h):
         a, b = run[h]
@@ -284,31 +289,23 @@ def rank_program(g, core, T, topo):
         mx(bank(CS, 0, w), T.qob[:], T.sob[:], T["qb%d" % t][:, 0:w], T["sb%d" % t][:, 0:w], start, stop, ["qob", "qb%d" % t], ["P:%d" % CS])
 
     def p1(c):
-        o, k = 8 * c * (c - 1), AA if 16 * c < H else SA
+        o, k = 8 * c * (c - 1), AA if 16 * c <= H else SA
         act(T.sga[:, o:o + 16 * c], bank(k, 0, 16 * c), AF.Sign, ["P:%d" % k, hname(c)], ["sga.%d" % c], bias=T.hh[:, 16 * c + 15:16 * c + 16], scale=-1.0)
 
     def p2(c):
         o = 8 * c * (c - 1)
-        act(lview(c, 0, 16 * c), T.sga[:, o:o + 16 * c], AF.Relu, ["sga.%d" % c], [lname(c), "rs.%d" % c],
-            accum_out=T.rs[:, RP * c + RP - 1:RP * c + RP])
-
-    def rows(cs):
-        p1(cs[0])
-        for c, d in zip(cs[1:], cs):
-            p1(c)
-            p2(d)
-        p2(cs[-1])
+        act(lview(c, 0, 16 * c), T.sga[:, o:o + 16 * c], AF.Relu, ["sga.%d" % c], [lname(c), "rs.%d" % c], accum_out=T.rs[:, c:c + 1])
 
     def bits(c):
         k = AV if 16 * c <= H else SV
         ts(lview(c, 0, 16 * c), bank(k, 0, 16 * c), T.hh[:, 16 * c + 15:16 * c + 16], None, Op.is_lt, None, ["P:%d" % k, hname(c)], [lname(c)])
 
     def rsum(c):
-        scan(T.rs[:, RP * c + RP - 8 * c:RP * c + RP], lview(c, 0, 8 * c), lview(c, 8 * c, 16 * c), 0.0, Op.add, Op.add, [lname(c)], ["rs.%d" % c])
+        scan(T.rb[:, RP * c + RP - 8 * c:RP * c + RP], lview(c, 0, 8 * c), lview(c, 8 * c, 16 * c), T.rsd[:, 16 * c + 15:16 * c + 16], Op.add, Op.add,
+             [lname(c), "rsd"], ["rb.%d" % c])
 
     def asum(c):
-        act(T.jka[:, 8 * c * (c - 1):8 * c * (c + 1)], lview(c, 0, 16 * c), AF.Copy, [lname(c)], ["rs.%d" % c],
-            accum_out=T.rs[:, RP * c + RP - 1:RP * c + RP])
+        act(T.jka[:, 8 * c * (c - 1):8 * c * (c + 1)], lview(c, 0, 16 * c), AF.Copy, [lname(c)], ["rs.%d" % c], accum_out=T.rs[:, c:c + 1])
 
     dmas("a", "ldu", [(T.ut[:], T.u[:])], [], ["ut"])
     dmas("s", "ldx", [(T.xt[:, 0:4 * H], T.x[:, 0:4 * H])], [], ["xt.a"])
@@ -316,25 +313,29 @@ def rank_program(g, core, T, topo):
     dmas("s", "ldw", [(T.qw[:].bitcast(dt.uint8), T.wc[:]), (T.sw[:], T.ws[:]), (T.vt[:], T.v[:])], ["xt.a", "xt.b"], ["qw", "vt"])
     iota(T.li[:, 0:8], [[16, 8]], 0, 0, ["li.a"])
     iota(T.pi[:], [[0, 2]], 0, 1, ["pi"])
-    iota(T.km[:], [[0, 18], [1, 16]], 0, 0, ["km"], True)
-    iota(T.c16[:], [[16, 18]], 0, 0, ["c16"], True)
-    iota(T.obi[:], [[1, 8], [0, 64]], 0, 0, ["obi"], True)
+    iota(mk("km"), [[0, 18], [1, 16]], 0, 0, ["km"], True)
     iota(T.li[:, 10:18], [[1, 8]], 0, 0, ["li.b"])
+    iota(T.c16[:], [[16, 18]], 0, 0, ["c16"], True)
     ms(T.one[:], 1.0, ["one"])
-    ms(T.kk[:], BIG, ["kk"])
+
+    def ones(in_, base, cmul, reads):
+        op("g", lambda: g.affine_select(T.obt[:], in_, [[-16 * cmul, 8], [0, 64]], Op.is_ge, 0.0, base, cmul), reads, ["obt"])
+
+    ones(T.one[:, 0:512], 0, 1, ["one"])
+    ms(mk("kk"), BIG, ["kk"])
     cp(T.la[:], T.li[:, 0:8], ["li.a"], ["la"])
-    ts(T.ti[:, 4:6], T.pi[:], 7, None, Op.bitwise_and, None, ["pi"], ["ti.3"])
+    ts(T.ti[:, 6:8], T.pi[:], 7, None, Op.bitwise_and, None, ["pi"], ["ti.6"])
     ts(T.ti[:, 0:1], T.pi[:, 0:1], 15, None, Op.bitwise_and, None, ["pi"], ["ti.0"])
     ts(T.ti[:, 1:2], T.pi[:, 0:1], 31, None, Op.bitwise_and, None, ["pi"], ["ti.1"])
-    ts(T.ti[:, 2:3], T.pi[:, 0:1], 4, None, Op.logical_shift_right, None, ["pi"], ["ti.2"])
-    ts(T.lst[:, 0:2], T.ti[:, 4:6], 16.0, None, Op.mult, None, ["ti.3"], ["lc"])
-    ms(T.kk[:, 0:C:16], -BIG, ["kk"])
-    cp(T.pf[:, 0:3], T.ti[:, 0:3], ["ti.0", "ti.1", "ti.2"], ["pf"])
-    ts(T.eqm[:], T.km[:], T.pf[:, 0:1], None, Op.is_equal, None, ["km", "pf"], ["eqm"])
-    for a, lo_ in ((2, 112), (3, 48), (4, 0), (0, 240)):
+    ts(T.ti[:, 2:3], T.pi[:, 0:1], 15, 2, Op.bitwise_and, Op.logical_shift_right, ["pi"], ["ti.2"])
+    ts(T.ti[:, 3:4], T.pi[:, 0:1], 3, None, Op.bitwise_and, None, ["pi"], ["ti.3"])
+    ts(T.lst[:, 0:2], T.ti[:, 6:8], 16.0, None, Op.mult, None, ["ti.6"], ["lc"])
+    ms(mk("kk", 0, C, 16), -BIG, ["kk"])
+    cp(T.pf[:, 0:4], T.ti[:, 0:4], ["ti.0", "ti.1", "ti.2", "ti.3"], ["pf"])
+    ts(mk("eqm"), mk("km"), T.pf[:, 0:1], None, Op.is_equal, None, ["km", "pf"], ["eqm"])
+    for a, lo_ in ((4, 0), (2, 112), (3, 48), (0, 240)):
         pad(a, lo_)
-    ms(T.bt4[:, 512:], 0.0, ["bt4.z"])
-    ts(T.mb[:], T.eqm[:], 2.0 * BIG, -BIG, Op.mult, Op.add, ["eqm"], ["mb"])
+    cp(T.lb[:], T.li[:, 10:18], ["li.b"], ["lb"])
     qz(T.qu[:], T.su[:], T.ut[:], ["ut"], ["qu"])
     qx_of(T.xt, "a", ["xt.a"])
     act(T.sur[:], T.su[:].indirect(T.la[:]), AF.Copy, ["qu", "la"], ["sur"])
@@ -343,94 +344,155 @@ def rank_program(g, core, T, topo):
     scores_a()
     cp(T.quc[:].bitcast(dt.uint32), T.qu[:].bitcast(dt.uint32).indirect(T.lst[:, 0:2]), ["qu", "lc"], ["quc"])
     pad(1, 176)
-    fill(T.kz[:], C, 512.0, ["kz"])
-    fill(T.rs[:, RP - 1:RP], 1, 0.0, ["rs.0"])
-    act(T.kz[:, 0:C:16], T.c16[:], AF.Identity, ["c16"], ["kz"], scale=-1.0, bias=128.0)
+    fill(mk("kz"), C, 512.0, ["kz"])
+    fill(T.rs[:], 18, 0.0, ["rs.%d" % c for c in range(18)])
+    act(mk("kz", 0, C, 16), T.c16[:], AF.Identity, ["c16"], ["kz"], scale=-1.0, bias=128.0)
     items = []
     for e in range(2):
         items.append((T.cores[snd[e]], T.quc[:, 0:8].bitcast(dt.uint8), T.qul[:, 32 * e:32 * e + 8].bitcast(dt.uint8), "uarr"))
         items.append((T.cores[snd[e]], T.suc[:], T.sul[:, 32 * e:32 * e + 32], "uarr"))
     send(items, ["quc", "suc"])
     arrives("uarr", 2 * share(rcv[0], 4) + 2 * share(rcv[1], 4), ["qul.0", "qul.1"])
+    ts(mk("mb"), mk("eqm"), 2.0 * BIG, -BIG, Op.mult, Op.add, ["eqm"], ["mb"])
     qx_of(T.xt, "b", ["xt.b"])
-    hold1("a")
     scores_b()
-    cp(T.lb[:], T.li[:, 10:18], ["li.b"], ["lb"])
-    hold2("a")
-    ts(T.obt[:], T.obi[:], T.pf[:, 2:3], None, Op.is_equal, None, ["obi", "pf"], ["obt"])
-    rows(AEARLY)
-    diag("a")
+    ones(T.obt[:], 15, -1, ["obt"])
+
+    def zeros(a):
+        qz(T.qb4[:, a:a + 128], T.sb4[:, a:a + 128], T.bt4[:], ["bt4.%s" % k for k in "0123b"], ["qb4"])
+
+    gaps = {"ha": lambda: zeros(128), "Ha": lambda: zeros(160),
+            "q2": lambda: ts(mk("mi"), mk("eqm"), 1049600.0, -1024.0, Op.mult, Op.add, ["eqm"], ["mi"])}
+
+    vps = ["vp.s"] + ["vp.d%d" % b for b in range(4)]
+
+    def span(k):
+        a, b = k.split("-")
+        return int(a), int(b)
+
+    def cols(name, a, b):
+        return ["%s.%d" % (name, k) for k in range(max(a, 0) // 8, (b + 7) // 8)]
+
+    def gather(k):
+        a, b = span(k[1:])
+        move(k[0], T.gp[:, 4 * a + 4:4 * b + 4], T.vp[:].indirect(T.lo[:, a // 4:b // 4]), vps + cols("lo", a, b), cols("gp", a, b))
+
+    def blend(k):
+        a, b = span(k)
+        tt(T.zt[:, 4 * a:4 * b], T.gp[:, 4 * a + 4:4 * b + 4], T.gp[:, 4 * a:4 * b], Op.add, ["gp.z"] + cols("gp", a - 1, b), cols("zt", a, b))
+
+    def pb_(h, t):
+        return t if h == "a" else 4 + t
+
+    def layer(h):
+        a, b = run[h]
+        qz(T.qz[:, a:b], T.sz[:, a:b], T.zt[:, 4 * a:4 * b], cols("zt", a, b), ["qz." + h])
+        for t in range(4):
+            mx(bank(pb_(h, t), 0, b - a), T.qw[:, 128 * t:128 * t + 128], T.sw[:, 128 * t:128 * t + 128], T.qz[:, a:b], T.sz[:, a:b], True, True,
+               ["qw", "qz." + h], ["P:%d" % pb_(h, t)])
+
+    def z32(k):
+        a, b = span(k[1:])
+        scale(k[0], T.zp[:, 4 * a:4 * b], T.zt[:, 4 * a:4 * b], 32.0, cols("zt", a, b), cols("zp", a, b))
+
+    def state(k):
+        h, t = k[0], int(k[1])
+        a, b = run[h]
+        tt(T.xp[:, 4 * a + t:4 * b:4], bank(pb_(h, t), 0, b - a), T.zp[:, 4 * a + t:4 * b:4], Op.add,
+           ["P:%d" % pb_(h, t)] + cols("zp", a, b), ["xp.%s%d" % (h, t)])
+
+    def back(k):
+        e, h, t = k[0], k[1], int(k[2])
+        a, b = run[h]
+        scale(e, T.xn[:, 4 * a + t:4 * b:4], T.xp[:, 4 * a + t:4 * b:4], 2.0 ** -5, ["xp.%s%d" % (h, t)], ["xn.%s%d" % (h, t)])
+
+    def xns(h):
+        return ["xn.%s%d" % (h, t) for t in range(4)]
+
+    def anew(h):
+        qx_of(T.xn, h, xns(h))
+        (scores_a if h == "a" else scores_b)()
+
+    def inside(_):
+        scan(T.rsd[:], mk("kz"), T.bt0[:, 0:4 * C:4], 512.0, Op.min, Op.add, ["kz", "bt0.a", "bt0.b"], ["rsd"])
+
+    ends, rbs = T.rb[:, RP - 1:18 * RP:RP], ["rb.%d" % c for c in range(18)]
+
+    def join(k):
+        a, b = span(k)
+        tt(T.rb[:, RP * a + RP - 1:RP * b:RP], T.rs[:, a:b], T.rsd[:, 16 * a + 15:16 * b:16], Op.add, ["rs.%d" % c for c in range(a, b)] + ["rsd"], rbs[a:b])
+
+    def number(f):
+        return lambda k: f(int(k))
+
+    renew = {"G": gather, "B": blend, "L": layer, "Z": z32, "S": state, "K": back, "X": anew}
 
     for r in range(R):
         first, last = r == 0, r == R - 1
         hs = T.hs[:, 20 * r:20 * r + 18]
         qa, sa = T.qa[:, 128 * r:128 * r + 128], T.sa[:, 128 * r:128 * r + 128]
         ql, sl = T.ql[:, 192 * r:192 * r + 192], T.sl[:, 192 * r:192 * r + 192]
-
-        low = [c for c in range(9, 0, -1) if c not in AEARLY + ALATE]
-        bits(low[0])
-        hold1("b")
-        for c in low[-2:]:
-            bits(c)
-        hold2("b")
-        rows(ALATE)
-        if first:
-            qz(T.qob[:], T.sob[:], T.obt[:], ["obt"], ["qob"])
-        else:
-            quant(4)
-        cp(hs, T.hh[:, 15:C:16], ["hh.a", "hh.b"], ["hs%d" % r])
-        send([(T.cores[snd[e]], hs, T.sc[2 * r + e], "%s%d" % (("sca", "scb")[e], r)) for e in range(2)], ["hs%d" % r])
+        xs, xnames = (T.xt, ["xt.a", "xt.b"]) if first else (T.xn, xns("a") + xns("b"))
 
         def spread(e, q):
             arrives("%s%d" % (("sca", "scb")[e], r), share(rcv[e], 2), ["sc%d.%d" % (r, e)])
             dmas(q, "%s%d" % (("rpa", "rpb")[e], r), [(T.rep[i:128:16, C * e:C * e + C], T.sc[2 * r + e]) for i in range(16)],
                  ["sc%d.%d" % (r, e)], ["rep.%d" % e])
 
-        spread(0, "s")
+        def tell(_):
+            cp(hs, T.hh[:, 15:C:16], ["hh.a", "hh.b"], ["hs%d" % r])
+            send([(T.cores[snd[e]], hs, T.sc[2 * r + e], "%s%d" % (("sca", "scb")[e], r)) for e in range(2)], ["hs%d" % r])
+            iota(T.ww[:], [[0, 384]], -512, 0, ["ww"], True)
+            spread(0, "s")
+            if first:
+                iota(T.jv[:], [[1, C]], 0, 0, ["jv"], True)
+                iota(mk("mi4"), [[0, 72], [1, 4]], 0, 0, ["mi4"], True)
+                iota(T.li[:, 26:38], [[1, 6], [0, 2]], 0, 0, ["li.d"])
+                iota(T.li[:, 50:54], [[32, 4]], 0, 0, ["li.e"])
+                iota(T.li[:, 54:66], [[192, 2], [32, 3], [96, 2]], 0, 0, ["li.f"])
+                iota(T.idn[:], [[16, 2], [32, 3], [1, 16]], 0, 0, ["idn"], True)
+                iota(T.ja[:], [[16, 6]], 0, 0, ["ja"], True)
+
+        done = []
+
+        def column_sums(t):
+            quant(t)
+            if first and not done:
+                qz(T.qob[:], T.sob[:], T.obt[:], ["obt"], ["qob"])
+            done.append(t)
+            sums(t, len(done) == 1, len(done) == len(TW))
+
+        steps = {"h": hold1, "H": hold2, "D": diag, "e": tell, "p": number(p1), "P": number(p2), "b": number(bits), "a": number(asum),
+                 "s": number(rsum), "d": inside, "q": number(column_sums), "j": join,
+                 "x": lambda k: scan(T.ext[:], mk("mi"), bank(CS, 0, C), 0.0, Op.add, Op.min, ["mi", "P:%d" % CS], ["ext"])}
+        for w in ORDER.split():
+            if w[0] in steps:
+                steps[w[0]](w[1:])
+            elif not first:
+                renew[w[0]](w[1:])
+            if first and w in gaps:
+                gaps[w]()
         if first:
-            qz(T.qb4[:, 0:C], T.sb4[:, 0:C], T.bt4[:, 0:4 * C], ["bt4.z"] + ["bt4.%d" % k for k in range(4)], ["qb4"])
-            iota(T.jv[:], [[1, C]], 0, 0, ["jv"], True)
-            iota(T.li[:, 26:38], [[1, 6], [0, 2]], 0, 0, ["li.d"])
-            iota(T.li[:, 50:56], [[32, 6]], 0, 0, ["li.e"])
-            iota(T.li[:, 56:68], [[96, 2], [192, 2], [32, 3]], 0, 0, ["li.f"])
-            iota(T.ja[:], [[48, 2], [96, 2], [16, 3]], 0, 0, ["ja"], True)
-            iota(T.idn[:], [[48, 2], [96, 2], [1, 48]], 0, 0, ["idn"], True)
-        diag("b")
-        for c in low[1:-2] + list(range(10, VTOP + 1)):
-            bits(c)
-        quant(2)
-        scan(T.rsd[:], T.kz[:], T.bt0[:, 0:4 * C:4], 512.0, Op.min, Op.add, ["kz", "bt0.a", "bt0.b"], ["rsd"])
-        for c in low + [10]:
-            asum(c)
-        sums(4, True, False)
-        sums(2, False, False)
-        quant(1)
-        sums(1, False, False)
-        quant(0)
-        sums(0, False, False)
-        if first:
-            act(T.mi[:], T.eqm[:], AF.Identity, ["eqm"], ["mi"], scale=1049600.0, bias=-1024.0)
             act(T.pf[:, 5:6], T.pf[:, 0:1], AF.Identity, ["pf"], ["pf.q2"], scale=-1025.0, bias=15503.0)
-            act(T.pf[:, 4:5], T.pf[:, 0:1], AF.Identity, ["pf"], ["pf.q"], scale=-1024.0, bias=15360.0)
-            for t in range(4):
-                xplane(t)
+            act(mk("m4"), mk("mi4"), AF.Abs, ["mi4", "pf"], ["m4"], scale=-1.0, bias=T.pf[:, 2:3])
+            act(T.pf[:, 8:9], T.pf[:, 3:4], AF.Identity, ["pf"], ["pf.8"], scale=0.25, bias=3072.0)
+            act(T.pf[:, 7:8], T.pf[:, 3:4], AF.Identity, ["pf"], ["pf.ql"], scale=0.25, bias=191.0)
+            act(mk("eq4"), mk("m4"), AF.Relu, ["m4"], ["eq4"], scale=-1.0, bias=1.0)
+            act(T.pf[:, 6:7], T.pf[:, 2:3], AF.Identity, ["pf", "pf.8"], ["pf.q4"], scale=-1024.0, bias=T.pf[:, 8:9])
             fill(T.at[:, 4 * L:], 128, 0.0, ["at.z"])
         spread(1, "s" if first else "a")
-        quant(3)
-        sums(3, False, True)
-        for c in range(11, VTOP + 1):
-            rsum(c)
-        scan(T.ext[:], T.mi[:], bank(CS, 0, C), 0.0, Op.add, Op.min, ["mi", "P:%d" % CS], ["ext"])
-        tt(T.rs2[:], T.rs[:, RP - 1:18 * RP:RP], T.rsd[:, 15:C:16], Op.add, ["rs.%d" % c for c in range(18)] + ["rsd"], ["rs2"])
         if first:
-            cp(T.lst[:, 26:33], T.li[:, 26:33], ["li.d"], ["lst.c"])
-        tt(T.rkf[:], T.ext[:, 15:C:16], T.rs2[:], Op.subtract, ["ext", "rs2"], ["rkf"])
+            cp(T.lst[:, 26:38], T.li[:, 26:38], ["li.d"], ["lst.d"])
+        tt(T.rkf[:], T.ext[:, 15:C:16], T.rb[:, RP - 1:18 * RP:RP], Op.subtract, ["ext"] + ["rb.%d" % c for c in range(18)], ["rkf"])
         if first:
-            cp(T.lst[:, 40:45], T.li[:, 33:38], ["li.d"], ["lst.d"])
-            act(T.ngn[:], T.idn[:], AF.Identity, ["idn"], ["ngn"], scale=-1.0, bias=-64.0)
+            act(mk("mi4"), mk("eq4"), AF.Identity, ["eq4"], ["mi4"], scale=1049600.0, bias=-1024.0)
+            act(T.ngn[:], T.jv[:, 0:192], AF.Identity, ["jv"], ["ngn"], scale=-1.0, bias=-64.0)
             fill(T.pw[:, 0:16], 16, 1.0 / 16, ["pw.a"])
-            act(T.pw[:, 16:32], T.eqm[:, 0:16], AF.Copy, ["eqm"], ["pw.b"], scale=-1.0)
+            act(T.pw[:, 16:32], mk("eqm", 0, 16), AF.Copy, ["eqm"], ["pw.b"], scale=-1.0)
+            act(T.pw[:, 48:52], mk("eq4", 0, 4), AF.Copy, ["eq4"], ["pw.c"], scale=-1.0)
             act(T.idn[:], T.idn[:], AF.Copy, ["idn"], ["idn"], scale=1.0 / 128)
+            iota(T.st[:, 1:2 * C:2], [[0, C]], 512, 0, ["st.z"], True)
+            iota(mk("mb8", 1, 2 * C, 2), [[0, C]], -512, 0, ["mb8"], True)
             for h in range(2):
                 op("g", lambda: g.affine_select(T.et[:, EW * h:EW * h + EW], T.one[:], [[1, EW]], Op.is_equal, 0.0, -2 - h, -4), ["one"], ["et.%d" % h])
 
@@ -443,19 +505,19 @@ def rank_program(g, core, T, topo):
 
         ts(T.rko[:], T.rkf[:], T.pf[:, 5:6], None, Op.add, None, ["rkf", "pf.q2"], ["rko"])
         if first:
-            ts(T.lst[:, 50:68], T.li[:, 50:68], T.pf[:, 1:2], None, Op.add, None, ["li.e", "li.f", "pf"], ["lst.e"])
+            ts(T.lst[:, 50:66], T.li[:, 50:66], T.pf[:, 1:2], None, Op.add, None, ["li.e", "li.f", "pf"], ["lst.e"])
         cp(T.cm[:, 96:384].indirect(T.rko[:]), T.jv[:], ["rko", "jv"], ["cm"])
         theirs(0)
-        scan(T.ex2[:, 0:L], T.mi[:, 0:L], T.cm[:, 96:192], 0.0, Op.add, Op.min, ["mi", "cm"], ["ex2.a"])
+        scan(T.ex2[:, 0:L], mk("mi4", 0, L), T.cm[:, 96:192], 0.0, Op.add, Op.min, ["mi4", "cm"], ["ex2.a"])
         theirs(1)
-        ts(T.oro[:, 0:6], T.ex2[:, 15:L:16], T.pf[:, 4:5], None, Op.add, None, ["ex2.a", "pf.q"], ["oro.a"])
+        ts(T.oro[:, 0:24], T.ex2[:, 3:L:4], T.pf[:, 6:7], 4.0, Op.add, Op.mult, ["ex2.a", "pf.q4"], ["oro.a"])
         if first:
             ts(T.ja[:], T.ja[:], T.pf[:, 0:1], 1.0 / 128, Op.add, Op.mult, ["ja", "pf"], ["ja"])
-        for t in range(4):
-            scale("vvaa"[t], T.at[:, t:4 * L:4], T.xp[:, C * t:C * t + C].indirect(T.oro[:, 0:6]), 2.0 ** -5, xps(t) + ["oro.a"], ["at.%d" % t])
+        for k, e in enumerate("va"):
+            move(e, T.at[:, 192 * k:192 * k + 192], xs[:].indirect(T.oro[:, 12 * k:12 * k + 12]), xnames + ["oro.a"], ["at.%d" % k])
         if first:
             scan(T.pw[:, 32:48], T.pw[:, 0:16], T.pw[:, 16:32], 0.0, Op.mult, Op.min, ["pw.a", "pw.b"], ["pw"])
-        qz(qa, sa, T.at[:], ["at.z", "at.0", "at.1", "at.2", "at.3"], ["qa%d" % r])
+        qz(qa, sa, T.at[:], ["at.z", "at.0", "at.1"], ["qa%d" % r])
         hands = helpers(core, T, topo)
         send([(c, T.qa[:, 128 * r:128 * r + L].bitcast(dt.uint8), T.qh[:, L * r:L * r + L].bitcast(dt.uint8), "harr%d" % r) for c in hands], ["qa%d" % r])
         send([(c, T.sa[:, 128 * r:128 * r + L], T.sh[:, L * r:L * r + L], "harr%d" % r) for c in hands], ["qa%d" % r])
@@ -465,246 +527,204 @@ def rank_program(g, core, T, topo):
             mx(bank(4 + e, 0, 128), T.qu2[:, o:o + 128], T.su2[:, o:o + 128], qa, sa, True, True,
                ["qu2.%d" % e, "su2.%d" % e, "qa%d" % r], ["P:%d" % (4 + e)])
         if first:
-            fill(T.kb[:, 384:384 + 6 * 98:98], 6, -96.0, ["kb.y"])
-            fill(T.kb[:, 384 + 97:384 + 6 * 98:98], 6, 0.0, ["kb.z"])
-            fill(T.pb[:, 0:1], 1, -288.0, ["pb.z"])
-            fill(T.pb[:, C - SP + 1:C - SP + 2], 1, 0.0, ["pb.y"])
-        scan(T.ex2[:, L:C], T.mi[:, L:C], T.cm[:, 192:384], 0.0, Op.add, Op.min, ["mi", "cm"], ["ex2.b"])
+            act(mk("mb8", 0, 2 * C, 2), mk("eq4"), AF.Identity, ["eq4"], ["mb8"], scale=2.0 * BIG, bias=-BIG)
+            fill(T.kt[:, 0:1], 1, -96.0, ["kt.z"])
+            fill(T.kt[:, 97:98], 1, 0.0, ["kt.y"])
+        scan(T.ex2[:, L:C], mk("mi4", L, C), T.cm[:, 192:384], 0.0, Op.add, Op.min, ["mi4", "cm"], ["ex2.b"])
+        ts(T.oro[:, 24:72], T.ex2[:, L + 3:C:4], T.pf[:, 6:7], 4.0, Op.add, Op.mult, ["ex2.b", "pf.q4"], ["oro.b"])
         for e in range(2):
-            tt(T.ma[:, L * e:L * e + L], bank(4 + e, 0, L), T.mb[:, 0:L], Op.min, ["P:%d" % (4 + e), "mb"], ["ma.%d" % e])
+            tt(T.ma[:, L * e:L * e + L], bank(4 + e, 0, L), mk("mb", 0, L), Op.min, ["P:%d" % (4 + e), "mb"], ["ma.%d" % e])
         for e in range(2):
-            scan(T.ha[:, L * e:L * e + L], T.kk[:, 0:L], T.ma[:, L * e:L * e + L], 0.0, Op.min, Op.max, ["kk", "ma.%d" % e], ["ha.%d" % e])
+            scan(T.ha[:, L * e:L * e + L], mk("kk", 0, L), T.ma[:, L * e:L * e + L], 0.0, Op.min, Op.max, ["kk", "ma.%d" % e], ["ha.%d" % e])
         END = 6 * 143
 
-        def a1(c, n):
-            act(T.sgp[:, C * c:C * c + n], T.rep[:, 0:n], AF.Sign, ["rep.0", "ha.0"], ["sgp.%d" % c],
+        def a1(c):
+            act(T.sgp[:, C * c:C * c + C], T.rep[:, 0:C], AF.Sign, ["rep.0", "ha.0"], ["sgp.%d" % c],
                 bias=T.ha[:, 16 * c + 15:16 * c + 16], scale=-1.0)
 
         def a2(c):
             act(T.jkp[:, C * c:C * c + C], T.sgp[:, C * c:C * c + C], AF.Sign, ["sgp.%d" % c], ["y0.%d" % c], scale=-1.0, bias=-0.5,
                 accum_out=T.y0[:, END + c:END + c + 1])
 
-        def vb(e, c):
-            k = VC.index((e, c))
-            o, a = (1, SP) if k == 0 else (C * k, 0)
-            ts(T.pb[:, o:o + C - a], T.rep[:, C * e + a:C * e + C], T.ha[:, L * e + 16 * c + 15:L * e + 16 * c + 16], 2.0, Op.is_gt, Op.mult,
+        def vb(k):
+            e, c = k // 6, k % 6
+            ts(T.pb[:, C * k:C * k + C], T.rep[:, C * e:C * e + C], T.ha[:, L * e + 16 * c + 15:L * e + 16 * c + 16], 2.0, Op.is_gt, Op.mult,
                ["rep.%d" % e, "ha.%d" % e], ["pb.%d" % k])
 
-        def vs(e, c):
-            k = VC.index((e, c))
-            o = C * k
-            if k == 0:
-                w = (C - SP) // 2 + 1
-                scan(T.y0[:, END + c - 6 * (w - 1):END + c + 1:6], T.pb[:, 0:w], T.pb[:, w:2 * w], T.yh[:, 0:1], Op.add, Op.add,
-                     ["pb.0", "pb.z", "pb.y", "yh"], ["y0.%d" % c])
-            else:
-                scan((T.y0, T.y1)[e][:, c:6 * 144:6], T.pb[:, o:o + 144], T.pb[:, o + 144:o + C], -288.0, Op.add, Op.add, ["pb.%d" % k], ["y%d.%d" % (e, c)])
+        def vs(k):
+            e, c, o = k // 6, k % 6, C * k
+            scan((T.y0, T.y1)[e][:, c:6 * 144:6], T.pb[:, o:o + 144], T.pb[:, o + 144:o + C], -288.0, Op.add, Op.add, ["pb.%d" % k], ["y%d.%d" % (e, c)])
+
+        o = 16 * r
+        fm = [T.fm[:, 2 * o + 16 * h:2 * o + 16 * h + 3] for h in range(2)]
+        fl = [T.fl[:, 2 * o + 16 * h:2 * o + 16 * h + 6] for h in range(2)]
+        fmn, fln = ["fm%d%d" % (r, h) for h in range(2)], ["fl%d%d" % (r, h) for h in range(2)]
 
         def final(h):
-            o, n = 16 * (2 * r + h), "%d%d" % (r, h)
-            fm = T.fm[:, o:o + 3]
-            tt(fm, T.y0[:, END + 3 * h:END + 3 * h + 3], T.y1[:, END + 3 * h:END + 3 * h + 3], Op.max,
-               ["y%d.%d" % (e, c) for e in range(2) for c in range(3 * h, 3 * h + 3)], ["fm" + n])
-            send([(T.cores[d], fm, T.fl[:, o + 3 * slot_at(d):o + 3 * slot_at(d) + 3], "farr" + n) for d in rcv], ["fm" + n])
-            arrives("farr" + n, share(snd[0], 2) + share(snd[1], 2), ["fl" + n])
-
-        a1(0, C)
-        a1(1, C)
-        a2(0)
-        a1(5, SP)
-        a2(1)
-        a1(3, C)
-        act(T.jkp[:, C * 5:C * 5 + SP], T.sgp[:, C * 5:C * 5 + SP], AF.Relu, ["sgp.5"], ["yh"], scale=-2.0, accum_out=T.yh[:, 0:1])
-        a1(4, C)
-        a2(3)
-        a2(4)
-        seq = [(0, 2), (1, 0), (1, 1), (1, 2)]
-        vb(*seq[0])
-        for x, y in zip(seq[1:] + [(0, 5)], seq):
-            vb(*x)
-            vs(*y)
-        ts(T.oro[:, 6:18], T.ex2[:, L + 15:C:16], T.pf[:, 4:5], None, Op.add, None, ["ex2.b", "pf.q"], ["oro.b"])
-        final(0)
-        vb(1, 3)
-        for c in (4, 5):
-            vb(1, c)
-            vs(1, c - 1)
-        vs(0, 5)
-        vs(1, 5)
-        final(1)
+            tt(fm[h], T.y0[:, END + h:END + 6:2], T.y1[:, END + h:END + 6:2], Op.max, ["y%d.%d" % (e, c) for e in range(2) for c in range(h, 6, 2)], [fmn[h]])
+            at = [2 * o + 16 * h + 3 * slot_at(d) for d in rcv]
+            send([(T.cores[d], fm[h], T.fl[:, a:a + 3], "farr%d%d" % (r, h)) for d, a in zip(rcv, at)], [fmn[h]])
+            arrives("farr%d%d" % (r, h), share(snd[0], 2) + share(snd[1], 2), [fln[h]])
 
         def unpacker(b):
             o = EW * (b % 2) + 2 - 2 * (b // 2)
             if first:
                 qz(T.qe[:, 128 * b:128 * b + 128], T.se[:, 128 * b:128 * b + 128], T.et[:, o:o + 512], ["et.%d" % (b % 2)], ["qe.%d" % b])
 
-        def stayers(e, t):
-            scale(e, T.vp[:, 384 * t + 192:384 * t + 384], T.xp[:, C * t:C * t + C].indirect(T.oro[:, 6:18]), 2.0 ** -6, xps(t) + ["oro.b"], ["vp.s%d" % t])
+        def count_a(k, row, n, col, names, out, name):
+            act(T.jkq[:, L * k:L * k + L], row, AF.Sign, names, [name], bias=col, scale=-1.0, accum_out=out)
 
-        for t in range(2):
-            stayers("a", t)
-        if last:
-            qz(T.qv[:], T.sv[:], T.vt[:], ["vt"], ["qv"])
+        def count_v(k, row, col, names):
+            ts(T.kb[:, L * k:L * k + L] if k else T.kt[:, 1:97], row, col, 2.0, Op.is_lt, Op.mult, names, ["kb.%d" % k])
 
-        def keys(h, between):
-            n, o = "%d%d" % (r, h), 16 * (2 * r + h)
-            fl, w, c = T.fl[:, o:o + 6], 192 * h, slice(6 * h, 6 * h + 6)
-            act(T.ee[:, w + 112:w + 192], fl.indirect(T.lst[:, 40:45]), AF.Relu, ["fl" + n, "lst.d"], ["ee.1%d" % h], bias=96.0)
-            act(T.f2[:, c], fl, AF.Relu, ["fl" + n], ["f2.%d" % h], bias=96.0)
-            act(T.b2[:, c], T.f2[:, c], AF.Relu, ["f2.%d" % h], ["b2.%d" % h], scale=-1.0, bias=382.0)
-            ts(T.ee[:, w:w + 112], fl.indirect(T.lst[:, 26:33]), 96.0, 0.0, Op.add, Op.max, ["fl" + n, "lst.c"], ["ee.0%d" % h])
-            between()
-            op("v", lambda: V.transpose(T.r2[:, w:w + 192], T.ee[:, w:w + 192]), ["ee.0%d" % h, "ee.1%d" % h], ["r2.%d" % h])
-            tt(T.ka[:, c], T.f2[:, c], T.ja[:, c], Op.add, ["f2.%d" % h, "ja"], ["ka.%d" % h])
-            tt(T.kys[:, L * h:L * h + L], T.r2[:, w:w + 192].indirect(T.lst[:, 50:56]), T.idn[:, L * h:L * h + L], Op.add,
-               ["r2.%d" % h, "lst.e", "idn"], ["kys.%d" % h])
+        def sum_v(k, out, init, name, reads=[]):
+            scan(out, T.kb[:, L * k:L * k + 48], T.kb[:, L * k + 48:L * k + L], init, Op.add, Op.add, ["kb.%d" % k] + reads, [name])
 
-        def ka(c, a, b, out, name):
-            act(T.jkq[:, 192 * c + a:192 * c + b], T.kys[:, a:b], AF.Sign, ["kys.%d" % (a // L), "kys.%d" % ((b - 1) // L), "ka.%d" % (c // 6)], [name],
-                bias=T.ka[:, c:c + 1], scale=-1.0, accum_out=out)
-
-        def kb(c, a, o):
-            ts(T.kb[:, o:o + L], T.kys[:, a:a + L], T.ka[:, c:c + 1], 2.0, Op.is_lt, Op.mult, ["kys.%d" % (a // L), "ka.%d" % (c // 6)], ["kb.%d" % o])
-
-        def ks(c, o, m, out, init, reads, name):
-            scan(out[:, 96 * c + 96 - m:96 * c + 96], T.kb[:, o:o + m], T.kb[:, o + m:o + 2 * m], init, Op.add, Op.add, reads, [name])
-
-        def old(c):
-            return 384 + 98 * c
-
-        unpacker(0)
-        ms(T.ww[:], -512.0, ["ww"])
-        keys(0, lambda: None)
-        for c in range(2, 6):
-            ka(c, 0, L, T.rh[:, 96 * c + 95:96 * c + 96], "rh.%d" % c)
-        kb(0, 0, 0)
-        kb(1, 0, L)
-        ks(0, 0, 48, T.rh, -95.0, ["kb.0"], "rh.0")
-        ks(1, L, 48, T.rh, -95.0, ["kb.96"], "rh.1")
-        keys(1, lambda: tt(T.ini[:, 0:6], T.rh[:, 95:6 * 96:96], T.b2[:, 0:6], Op.subtract, ["rh.%d" % c for c in range(6)] + ["b2.0"], ["ini.0"]))
-        act(T.ini[:, 6:7], T.b2[:, 6:7], AF.Identity, ["b2.1"], ["ini.1"], scale=-1.0, bias=-191.0)
-        for c in range(7, 12):
-            ka(c, 0, 2 * L, T.rk[:, c:c + 1], "rk.%d" % c)
-        kb(6, 0, 192)
-        kb(6, L, 288)
-        kb(0, L, old(0) + 1)
-        ks(6, 192, L, T.plf, T.ini[:, 6:7], ["kb.192", "kb.288", "ini.1"], "plf.6")
-        for c in range(1, 7):
-            if c < 6:
-                kb(c, L, old(c) + 1)
+        def repeat(e, out, window, a, b, reads, writes):
+            in_ = window.indirect(T.lst[:, 26 + a:26 + b])
+            if e == "v":
+                ts(out, in_, 96.0, 0.0, Op.add, Op.max, reads + ["lst.d"], writes)
             else:
-                tt(T.plf[:, 96 * 7 + 95:96 * 12:96], T.rk[:, 7:12], T.b2[:, 7:12], Op.subtract, ["rk.%d" % c for c in range(7, 12)] + ["b2.1"], ["plf.7"])
-            ks(c - 1, old(c - 1), 49, T.plf, T.ini[:, c - 1:c], ["kb.%d" % (old(c - 1) + 1), "kb.y", "kb.z", "ini.0"], "plf.%d" % (c - 1))
-        unpacker(1)
-        ts(T.plo[:], T.plf[:, 95:12 * 96:96], 575.0, 0.5, Op.add, Op.mult, ["plf.%d" % c for c in range(8)], ["plo"])
-        if first:
-            act(T.m16[:], T.eqm[:], AF.Identity, ["eqm"], ["m16"], scale=-16.0, bias=16.0)
-        unpacker(2)
+                act(out, in_, AF.Relu, reads + ["lst.d"], writes, bias=96.0)
+
+        f2, ka, po = T.so[:, 0:6], T.so[:, 6:12], C * r
+        ownv = len([w for w in QUEUE.split() if w[0] == "w"])
+
+        def own_repeat(k):
+            e, h, a, b = k[0], int(k[1]), int(k[2]), int(k[3])
+            repeat(e, T.eo[:, L * h + 16 * a:L * h + 16 * b], fm[h], a, b, [fmn[h]], ["eo.%d%d" % (h, j) for j in range(a, b, 2)])
+
+        def own_small(k):
+            k, h = k[0], int(k[1:] or 0)
+            if k == "f":
+                act(T.so[:, h:6:2], fm[h], AF.Relu, [fmn[h]], ["f2.%d" % h], bias=96.0)
+            elif k == "k":
+                tt(ka, f2, T.ja[:], Op.add, ["f2.0", "f2.1", "ja"], ["ka"])
+            elif k == "a":
+                ts(T.so[:, 12:18], f2, 382.0, -191.0, Op.min, Op.add, ["f2.0", "f2.1"], ["b3"])
+            elif k == "v":
+                ts(T.so[:, 18:24], f2, 382.0, -286.0, Op.min, Op.add, ["f2.0", "f2.1"], ["b4"])
+            elif k == "t":
+                turn(T.ro[:, L * h:L * h + L], T.eo[:, L * h:L * h + L], ["eo.%d%d" % (h, j) for j in (0, 2, 4)], ["ro.%d" % h])
+            elif k == "y":
+                tt(T.kyo[:, 48 * h:48 * h + 48], T.ro[:, L * h:L * h + L].indirect(T.lst[:, 50:53]), T.idn[:, 48 * h:48 * h + 48], Op.add,
+                   ["ro.%d" % h, "lst.e", "idn"], ["kyo.%d" % h])
+            else:
+                tt(T.pm[:, po + C - 6 + ownv:po + C], T.rh[:, ownv:6], T.so[:, 12 + ownv:18], Op.add, ["rh.%d" % c for c in range(ownv, 6)] + ["b3"], ["pm%d.a" % r])
+
+        def own_count(c):
+            if c < ownv:
+                count_v(12 + c, T.kyo[:], T.so[:, 6 + c:7 + c], ["kyo.0", "kyo.1", "ka"])
+            else:
+                count_a(12 + c, T.kyo[:], L, T.so[:, 6 + c:7 + c], ["kyo.0", "kyo.1", "ka"], T.rh[:, c:c + 1], "rh.%d" % c)
+
+        def own_sum(c):
+            sum_v(12 + c, T.pm[:, po + c:po + C:6], T.so[:, 18 + c:19 + c], "pm%d.%d" % (r, c), ["b4"])
+
+        def own_send(_):
+            send([(T.cores[d], T.pm[:, po + C - 6:po + C], T.pl[:, o + 6 * slot_at(d):o + 6 * slot_at(d) + 6], "parr%d" % r) for d in rcv],
+                 ["pm%d.a" % r] + ["pm%d.%d" % (r, c) for c in range(ownv)])
+            arrives("parr%d" % r, share(snd[0], 2) + share(snd[1], 2), ["pl%d" % r])
+
+        def beside(b):
+            unpacker(b)
+            if first and b == 3:
+                act(mk("m4"), mk("eq4"), AF.Identity, ["eq4"], ["m4"], scale=-16.0, bias=16.0)
+                scan(T.pw[:, 52:56], T.pw[:, 0:4], T.pw[:, 48:52], 0.0, Op.mult, Op.min, ["pw.a", "pw.c"], ["pw4"])
+            if last and b == 0:
+                qz(T.qv[:], T.sv[:], T.vt[:], ["vt"], ["qv"])
+
+        def pick(k):
+            e, q = k[0], int(k[1])
+            out, in_, c = T.xr[:, 48 * q:48 * q + 48], T.r2[:, L * q:L * q + L].indirect(T.lst[:, 50:53]), 2.0 * (q // 2) - 193.0
+            if e == "v":
+                ts(out, in_, c, None, Op.add, None, ["r2.%d" % q, "lst.e"], ["xr.%d" % q])
+            else:
+                act(out, in_, AF.Identity, ["r2.%d" % q, "lst.e"], ["xr.%d" % q], bias=c)
+
+        def came(k):
+            e, q = k[0], int(k[1])
+            repeat(e, T.ee[:, L * q:L * q + L], fl[q % 2], 6 * (q // 2), 6 * (q // 2) + 6, [fln[q % 2]], ["ee.%d" % q])
+
+        def cross(k):
+            c = int(k[1:])
+            h = 1 - c // 6
+            row, names = T.xr[:, L * h:L * h + L], ["xr.%d" % (2 * h), "xr.%d" % (2 * h + 1), "sc2.%d" % (c % 2)]
+            if k[0] == "v":
+                count_v(c, row, T.sc2[:, c:c + 1], names)
+            else:
+                count_a(c, row, L, T.sc2[:, c:c + 1], names, T.rk[:, 48 * c + 47:48 * c + 48], "rk.%d" % c)
+
+        def cross_sum(c):
+            if c:
+                sum_v(c, T.rk[:, 48 * c:48 * c + 48], -96.0, "rk.%d" % c)
+            else:
+                scan(T.plf[:, 0:49], T.kt[:, 0:49], T.kt[:, 49:98], T.pl[:, o:o + 1], Op.add, Op.add, ["kb.0", "kt.z", "kt.y", "pl%d" % r], ["plf.0"])
+
+        steps = {"g": number(a1), "G": number(a2), "b": number(vb), "B": number(vs), "F": number(final), "O": own_repeat,
+                 "n": own_small, "r": number(own_count), "w": number(own_sum), "P": own_send, "U": number(beside), "E": came,
+                 "s": number(lambda h: ts(T.sc2[:, h:12:2], fl[h], -96.0, -192.0, Op.add, Op.max, [fln[h]], ["sc2.%d" % h])),
+                 "t": number(lambda q: turn(T.r2[:, L * q:L * q + L], T.ee[:, L * q:L * q + L], ["ee.%d" % q], ["r2.%d" % q])),
+                 "x": pick, "c": cross, "d": number(cross_sum),
+                 "J": lambda k: tt(T.plf[:, 97:12 * 49:49], T.rk[:, 95:12 * 48:48], T.pl[:, o + 1:o + 12], Op.add, ["rk.%d" % c for c in range(1, 12)] + ["pl%d" % r], ["plf"])}
+        for w in QUEUE.split():
+            steps[w[0]](w[1:])
+        ts(T.plo[:], T.plf[:, 48:12 * 49:49], 384.0, 0.5, Op.add, Op.mult, ["plf", "plf.0"], ["plo"])
         cp(T.ww[:].indirect(T.plo[:]), T.ngn[:], ["plo", "ngn"], ["ww"])
-        unpacker(3)
-        for t in (2, 3):
-            stayers("a", t)
+        scale("a", T.vp[:, 768:1536], xs[:].indirect(T.oro[:, 24:72]), 0.5, xnames + ["oro.b"], ["vp.s"])
         for b in range(4):
             mx(bank(b, 0, 192), T.qe[:, 128 * b:128 * b + 128], T.se[:, 128 * b:128 * b + 128], ql, sl, True, True,
                ["qe.%d" % b, "ql%d" % r], ["P:%d" % b])
+        act(T.gp[:, 0:4], T.vp[:, 768:772], AF.Copy, ["vp.s"], ["gp.z"])
         for b in range(4):
-            scale("a", T.vp[:, 384 * b:384 * b + 192], bank(b, 0, 192), 0.5, ["P:%d" % b], ["vp.d%d" % b])
-        act(T.gp[:, 0:4 * GW:GW], T.vp[:, 192:4 * 384:384], AF.Copy, ["vp.s%d" % t for t in range(4)], ["gp.z"])
+            scale("a", T.vp[:, b:768:4], bank(b, 0, 192), 0.5, ["P:%d" % b], ["vp.d%d" % b])
+
         ts(T.flg[:], T.ww[:, 0:C], -300.0, None, Op.is_lt, None, ["ww"], ["flg"])
-        scan(T.exw[:], T.m16[:], T.ww[:, 0:C], 0.0, Op.mult, Op.min, ["m16", "ww"], ["exw"])
-        scan(T.st[:], T.flg[:], T.flg[:], 0.0, Op.add, Op.max, ["flg"], ["st"])
-        ts(T.wa[:], T.exw[:, 15:C:16], T.pw[:, 47:48], -255.0, Op.mult, Op.add, ["exw", "pw"], ["wa"])
-        scan(T.exs[:], T.mb[:], T.st[:], 0.0, Op.max, Op.min, ["mb", "st"], ["exs"])
-        tt(T.lf[:], T.wa[:], T.exs[:, 15:C:16], Op.min, ["wa", "exs"], ["lf"])
+        scan(T.exw[:, 0:C], mk("m4"), T.ww[:, 0:C], 0.0, Op.mult, Op.min, ["m4", "ww"], ["exw.0"])
+        scan(T.st[:, 0:2 * C:2], T.flg[:], T.flg[:], 0.0, Op.add, Op.max, ["flg"], ["st"])
+        ts(T.st[:, 7:2 * C:8], T.exw[:, 3:C:4], T.pw[:, 55:56], -255.0, Op.mult, Op.add, ["exw.0", "pw4", "st.z"], ["st.w"])
         if last:
-            act(T.lsb[:, C:480], T.r2[:].indirect(T.lst[:, 56:68]), AF.Copy, ["r2.0", "r2.1", "lst.e"], ["lsb.b"], scale=0.5)
-            act(T.cm[:, 0:192], T.jv[:, 0:192], AF.Identity, ["jv"], ["cm"], bias=288.0)
-        ts(T.lo[:], T.lf[:], 191.0, None, Op.add, None, ["lf"], ["lo"])
+            scan(T.exw[:, C:2 * C], mk("m16"), T.ww[:, 0:C], 0.0, Op.mult, Op.min, ["m16", "ww"], ["exw.1"])
+        parts = ((0, FIRST), (FIRST, C))
+        for a, b in parts:
+            scan(T.exs[:, 2 * a:2 * b], mk("mb8", 2 * a, 2 * b), T.st[:, 2 * a:2 * b], 0.0, Op.max, Op.min, ["mb8", "st", "st.w", "st.z"], ["exs.%d" % a])
+        for a, b in parts:
+            ts(T.lo[:, a // 4:b // 4], T.exs[:, 2 * a + 7:2 * b:8], T.pf[:, 7:8], 4.0, Op.add, Op.mult, ["exs.%d" % a, "pf.ql"], cols("lo", a, b))
+            if last and a == 0:
+                scan(T.exs[:, 2 * C:3 * C], mk("mb"), T.st[:, 0:2 * C:2], 0.0, Op.max, Op.min, ["mb", "st"], ["exs.1"])
+        if r == R - 2:
+            act(mk("m16"), mk("eqm"), AF.Identity, ["eqm"], ["m16"], scale=-16.0, bias=16.0)
 
-        def gather(e, t, h):
-            a, b = run[h]
-            move(e, T.gp[:, GW * t + 1 + a:GW * t + 1 + b], T.vp[:, 384 * t:384 * t + 384].indirect(T.lo[:, a // 16:b // 16]),
-                 ["vp.s%d" % t, "vp.d%d" % t, "lo"], ["gp.%s%d" % (h, t)])
+    def listed(k):
+        if k == "w":
+            ts(T.wa[:], T.exw[:, C + 15:2 * C:16], T.pw[:, 47:48], -255.0, Op.mult, Op.add, ["exw.1", "pw"], ["wa"])
+        elif k == "f":
+            tt(T.lf[:], T.wa[:], T.exs[:, 2 * C + 15:3 * C:16], Op.min, ["wa", "exs.1"], ["lf"])
+        else:
+            ts(T.lo[:, 72:90], T.lf[:], 191.0, None, Op.add, None, ["lf"], ["lo.s"])
 
-        def blend(t, h):
-            a, b = run[h]
-            o = GW * t
-            tt(T.zt[:, 4 * a + t:4 * b:4], T.gp[:, o + 1 + a:o + 1 + b], T.gp[:, o + a:o + b], Op.add,
-               ["gp.a%d" % t, "gp.z" if h == "a" else "gp.b%d" % t], ["zt.%s%d" % (h, t)])
-
-        def pb_(h, t):
-            return t if h == "a" else 4 + t
-
-        def layer(h):
-            a, b = run[h]
-            qz(T.qz[:, a:b], T.sz[:, a:b], T.zt[:, 4 * a:4 * b], ["zt.%s%d" % (h, t) for t in range(4)], ["qz." + h])
-            for t in range(4):
-                mx(bank(pb_(h, t), 0, b - a), T.qw[:, 128 * t:128 * t + 128], T.sw[:, 128 * t:128 * t + 128], T.qz[:, a:b], T.sz[:, a:b], True, True,
-                   ["qw", "qz." + h], ["P:%d" % pb_(h, t)])
-
-        def z32(h):
-            a, b = run[h]
-            for t in range(4):
-                scale("a", T.zp[:, 4 * a + t:4 * b:4], T.zt[:, 4 * a + t:4 * b:4], 32.0, ["zt.%s%d" % (h, t)], ["zp.%s%d" % (h, t)])
-
-        def state(t, h):
-            a, b = run[h]
-            tt(T.xp[:, C * t + a:C * t + b], bank(pb_(h, t), 0, b - a), T.zp[:, 4 * a + t:4 * b:4], Op.add,
-               ["P:%d" % pb_(h, t), "zp.%s%d" % (h, t)], ["xp.%s%d" % (h, t)])
-
-        def back(e, t, h):
-            a, b = run[h]
-            scale(e, T.xn[:, 4 * a + t:4 * b:4], T.xp[:, C * t + a:C * t + b], 2.0 ** -5, ["xp.%s%d" % (h, t)], ["xn.%s%d" % (h, t)])
-
-        def xns(h):
-            return ["xn.%s%d" % (h, t) for t in range(4)]
-
-        for t in (2, 3):
-            gather("a", t, "a")
-        for t in (0, 1):
-            gather("v", t, "a")
-        for t in range(4):
-            gather("a", t, "b")
-        for t in (0, 2, 1, 3):
-            blend(t, "a")
-        blend(0, "b")
-        layer("a")
-        z32("a")
-        for t in (1, 2, 3):
-            blend(t, "b")
-        state(0, "a")
-        layer("b")
-        z32("b")
-        for t in range(1, 4):
-            state(t, "a")
-        for t in range(4):
-            back("aavv"[t], t, "a")
-        state(0, "b")
-        qx_of(T.xn, "a", xns("a"))
-        if last:
+    def closing(h):
+        qx_of(T.xn, h, xns(h))
+        if h == "a":
             mx(bank(0, 0, H), T.qv[:], T.sv[:], T.qx[:, 0:H], T.sx[:, 0:H], True, True, ["qv", "qx.a"], ["P:0"])
             dmas("s", "stp", [(T.oc[:, 0:4 * H], T.qx[:, 0:H].bitcast(dt.uint8))], ["qx.a"], [])
+
+    def lists_out(k):
+        if k == "0":
+            act(T.cm[:, 0:192], T.jv[:, 0:192], AF.Identity, ["jv"], ["cm"], bias=288.0)
+        elif k == "1":
+            act(T.lsb[:, C:480], T.r2[:].indirect(T.lst[:, 54:66]), AF.Copy, ["r2.%d" % q for q in range(4)] + ["lst.e"], ["lsb.b"], scale=0.5)
         else:
-            scores_a()
-        for t in range(1, 4):
-            state(t, "b")
-        for t in range(3):
-            back("a", t, "b")
-        if last:
-            act(T.yb[:, 0:H], bank(0, 0, H), AF.Copy, ["P:0"], ["yb.0"])
-            dmas("a", "stz", [(T.y[:, 0:H], T.yb[:, 0:H])], ["yb.0"], [])
-            act(T.lsb[:, 0:C], T.cm[:].indirect(T.lo[:]), AF.Copy, ["cm", "lo"], ["lsb.a"])
+            act(T.lsb[:, 0:C], T.cm[:].indirect(T.lo[:, 72:90]), AF.Copy, ["cm", "lo.s"], ["lsb.a"])
             dmas("a", "stl", [(T.ls[:], T.lsb[0:128:16, :])], ["lsb.a", "lsb.b"], [])
-            back("v", 3, "b")
-            qx_of(T.xn, "b", xns("b"))
-        else:
-            hold1("a")
-            back("v", 3, "b")
-            hold2("a")
-            rows(AEARLY)
-            qx_of(T.xn, "b", xns("b"))
-            scores_b()
-            diag("a")
+
+    def y_a(_):
+        act(T.yb[:, 0:H], bank(0, 0, H), AF.Copy, ["P:0"], ["yb.0"])
+        dmas("a", "stz", [(T.y[:, 0:H], T.yb[:, 0:H])], ["yb.0"], [])
+
+    renew.update({"X": closing, "l": listed, "o": lists_out, "y": y_a})
+    for w in LAST.split():
+        renew[w[0]](w[1:])
 
     mx(bank(1, 0, C - H), T.qv[:], T.sv[:], T.qx[:, H:C], T.sx[:, H:C], True, True, ["qv", "qx.b"], ["P:1"])
     dmas("s", "sto", [(T.oc[:, 4 * H:], T.qx[:, H:C].bitcast(dt.uint8))] + [(T.osc[4 * k:4 * k + 4, :], T.sx[32 * k:32 * k + 4, :]) for k in range(4)],

from concourse.bass import DstId, RemoteDMATransfer
from concourse.mybir import dt, AluOpType as Op, ActivationFunctionType as AF

C, L, R = 288, 96, 3
H = 160
BIG = 1.0e29
F8, U8, BF, F32, I32, U16 = "float8_e4m3fn_x4", "uint8", "bfloat16", "float32", "int32", "uint16"
EW = 520
TW = [288, 224, 160, 128, 128]
RP = 136
FIRST = 96
QUEUE = ("g0 g2 G0 g1 G2 g3 G1 G3 b4 b6 b8 b10 B4 B6 B8 b5 B10 b7 F0 b9 b11 B5 B7 B9 B11 nf0 Ov006 F1 nt0 Ov104 Oa146 nf1 ny0 nt1 nk na nv ny1 "
         "Ev0 r0 r1 r2 r3 r4 r5 Ea2 t0 w0 w1 w2 s0 nj P Ea3 Ev1 t2 xv0 t3 t1 s1 xa2 xv3 xa1 U0 U1 "
         "ca11 ca10 ca9 ca8 ca7 cv5 cv4 cv3 cv2 cv1 cv0 cv6 d5 d4 d3 d2 d1 d6 d0 U2 J U3")
ORDER = ("Gv0-24 Ga48-96 Gv24-48 Ga96-160 Ga160-224 Ga224-288 B0-24 B24-48 B48-96 B96-160 B160-224 La Za0-160 B224-288 Za160-288 Sa0 Lb Sa1 Sa2 Kaa1 Kaa0 Sa3 Kva2 "
         "Sb0 Kva3 Sb2 Kab2 Xa Sb1 Kab1 Sb3 Kvb0 Kvb3 ha Xb Ha p9 p8 P9 P8 b7 hb b3 Da b4 a7 Hb b1 b5 b2 p12 p11 p10 p13 P12 P10 P13 P11 "
         "e Db b15 b6 d b16 b17 s15 b14 j0-1 q4 q0 q2 q3 q1 a5 a6 a4 s16 s2 s1 s3 s14 s17 j4-14 x")
LAST = ("Gv0-24 Ga48-96 Gv24-48 Ga96-160 Ga160-224 Ga224-288 lw B0-24 B24-48 B48-96 B96-160 lf B160-224 La Za0-160 B224-288 lo Za160-288 o0 Sa0 Lb Sa1 Sa2 Kaa0 Kaa1 "
        "Sa3 Kva2 Sb0 o1 o2 Sb1 Sb2 Kva3 Sb3 Kvb0 Kvb1 Kvb2 Xa Kvb3 y Xb")
MASKS = ["eqm", "mb", "mi", "kk", "kz", "m16", "km", "eq4", "mi4", "m4", "mb8", "(mb8 is twice as long)"]


def _sb(n, d):
    return ("sbuf", [128, n], d)


SCRATCH = {
    "xt": _sb(4 * C, BF), "ut": _sb(512, BF), "vt": _sb(512, BF), "xn": _sb(4 * C, BF),
    "qx": _sb(C, F8), "sx": _sb(C, U8), "qu": _sb(128, F8), "su": _sb(128, U8), "qv": _sb(128, F8), "sv": _sb(128, U8),
    "qw": _sb(512, F8), "sw": _sb(512, U8),
    "qur": _sb(128, F8), "sur": _sb(128, U8), "quc": _sb(32, F8), "suc": _sb(32, U8),
    "qul": _sb(64, F8), "sul": _sb(64, U8), "qu2": _sb(256, F8), "su2": _sb(256, U8),
    "pi": _sb(2, I32), "ti": _sb(8, I32), "pf": _sb(12, F32), "li": _sb(80, I32), "lst": _sb(80, U16),
    "la": _sb(8, U16), "lb": _sb(8, U16), "qh": _sb(L * R, F8), "sh": _sb(128 * R, U8),
    "mk": _sb(C * len(MASKS), BF), "pw": _sb(56, F32),
    "c16": _sb(18, F32), "ja": _sb(6, F32), "jv": _sb(C, F32), "idn": _sb(L, F32), "ngn": _sb(192, BF),
    "obt": _sb(512, BF), "qob": _sb(128, F8), "sob": _sb(128, U8),
    "one": _sb(EW, BF), "et": _sb(2 * EW, BF), "qe": _sb(512, F8), "se": _sb(512, U8),
    "mm": _sb(C, F32), "hh": _sb(C, F32), "sga": _sb(8 * 18 * 17, BF), "jka": _sb(8 * 18 * 17, BF),
    "rs": _sb(18, F32), "rb": _sb(18 * RP, BF), "rsd": _sb(C, BF), "ext": _sb(C, F32),
    "rkf": _sb(18, F32), "rko": _sb(18, U16), "cm": _sb(384, F32), "ex2": _sb(C, F32), "oro": _sb(72, U16),
    "xp": _sb(4 * C, BF), "at": _sb(512, BF), "vp": _sb(4 * 384, BF), "gp": _sb(4 * C + 4, BF),
    "zt": _sb(4 * C, BF), "zp": _sb(4 * C, BF), "qz": _sb(C, F8), "sz": _sb(C, U8),
    "ma": _sb(192, F32), "ha": _sb(192, F32), "rep": _sb(2 * C, F32), "pb": _sb(12 * C, BF), "sgp": _sb(6 * C, BF),
    "jkp": _sb(6 * C, BF), "y0": _sb(6 * 144, F32), "y1": _sb(6 * 144, BF),
    "eo": _sb(192, BF), "ro": _sb(192, BF), "kyo": _sb(L, F32), "so": _sb(24, F32), "kb": _sb(18 * L, BF), "jkq": _sb(18 * L, BF),
    "rh": _sb(6, F32), "ee": _sb(384, BF), "r2": _sb(384, BF), "xr": _sb(192, BF), "sc2": _sb(12, BF),
    "rk": _sb(12 * 48, F32), "plf": _sb(12 * 49, BF), "kt": _sb(98, BF), "plo": _sb(12, U16),
    "ww": _sb(384, BF), "flg": _sb(C, BF), "st": _sb(2 * C, BF), "exw": _sb(2 * C, BF), "exs": _sb(3 * C, BF),
    "wa": _sb(18, F32), "lf": _sb(18, F32), "lo": _sb(90, U16), "lsb": _sb(480, F32), "yb": _sb(C, F32),
    "hs": _sb(20 * R, F32), "qa": _sb(128 * R, F8), "sa": _sb(128 * R, U8), "ql": _sb(192 * R, F8), "sl": _sb(192 * R, U8),
    "fm": _sb(32 * R, BF), "fl": _sb(32 * R, BF), "pm": _sb(C * R, BF), "pl": _sb(16 * R, BF), "sc": ("dram", [2 * R, 128, 18], F32),
    "ps": ("psum", [128, 4096], F32),
}
for _a in range(5):
    _w = C if _a == 4 else TW[_a]
    SCRATCH["bt%d" % _a] = _sb(4 * TW[_a], BF)
    SCRATCH["qb%d" % _a] = _sb(_w, F8)
    SCRATCH["sb%d" % _a] = _sb(_w, U8)

SEMAPHORES = ["cv", "ca", "cp", "cg", "ldx", "ldy", "ldu", "ldw", "sent", "uarr", "sty", "stz", "sto", "stp", "stl"]
for _r in range(R):
    SEMAPHORES += ["%s%d" % (_n, _r) for _n in ("qarr", "harr", "sca", "scb", "rpa", "rpb", "parr")] + ["farr%d%d" % (_r, _h) for _h in range(2)]


def helpers(c, T, topo):
    return [x for x in topo.cores_of(c) if x not in T.cores and topo.die(x) == topo.die(c)][:2]


def helper_program(g, core, rank, e, T, topo):
    N = len(T.cores)
    d = (rank + 1 + e) % N
    rid, pid = topo.addr(T.cores[d], core)
    mask = topo.mask(core, T.cores[d])
    came = len(topo.engines(T.cores[rank], core)) // 2
    for r in range(R):
        a = 192 * r + (0 if rank == min((d - 1) % N, (d - 2) % N) else L)
        g.wait_ge(T.sem["harr%d" % r], 2 * came)
        g.remote_dma(T.ql[:, a:a + L].bitcast(dt.uint8), T.qh[:, L * r:L * r + L].bitcast(dt.uint8), T.sem["qarr%d" % r], T.sem.sent, pid, rid, mask)
        g.remote_dma(T.sl[:, a:a + L], T.sh[:, L * r:L * r + L], T.sem["qarr%d" % r], T.sem.sent, pid, rid, mask)
    g.wait_ge(T.sem.sent, 2 * R * len(topo.engines(core, T.cores[d])))


def rank_program(g, core, T, topo):
    rank = T.rank_of(core)
    if rank is None:
        for k, c in enumerate(T.cores):
            if core in helpers(c, T, topo):
                helper_program(g, core, k, helpers(c, T, topo).index(core), T, topo)
        return
    N = len(T.cores)
    Q = {"v": g.vector, "a": g.scalar, "p": g.tensor, "g": g, "s": g.sync}
    own = {"v": "cv", "a": "ca", "p": "cp", "g": "cg"}
    clock = {e: {} for e in Q}
    count = {}
    waited = {}
    wr, rd = {}, {}

    def need(e, rec):
        sem, val, snap = rec[0], rec[1], rec[2]
        if clock[e].get(sem, 0) < val:
            Q[e].wait_ge(T.sem[sem], val)
            waited[sem] = max(waited.get(sem, 0), val)
            clock[e][sem] = val
        for k, x in snap.items():
            if clock[e].get(k, 0) < x:
                clock[e][k] = x

    def before(e, reads, writes):
        recs = []
        for k in reads:
            if k in wr:
                recs.append(wr[k])
            if k.startswith("P:"):
                recs += [x for x in rd.get(k, []) if x[3] != e]
        for k in writes:
            if k in wr and not (e == "p" and wr[k][3] == "p"):
                recs.append(wr[k])
            recs += rd.get(k, [])
        recs.sort(key=lambda x: -x[1])
        for x in recs:
            need(e, x)

    def after(rec, reads, writes):
        for k in reads:
            rd.setdefault(k, []).append(rec)
        for k in writes:
            wr[k] = rec
            rd[k] = []

    def op(e, fn, reads, writes):
        before(e, reads, writes)
        s = own[e]
        count[s] = count.get(s, 0) + 1
        fn().then_inc(T.sem[s], 1)
        after((s, count[s], dict(clock[e]), e), reads, writes)

    def dmas(e, sem, pairs, reads, writes):
        before(e, reads, writes)
        for o, i in pairs:
            count[sem] = count.get(sem, 0) + 16
            Q[e].dma_start(o, i).then_inc(T.sem[sem], 16)
        after((sem, count[sem], dict(clock[e]), "d"), reads, writes)

    def arrives(sem, n, writes):
        count[sem] = n
        after((sem, n, {}, "r"), [], writes)

    def send(items, reads):
        before("g", reads, [])
        tr = []
        for k, (c, src, dst, sem) in enumerate(items):
            eng = topo.engines(core, c)
            w = len(eng) // len(items)
            rid, pid = topo.addr(c, core)
            tr.append(RemoteDMATransfer(dst_ids=[DstId(rid=rid, pnc=pid)], dma_engine_mask=sum(1 << x for x in eng[k * w:(k + 1) * w]),
                                        remote_sem=T.sem[sem], src=src, dst=dst))
            count["sent"] = count.get("sent", 0) + w
        g.remote_dma_fused(tr, local_sem=T.sem.sent)

    def share(s, n):
        return len(topo.engines(T.cores[s], core)) // n

    V, A, PE = g.vector, g.scalar, g.tensor

    def ts(out, in0, s1, s2, o0, o1, reads, writes):
        if s2 is None:
            op("v", lambda: V.tensor_scalar(out, in0, s1, None, o0), reads, writes)
        else:
            op("v", lambda: V.tensor_scalar(out, in0, s1, s2, o0, o1), reads, writes)

    def tt(out, a, b, o, reads, writes):
        op("v", lambda: V.tensor_tensor(out, a, b, o), reads, writes)

    def cp(out, a, reads, writes):
        op("v", lambda: V.tensor_copy(out, a), reads, writes)

    def ms(ap, val, writes):
        op("v", lambda: V.memset(ap, val), [], writes)

    def scan(out, d0, d1, init, o0, o1, reads, writes):
        op("v", lambda: V.tensor_tensor_scan(out, d0, d1, init, o0, o1), reads, writes)

    def turn(out, in_, reads, writes):
        op("v", lambda: V.transpose(out, in_), reads, writes)

    def qz(q, s, t, reads, writes):
        op("v", lambda: V.quantize_mx(q, s, t), reads, writes)

    def mx(out, wq, ws_, xq, xs, start, stop, reads, writes):
        op("p", lambda: PE.matmul_mx(out, wq, ws_, xq, xs, start, stop), reads, writes)

    def act(out, in_, f, reads, writes, **kw):
        op("a", lambda: A.activation(out, in_, f, **kw), reads, writes)

    def iota(out, pat, base, cmul, writes, flt=False):
        if flt:
            op("g", lambda: g.iota(out, pat, base, cmul, allow_small_or_imprecise_dtypes=True), [], writes)
        else:
            op("g", lambda: g.iota(out, pat, base, cmul), [], writes)

    def scale(e, out, in_, c, reads, writes):
        if e == "v":
            ts(out, in_, c, None, Op.mult, None, reads, writes)
        else:
            act(out, in_, AF.Copy, reads, writes, scale=c)

    def move(e, out, in_, reads, writes):
        if e == "v":
            cp(out, in_, reads, writes)
        else:
            act(out, in_, AF.Copy, reads, writes)

    def fill(out, n, c, writes):
        act(out, T.one[:, 0:n], AF.Copy, ["one"], writes, scale=c)

    def bank(k, a, b):
        return T.ps[:, 512 * k + a:512 * k + b]

    def mk(name, a=0, b=C, step=1):
        o = C * MASKS.index(name)
        return T.mk[:, o + a:o + b:step]

    rcv = [(rank + 1) % N, (rank + 2) % N]
    snd = [(rank - 1) % N, (rank - 2) % N]
    run = {"a": (0, H), "b": (H, C)}
    top = {k: max(int(w[1:]) for w in ORDER.split() if w[0] == k) for k in "pb"}

    def slot_at(d):
        return 0 if rank == min((d - 1) % N, (d - 2) % N) else 1

    def qx_of(t, h, reads):
        a, b = run[h]
        qz(T.qx[:, a:b], T.sx[:, a:b], t[:, 4 * a:4 * b], reads, ["qx." + h])

    AV, AA, BV, SV, SA, CS = 0, 1, 4, 2, 3, 5

    def scores(k, a, b, names):
        mx(bank(k, 0, b - a), T.qur[:], T.sur[:], T.qx[:, a:b], T.sx[:, a:b], True, True, ["qur", "sur"] + names, ["P:%d" % k])

    def scores_a():
        scores(AV, 0, H, ["qx.a"])
        scores(AA, 0, H, ["qx.a"])

    def scores_b():
        scores(BV, H, C, ["qx.b"])
        for k, e in ((SV, "b"), (SA, "p")):
            if 16 * top[e] > H:
                scores(k, 0, 16 * top[e], ["qx.a", "qx.b"])

    def src_of(h):
        return (bank(AV, 0, H), "P:%d" % AV) if h == "a" else (bank(BV, 0, C - H), "P:%d" % BV)

    def hold1(h):
        a, b = run[h]
        tt(T.mm[:, a:b], src_of(h)[0], mk("mb", a, b), Op.min, [src_of(h)[1], "mb"], ["mm." + h])

    def hold2(h):
        a, b = run[h]
        scan(T.hh[:, a:b], mk("kk", a, b), T.mm[:, a:b], 0.0, Op.min, Op.max, ["kk", "mm." + h], ["hh." + h])

    def diag(h):
        a, b = run[h]
        tt(T.bt0[:, 4 * a:4 * b:4], src_of(h)[0], T.hh[:, a:b], Op.is_le, [src_of(h)[1], "hh." + h], ["bt0." + h])

    def lane(c):
        n = 18 - c
        return n // 4, n % 4

    def lview(c, a, b):
        t, k = lane(c)
        return T["bt%d" % t][:, 4 * a + k:4 * b:4]

    def lname(c):
        return "bt%d.%d" % lane(c)

    def hname(c):
        return "hh.a" if 16 * c < H else "hh.b"

    def pad(a, lo_):
        fill(T["bt%d" % a][:, 4 * lo_:4 * TW[a]], 4 * (TW[a] - lo_), 0.0, ["bt%d.%s" % (a, t) for t in "0123b"])

    def quant(t):
        w = TW[t]
        qz(T["qb%d" % t][:, 0:w], T["sb%d" % t][:, 0:w], T["bt%d" % t][:, 0:4 * w], ["bt%d.%s" % (t, k) for k in "0123ab"], ["qb%d" % t])

    def sums(t, start, stop):
        w = C if start else TW[t]
        mx(bank(CS, 0, w), T.qob[:], T.sob[:], T["qb%d" % t][:, 0:w], T["sb%d" % t][:, 0:w], start, stop, ["qob", "qb%d" % t], ["P:%d" % CS])

    def p1(c):
        o, k = 8 * c * (c - 1), AA if 16 * c <= H else SA
        act(T.sga[:, o:o + 16 * c], bank(k, 0, 16 * c), AF.Sign, ["P:%d" % k, hname(c)], ["sga.%d" % c], bias=T.hh[:, 16 * c + 15:16 * c + 16], scale=-1.0)

    def p2(c):
        o = 8 * c * (c - 1)
        act(lview(c, 0, 16 * c), T.sga[:, o:o + 16 * c], AF.Relu, ["sga.%d" % c], [lname(c), "rs.%d" % c], accum_out=T.rs[:, c:c + 1])

    def bits(c):
        k = AV if 16 * c <= H else SV
        ts(lview(c, 0, 16 * c), bank(k, 0, 16 * c), T.hh[:, 16 * c + 15:16 * c + 16], None, Op.is_lt, None, ["P:%d" % k, hname(c)], [lname(c)])

    def rsum(c):
        scan(T.rb[:, RP * c + RP - 8 * c:RP * c + RP], lview(c, 0, 8 * c), lview(c, 8 * c, 16 * c), T.rsd[:, 16 * c + 15:16 * c + 16], Op.add, Op.add,
             [lname(c), "rsd"], ["rb.%d" % c])

    def asum(c):
        act(T.jka[:, 8 * c * (c - 1):8 * c * (c + 1)], lview(c, 0, 16 * c), AF.Copy, [lname(c)], ["rs.%d" % c], accum_out=T.rs[:, c:c + 1])

    dmas("a", "ldu", [(T.ut[:], T.u[:])], [], ["ut"])
    dmas("s", "ldx", [(T.xt[:, 0:4 * H], T.x[:, 0:4 * H])], [], ["xt.a"])
    dmas("s", "ldy", [(T.xt[:, 4 * H:], T.x[:, 4 * H:])], [], ["xt.b"])
    dmas("s", "ldw", [(T.qw[:].bitcast(dt.uint8), T.wc[:]), (T.sw[:], T.ws[:]), (T.vt[:], T.v[:])], ["xt.a", "xt.b"], ["qw", "vt"])
    iota(T.li[:, 0:8], [[16, 8]], 0, 0, ["li.a"])
    iota(T.pi[:], [[0, 2]], 0, 1, ["pi"])
    iota(mk("km"), [[0, 18], [1, 16]], 0, 0, ["km"], True)
    iota(T.li[:, 10:18], [[1, 8]], 0, 0, ["li.b"])
    iota(T.c16[:], [[16, 18]], 0, 0, ["c16"], True)
    ms(T.one[:], 1.0, ["one"])

    def ones(in_, base, cmul, reads):
        op("g", lambda: g.affine_select(T.obt[:], in_, [[-16 * cmul, 8], [0, 64]], Op.is_ge, 0.0, base, cmul), reads, ["obt"])

    ones(T.one[:, 0:512], 0, 1, ["one"])
    ms(mk("kk"), BIG, ["kk"])
    cp(T.la[:], T.li[:, 0:8], ["li.a"], ["la"])
    ts(T.ti[:, 6:8], T.pi[:], 7, None, Op.bitwise_and, None, ["pi"], ["ti.6"])
    ts(T.ti[:, 0:1], T.pi[:, 0:1], 15, None, Op.bitwise_and, None, ["pi"], ["ti.0"])
    ts(T.ti[:, 1:2], T.pi[:, 0:1], 31, None, Op.bitwise_and, None, ["pi"], ["ti.1"])
    ts(T.ti[:, 2:3], T.pi[:, 0:1], 15, 2, Op.bitwise_and, Op.logical_shift_right, ["pi"], ["ti.2"])
    ts(T.ti[:, 3:4], T.pi[:, 0:1], 3, None, Op.bitwise_and, None, ["pi"], ["ti.3"])
    ts(T.lst[:, 0:2], T.ti[:, 6:8], 16.0, None, Op.mult, None, ["ti.6"], ["lc"])
    ms(mk("kk", 0, C, 16), -BIG, ["kk"])
    cp(T.pf[:, 0:4], T.ti[:, 0:4], ["ti.0", "ti.1", "ti.2", "ti.3"], ["pf"])
    ts(mk("eqm"), mk("km"), T.pf[:, 0:1], None, Op.is_equal, None, ["km", "pf"], ["eqm"])
    for a, lo_ in ((4, 0), (2, 112), (3, 48), (0, 240)):
        pad(a, lo_)
    cp(T.lb[:], T.li[:, 10:18], ["li.b"], ["lb"])
    qz(T.qu[:], T.su[:], T.ut[:], ["ut"], ["qu"])
    qx_of(T.xt, "a", ["xt.a"])
    act(T.sur[:], T.su[:].indirect(T.la[:]), AF.Copy, ["qu", "la"], ["sur"])
    act(T.suc[:], T.su[:].indirect(T.lst[:, 0:2]), AF.Copy, ["qu", "lc"], ["suc"])
    cp(T.qur[:].bitcast(dt.uint32), T.qu[:].bitcast(dt.uint32).indirect(T.la[:]), ["qu", "la"], ["qur"])
    scores_a()
    cp(T.quc[:].bitcast(dt.uint32), T.qu[:].bitcast(dt.uint32).indirect(T.lst[:, 0:2]), ["qu", "lc"], ["quc"])
    pad(1, 176)
    fill(mk("kz"), C, 512.0, ["kz"])
    fill(T.rs[:], 18, 0.0, ["rs.%d" % c for c in range(18)])
    act(mk("kz", 0, C, 16), T.c16[:], AF.Identity, ["c16"], ["kz"], scale=-1.0, bias=128.0)
    items = []
    for e in range(2):
        items.append((T.cores[snd[e]], T.quc[:, 0:8].bitcast(dt.uint8), T.qul[:, 32 * e:32 * e + 8].bitcast(dt.uint8), "uarr"))
        items.append((T.cores[snd[e]], T.suc[:], T.sul[:, 32 * e:32 * e + 32], "uarr"))
    send(items, ["quc", "suc"])
    arrives("uarr", 2 * share(rcv[0], 4) + 2 * share(rcv[1], 4), ["qul.0", "qul.1"])
    ts(mk("mb"), mk("eqm"), 2.0 * BIG, -BIG, Op.mult, Op.add, ["eqm"], ["mb"])
    qx_of(T.xt, "b", ["xt.b"])
    scores_b()
    ones(T.obt[:], 15, -1, ["obt"])

    def zeros(a):
        qz(T.qb4[:, a:a + 128], T.sb4[:, a:a + 128], T.bt4[:], ["bt4.%s" % k for k in "0123b"], ["qb4"])

    gaps = {"ha": lambda: zeros(128), "Ha": lambda: zeros(160),
            "q2": lambda: ts(mk("mi"), mk("eqm"), 1049600.0, -1024.0, Op.mult, Op.add, ["eqm"], ["mi"])}

    vps = ["vp.s"] + ["vp.d%d" % b for b in range(4)]

    def span(k):
        a, b = k.split("-")
        return int(a), int(b)

    def cols(name, a, b):
        return ["%s.%d" % (name, k) for k in range(max(a, 0) // 8, (b + 7) // 8)]

    def gather(k):
        a, b = span(k[1:])
        move(k[0], T.gp[:, 4 * a + 4:4 * b + 4], T.vp[:].indirect(T.lo[:, a // 4:b // 4]), vps + cols("lo", a, b), cols("gp", a, b))

    def blend(k):
        a, b = span(k)
        tt(T.zt[:, 4 * a:4 * b], T.gp[:, 4 * a + 4:4 * b + 4], T.gp[:, 4 * a:4 * b], Op.add, ["gp.z"] + cols("gp", a - 1, b), cols("zt", a, b))

    def pb_(h, t):
        return t if h == "a" else 4 + t

    def layer(h):
        a, b = run[h]
        qz(T.qz[:, a:b], T.sz[:, a:b], T.zt[:, 4 * a:4 * b], cols("zt", a, b), ["qz." + h])
        for t in range(4):
            mx(bank(pb_(h, t), 0, b - a), T.qw[:, 128 * t:128 * t + 128], T.sw[:, 128 * t:128 * t + 128], T.qz[:, a:b], T.sz[:, a:b], True, True,
               ["qw", "qz." + h], ["P:%d" % pb_(h, t)])

    def z32(k):
        a, b = span(k[1:])
        scale(k[0], T.zp[:, 4 * a:4 * b], T.zt[:, 4 * a:4 * b], 32.0, cols("zt", a, b), cols("zp", a, b))

    def state(k):
        h, t = k[0], int(k[1])
        a, b = run[h]
        tt(T.xp[:, 4 * a + t:4 * b:4], bank(pb_(h, t), 0, b - a), T.zp[:, 4 * a + t:4 * b:4], Op.add,
           ["P:%d" % pb_(h, t)] + cols("zp", a, b), ["xp.%s%d" % (h, t)])

    def back(k):
        e, h, t = k[0], k[1], int(k[2])
        a, b = run[h]
        scale(e, T.xn[:, 4 * a + t:4 * b:4], T.xp[:, 4 * a + t:4 * b:4], 2.0 ** -5, ["xp.%s%d" % (h, t)], ["xn.%s%d" % (h, t)])

    def xns(h):
        return ["xn.%s%d" % (h, t) for t in range(4)]

    def anew(h):
        qx_of(T.xn, h, xns(h))
        (scores_a if h == "a" else scores_b)()

    def inside(_):
        scan(T.rsd[:], mk("kz"), T.bt0[:, 0:4 * C:4], 512.0, Op.min, Op.add, ["kz", "bt0.a", "bt0.b"], ["rsd"])

    ends, rbs = T.rb[:, RP - 1:18 * RP:RP], ["rb.%d" % c for c in range(18)]

    def join(k):
        a, b = span(k)
        tt(T.rb[:, RP * a + RP - 1:RP * b:RP], T.rs[:, a:b], T.rsd[:, 16 * a + 15:16 * b:16], Op.add, ["rs.%d" % c for c in range(a, b)] + ["rsd"], rbs[a:b])

    def number(f):
        return lambda k: f(int(k))

    renew = {"G": gather, "B": blend, "L": layer, "Z": z32, "S": state, "K": back, "X": anew}

    for r in range(R):
        first, last = r == 0, r == R - 1
        hs = T.hs[:, 20 * r:20 * r + 18]
        qa, sa = T.qa[:, 128 * r:128 * r + 128], T.sa[:, 128 * r:128 * r + 128]
        ql, sl = T.ql[:, 192 * r:192 * r + 192], T.sl[:, 192 * r:192 * r + 192]
        xs, xnames = (T.xt, ["xt.a", "xt.b"]) if first else (T.xn, xns("a") + xns("b"))

        def spread(e, q):
            arrives("%s%d" % (("sca", "scb")[e], r), share(rcv[e], 2), ["sc%d.%d" % (r, e)])
            dmas(q, "%s%d" % (("rpa", "rpb")[e], r), [(T.rep[i:128:16, C * e:C * e + C], T.sc[2 * r + e]) for i in range(16)],
                 ["sc%d.%d" % (r, e)], ["rep.%d" % e])

        def tell(_):
            cp(hs, T.hh[:, 15:C:16], ["hh.a", "hh.b"], ["hs%d" % r])
            send([(T.cores[snd[e]], hs, T.sc[2 * r + e], "%s%d" % (("sca", "scb")[e], r)) for e in range(2)], ["hs%d" % r])
            iota(T.ww[:], [[0, 384]], -512, 0, ["ww"], True)
            spread(0, "s")
            if first:
                iota(T.jv[:], [[1, C]], 0, 0, ["jv"], True)
                iota(mk("mi4"), [[0, 72], [1, 4]], 0, 0, ["mi4"], True)
                iota(T.li[:, 26:38], [[1, 6], [0, 2]], 0, 0, ["li.d"])
                iota(T.li[:, 50:54], [[32, 4]], 0, 0, ["li.e"])
                iota(T.li[:, 54:66], [[192, 2], [32, 3], [96, 2]], 0, 0, ["li.f"])
                iota(T.idn[:], [[16, 2], [32, 3], [1, 16]], 0, 0, ["idn"], True)
                iota(T.ja[:], [[16, 6]], 0, 0, ["ja"], True)

        done = []

        def column_sums(t):
            quant(t)
            if first and not done:
                qz(T.qob[:], T.sob[:], T.obt[:], ["obt"], ["qob"])
            done.append(t)
            sums(t, len(done) == 1, len(done) == len(TW))

        steps = {"h": hold1, "H": hold2, "D": diag, "e": tell, "p": number(p1), "P": number(p2), "b": number(bits), "a": number(asum),
                 "s": number(rsum), "d": inside, "q": number(column_sums), "j": join,
                 "x": lambda k: scan(T.ext[:], mk("mi"), bank(CS, 0, C), 0.0, Op.add, Op.min, ["mi", "P:%d" % CS], ["ext"])}
        for w in ORDER.split():
            if w[0] in steps:
                steps[w[0]](w[1:])
            elif not first:
                renew[w[0]](w[1:])
            if first and w in gaps:
                gaps[w]()
        if first:
            act(T.pf[:, 5:6], T.pf[:, 0:1], AF.Identity, ["pf"], ["pf.q2"], scale=-1025.0, bias=15503.0)
            act(mk("m4"), mk("mi4"), AF.Abs, ["mi4", "pf"], ["m4"], scale=-1.0, bias=T.pf[:, 2:3])
            act(T.pf[:, 8:9], T.pf[:, 3:4], AF.Identity, ["pf"], ["pf.8"], scale=0.25, bias=3072.0)
            act(T.pf[:, 7:8], T.pf[:, 3:4], AF.Identity, ["pf"], ["pf.ql"], scale=0.25, bias=191.0)
            act(mk("eq4"), mk("m4"), AF.Relu, ["m4"], ["eq4"], scale=-1.0, bias=1.0)
            act(T.pf[:, 6:7], T.pf[:, 2:3], AF.Identity, ["pf", "pf.8"], ["pf.q4"], scale=-1024.0, bias=T.pf[:, 8:9])
            fill(T.at[:, 4 * L:], 128, 0.0, ["at.z"])
        spread(1, "s" if first else "a")
        if first:
            cp(T.lst[:, 26:38], T.li[:, 26:38], ["li.d"], ["lst.d"])
        tt(T.rkf[:], T.ext[:, 15:C:16], T.rb[:, RP - 1:18 * RP:RP], Op.subtract, ["ext"] + ["rb.%d" % c for c in range(18)], ["rkf"])
        if first:
            act(mk("mi4"), mk("eq4"), AF.Identity, ["eq4"], ["mi4"], scale=1049600.0, bias=-1024.0)
            act(T.ngn[:], T.jv[:, 0:192], AF.Identity, ["jv"], ["ngn"], scale=-1.0, bias=-64.0)
            fill(T.pw[:, 0:16], 16, 1.0 / 16, ["pw.a"])
            act(T.pw[:, 16:32], mk("eqm", 0, 16), AF.Copy, ["eqm"], ["pw.b"], scale=-1.0)
            act(T.pw[:, 48:52], mk("eq4", 0, 4), AF.Copy, ["eq4"], ["pw.c"], scale=-1.0)
            act(T.idn[:], T.idn[:], AF.Copy, ["idn"], ["idn"], scale=1.0 / 128)
            iota(T.st[:, 1:2 * C:2], [[0, C]], 512, 0, ["st.z"], True)
            iota(mk("mb8", 1, 2 * C, 2), [[0, C]], -512, 0, ["mb8"], True)
            for h in range(2):
                op("g", lambda: g.affine_select(T.et[:, EW * h:EW * h + EW], T.one[:], [[1, EW]], Op.is_equal, 0.0, -2 - h, -4), ["one"], ["et.%d" % h])

        def theirs(e):
            o = 128 * e
            if first:
                act(T.su2[:, o:o + 128], T.sul[:, 32 * e:32 * e + 8].indirect(T.lb[:]), AF.Copy, ["qul.%d" % e, "lb"], ["su2.%d" % e])
                cp(T.qu2[:, o:o + 128].bitcast(dt.uint32), T.qul[:, 32 * e:32 * e + 8].bitcast(dt.uint32).indirect(T.lb[:]),
                   ["qul.%d" % e, "lb"], ["qu2.%d" % e])

        ts(T.rko[:], T.rkf[:], T.pf[:, 5:6], None, Op.add, None, ["rkf", "pf.q2"], ["rko"])
        if first:
            ts(T.lst[:, 50:66], T.li[:, 50:66], T.pf[:, 1:2], None, Op.add, None, ["li.e", "li.f", "pf"], ["lst.e"])
        cp(T.cm[:, 96:384].indirect(T.rko[:]), T.jv[:], ["rko", "jv"], ["cm"])
        theirs(0)
        scan(T.ex2[:, 0:L], mk("mi4", 0, L), T.cm[:, 96:192], 0.0, Op.add, Op.min, ["mi4", "cm"], ["ex2.a"])
        theirs(1)
        ts(T.oro[:, 0:24], T.ex2[:, 3:L:4], T.pf[:, 6:7], 4.0, Op.add, Op.mult, ["ex2.a", "pf.q4"], ["oro.a"])
        if first:
            ts(T.ja[:], T.ja[:], T.pf[:, 0:1], 1.0 / 128, Op.add, Op.mult, ["ja", "pf"], ["ja"])
        for k, e in enumerate("va"):
            move(e, T.at[:, 192 * k:192 * k + 192], xs[:].indirect(T.oro[:, 12 * k:12 * k + 12]), xnames + ["oro.a"], ["at.%d" % k])
        if first:
            scan(T.pw[:, 32:48], T.pw[:, 0:16], T.pw[:, 16:32], 0.0, Op.mult, Op.min, ["pw.a", "pw.b"], ["pw"])
        qz(qa, sa, T.at[:], ["at.z", "at.0", "at.1"], ["qa%d" % r])
        hands = helpers(core, T, topo)
        send([(c, T.qa[:, 128 * r:128 * r + L].bitcast(dt.uint8), T.qh[:, L * r:L * r + L].bitcast(dt.uint8), "harr%d" % r) for c in hands], ["qa%d" % r])
        send([(c, T.sa[:, 128 * r:128 * r + L], T.sh[:, L * r:L * r + L], "harr%d" % r) for c in hands], ["qa%d" % r])
        arrives("qarr%d" % r, sum(2 * len(topo.engines(helpers(T.cores[snd[e]], T, topo)[e], core)) for e in range(2)), ["ql%d" % r])
        for e in range(2):
            o = 128 * e
            mx(bank(4 + e, 0, 128), T.qu2[:, o:o + 128], T.su2[:, o:o + 128], qa, sa, True, True,
               ["qu2.%d" % e, "su2.%d" % e, "qa%d" % r], ["P:%d" % (4 + e)])
        if first:
            act(mk("mb8", 0, 2 * C, 2), mk("eq4"), AF.Identity, ["eq4"], ["mb8"], scale=2.0 * BIG, bias=-BIG)
            fill(T.kt[:, 0:1], 1, -96.0, ["kt.z"])
            fill(T.kt[:, 97:98], 1, 0.0, ["kt.y"])
        scan(T.ex2[:, L:C], mk("mi4", L, C), T.cm[:, 192:384], 0.0, Op.add, Op.min, ["mi4", "cm"], ["ex2.b"])
        ts(T.oro[:, 24:72], T.ex2[:, L + 3:C:4], T.pf[:, 6:7], 4.0, Op.add, Op.mult, ["ex2.b", "pf.q4"], ["oro.b"])
        for e in range(2):
            tt(T.ma[:, L * e:L * e + L], bank(4 + e, 0, L), mk("mb", 0, L), Op.min, ["P:%d" % (4 + e), "mb"], ["ma.%d" % e])
        for e in range(2):
            scan(T.ha[:, L * e:L * e + L], mk("kk", 0, L), T.ma[:, L * e:L * e + L], 0.0, Op.min, Op.max, ["kk", "ma.%d" % e], ["ha.%d" % e])
        END = 6 * 143

        def a1(c):
            act(T.sgp[:, C * c:C * c + C], T.rep[:, 0:C], AF.Sign, ["rep.0", "ha.0"], ["sgp.%d" % c],
                bias=T.ha[:, 16 * c + 15:16 * c + 16], scale=-1.0)

        def a2(c):
            act(T.jkp[:, C * c:C * c + C], T.sgp[:, C * c:C * c + C], AF.Sign, ["sgp.%d" % c], ["y0.%d" % c], scale=-1.0, bias=-0.5,
                accum_out=T.y0[:, END + c:END + c + 1])

        def vb(k):
            e, c = k // 6, k % 6
            ts(T.pb[:, C * k:C * k + C], T.rep[:, C * e:C * e + C], T.ha[:, L * e + 16 * c + 15:L * e + 16 * c + 16], 2.0, Op.is_gt, Op.mult,
               ["rep.%d" % e, "ha.%d" % e], ["pb.%d" % k])

        def vs(k):
            e, c, o = k // 6, k % 6, C * k
            scan((T.y0, T.y1)[e][:, c:6 * 144:6], T.pb[:, o:o + 144], T.pb[:, o + 144:o + C], -288.0, Op.add, Op.add, ["pb.%d" % k], ["y%d.%d" % (e, c)])

        o = 16 * r
        fm = [T.fm[:, 2 * o + 16 * h:2 * o + 16 * h + 3] for h in range(2)]
        fl = [T.fl[:, 2 * o + 16 * h:2 * o + 16 * h + 6] for h in range(2)]
        fmn, fln = ["fm%d%d" % (r, h) for h in range(2)], ["fl%d%d" % (r, h) for h in range(2)]

        def final(h):
            tt(fm[h], T.y0[:, END + h:END + 6:2], T.y1[:, END + h:END + 6:2], Op.max, ["y%d.%d" % (e, c) for e in range(2) for c in range(h, 6, 2)], [fmn[h]])
            at = [2 * o + 16 * h + 3 * slot_at(d) for d in rcv]
            send([(T.cores[d], fm[h], T.fl[:, a:a + 3], "farr%d%d" % (r, h)) for d, a in zip(rcv, at)], [fmn[h]])
            arrives("farr%d%d" % (r, h), share(snd[0], 2) + share(snd[1], 2), [fln[h]])

        def unpacker(b):
            o = EW * (b % 2) + 2 - 2 * (b // 2)
            if first:
                qz(T.qe[:, 128 * b:128 * b + 128], T.se[:, 128 * b:128 * b + 128], T.et[:, o:o + 512], ["et.%d" % (b % 2)], ["qe.%d" % b])

        def count_a(k, row, n, col, names, out, name):
            act(T.jkq[:, L * k:L * k + L], row, AF.Sign, names, [name], bias=col, scale=-1.0, accum_out=out)

        def count_v(k, row, col, names):
            ts(T.kb[:, L * k:L * k + L] if k else T.kt[:, 1:97], row, col, 2.0, Op.is_lt, Op.mult, names, ["kb.%d" % k])

        def sum_v(k, out, init, name, reads=[]):
            scan(out, T.kb[:, L * k:L * k + 48], T.kb[:, L * k + 48:L * k + L], init, Op.add, Op.add, ["kb.%d" % k] + reads, [name])

        def repeat(e, out, window, a, b, reads, writes):
            in_ = window.indirect(T.lst[:, 26 + a:26 + b])
            if e == "v":
                ts(out, in_, 96.0, 0.0, Op.add, Op.max, reads + ["lst.d"], writes)
            else:
                act(out, in_, AF.Relu, reads + ["lst.d"], writes, bias=96.0)

        f2, ka, po = T.so[:, 0:6], T.so[:, 6:12], C * r
        ownv = len([w for w in QUEUE.split() if w[0] == "w"])

        def own_repeat(k):
            e, h, a, b = k[0], int(k[1]), int(k[2]), int(k[3])
            repeat(e, T.eo[:, L * h + 16 * a:L * h + 16 * b], fm[h], a, b, [fmn[h]], ["eo.%d%d" % (h, j) for j in range(a, b, 2)])

        def own_small(k):
            k, h = k[0], int(k[1:] or 0)
            if k == "f":
                act(T.so[:, h:6:2], fm[h], AF.Relu, [fmn[h]], ["f2.%d" % h], bias=96.0)
            elif k == "k":
                tt(ka, f2, T.ja[:], Op.add, ["f2.0", "f2.1", "ja"], ["ka"])
            elif k == "a":
                ts(T.so[:, 12:18], f2, 382.0, -191.0, Op.min, Op.add, ["f2.0", "f2.1"], ["b3"])
            elif k == "v":
                ts(T.so[:, 18:24], f2, 382.0, -286.0, Op.min, Op.add, ["f2.0", "f2.1"], ["b4"])
            elif k == "t":
                turn(T.ro[:, L * h:L * h + L], T.eo[:, L * h:L * h + L], ["eo.%d%d" % (h, j) for j in (0, 2, 4)], ["ro.%d" % h])
            elif k == "y":
                tt(T.kyo[:, 48 * h:48 * h + 48], T.ro[:, L * h:L * h + L].indirect(T.lst[:, 50:53]), T.idn[:, 48 * h:48 * h + 48], Op.add,
                   ["ro.%d" % h, "lst.e", "idn"], ["kyo.%d" % h])
            else:
                tt(T.pm[:, po + C - 6 + ownv:po + C], T.rh[:, ownv:6], T.so[:, 12 + ownv:18], Op.add, ["rh.%d" % c for c in range(ownv, 6)] + ["b3"], ["pm%d.a" % r])

        def own_count(c):
            if c < ownv:
                count_v(12 + c, T.kyo[:], T.so[:, 6 + c:7 + c], ["kyo.0", "kyo.1", "ka"])
            else:
                count_a(12 + c, T.kyo[:], L, T.so[:, 6 + c:7 + c], ["kyo.0", "kyo.1", "ka"], T.rh[:, c:c + 1], "rh.%d" % c)

        def own_sum(c):
            sum_v(12 + c, T.pm[:, po + c:po + C:6], T.so[:, 18 + c:19 + c], "pm%d.%d" % (r, c), ["b4"])

        def own_send(_):
            send([(T.cores[d], T.pm[:, po + C - 6:po + C], T.pl[:, o + 6 * slot_at(d):o + 6 * slot_at(d) + 6], "parr%d" % r) for d in rcv],
                 ["pm%d.a" % r] + ["pm%d.%d" % (r, c) for c in range(ownv)])
            arrives("parr%d" % r, share(snd[0], 2) + share(snd[1], 2), ["pl%d" % r])

        def beside(b):
            unpacker(b)
            if first and b == 3:
                act(mk("m4"), mk("eq4"), AF.Identity, ["eq4"], ["m4"], scale=-16.0, bias=16.0)
                scan(T.pw[:, 52:56], T.pw[:, 0:4], T.pw[:, 48:52], 0.0, Op.mult, Op.min, ["pw.a", "pw.c"], ["pw4"])
            if last and b == 0:
                qz(T.qv[:], T.sv[:], T.vt[:], ["vt"], ["qv"])

        def pick(k):
            e, q = k[0], int(k[1])
            out, in_, c = T.xr[:, 48 * q:48 * q + 48], T.r2[:, L * q:L * q + L].indirect(T.lst[:, 50:53]), 2.0 * (q // 2) - 193.0
            if e == "v":
                ts(out, in_, c, None, Op.add, None, ["r2.%d" % q, "lst.e"], ["xr.%d" % q])
            else:
                act(out, in_, AF.Identity, ["r2.%d" % q, "lst.e"], ["xr.%d" % q], bias=c)

        def came(k):
            e, q = k[0], int(k[1])
            repeat(e, T.ee[:, L * q:L * q + L], fl[q % 2], 6 * (q // 2), 6 * (q // 2) + 6, [fln[q % 2]], ["ee.%d" % q])

        def cross(k):
            c = int(k[1:])
            h = 1 - c // 6
            row, names = T.xr[:, L * h:L * h + L], ["xr.%d" % (2 * h), "xr.%d" % (2 * h + 1), "sc2.%d" % (c % 2)]
            if k[0] == "v":
                count_v(c, row, T.sc2[:, c:c + 1], names)
            else:
                count_a(c, row, L, T.sc2[:, c:c + 1], names, T.rk[:, 48 * c + 47:48 * c + 48], "rk.%d" % c)

        def cross_sum(c):
            if c:
                sum_v(c, T.rk[:, 48 * c:48 * c + 48], -96.0, "rk.%d" % c)
            else:
                scan(T.plf[:, 0:49], T.kt[:, 0:49], T.kt[:, 49:98], T.pl[:, o:o + 1], Op.add, Op.add, ["kb.0", "kt.z", "kt.y", "pl%d" % r], ["plf.0"])

        steps = {"g": number(a1), "G": number(a2), "b": number(vb), "B": number(vs), "F": number(final), "O": own_repeat,
                 "n": own_small, "r": number(own_count), "w": number(own_sum), "P": own_send, "U": number(beside), "E": came,
                 "s": number(lambda h: ts(T.sc2[:, h:12:2], fl[h], -96.0, -192.0, Op.add, Op.max, [fln[h]], ["sc2.%d" % h])),
                 "t": number(lambda q: turn(T.r2[:, L * q:L * q + L], T.ee[:, L * q:L * q + L], ["ee.%d" % q], ["r2.%d" % q])),
                 "x": pick, "c": cross, "d": number(cross_sum),
                 "J": lambda k: tt(T.plf[:, 97:12 * 49:49], T.rk[:, 95:12 * 48:48], T.pl[:, o + 1:o + 12], Op.add, ["rk.%d" % c for c in range(1, 12)] + ["pl%d" % r], ["plf"])}
        for w in QUEUE.split():
            steps[w[0]](w[1:])
        ts(T.plo[:], T.plf[:, 48:12 * 49:49], 384.0, 0.5, Op.add, Op.mult, ["plf", "plf.0"], ["plo"])
        cp(T.ww[:].indirect(T.plo[:]), T.ngn[:], ["plo", "ngn"], ["ww"])
        scale("a", T.vp[:, 768:1536], xs[:].indirect(T.oro[:, 24:72]), 0.5, xnames + ["oro.b"], ["vp.s"])
        for b in range(4):
            mx(bank(b, 0, 192), T.qe[:, 128 * b:128 * b + 128], T.se[:, 128 * b:128 * b + 128], ql, sl, True, True,
               ["qe.%d" % b, "ql%d" % r], ["P:%d" % b])
        act(T.gp[:, 0:4], T.vp[:, 768:772], AF.Copy, ["vp.s"], ["gp.z"])
        for b in range(4):
            scale("a", T.vp[:, b:768:4], bank(b, 0, 192), 0.5, ["P:%d" % b], ["vp.d%d" % b])

        ts(T.flg[:], T.ww[:, 0:C], -300.0, None, Op.is_lt, None, ["ww"], ["flg"])
        scan(T.exw[:, 0:C], mk("m4"), T.ww[:, 0:C], 0.0, Op.mult, Op.min, ["m4", "ww"], ["exw.0"])
        scan(T.st[:, 0:2 * C:2], T.flg[:], T.flg[:], 0.0, Op.add, Op.max, ["flg"], ["st"])
        ts(T.st[:, 7:2 * C:8], T.exw[:, 3:C:4], T.pw[:, 55:56], -255.0, Op.mult, Op.add, ["exw.0", "pw4", "st.z"], ["st.w"])
        if last:
            scan(T.exw[:, C:2 * C], mk("m16"), T.ww[:, 0:C], 0.0, Op.mult, Op.min, ["m16", "ww"], ["exw.1"])
        parts = ((0, FIRST), (FIRST, C))
        for a, b in parts:
            scan(T.exs[:, 2 * a:2 * b], mk("mb8", 2 * a, 2 * b), T.st[:, 2 * a:2 * b], 0.0, Op.max, Op.min, ["mb8", "st", "st.w", "st.z"], ["exs.%d" % a])
        for a, b in parts:
            ts(T.lo[:, a // 4:b // 4], T.exs[:, 2 * a + 7:2 * b:8], T.pf[:, 7:8], 4.0, Op.add, Op.mult, ["exs.%d" % a, "pf.ql"], cols("lo", a, b))
            if last and a == 0:
                scan(T.exs[:, 2 * C:3 * C], mk("mb"), T.st[:, 0:2 * C:2], 0.0, Op.max, Op.min, ["mb", "st"], ["exs.1"])
        if r == R - 2:
            act(mk("m16"), mk("eqm"), AF.Identity, ["eqm"], ["m16"], scale=-16.0, bias=16.0)

    def listed(k):
        if k == "w":
            ts(T.wa[:], T.exw[:, C + 15:2 * C:16], T.pw[:, 47:48], -255.0, Op.mult, Op.add, ["exw.1", "pw"], ["wa"])
        elif k == "f":
            tt(T.lf[:], T.wa[:], T.exs[:, 2 * C + 15:3 * C:16], Op.min, ["wa", "exs.1"], ["lf"])
        else:
            ts(T.lo[:, 72:90], T.lf[:], 191.0, None, Op.add, None, ["lf"], ["lo.s"])

    def closing(h):
        qx_of(T.xn, h, xns(h))
        if h == "a":
            mx(bank(0, 0, H), T.qv[:], T.sv[:], T.qx[:, 0:H], T.sx[:, 0:H], True, True, ["qv", "qx.a"], ["P:0"])
            dmas("s", "stp", [(T.oc[:, 0:4 * H], T.qx[:, 0:H].bitcast(dt.uint8))], ["qx.a"], [])

    def lists_out(k):
        if k == "0":
            act(T.cm[:, 0:192], T.jv[:, 0:192], AF.Identity, ["jv"], ["cm"], bias=288.0)
        elif k == "1":
            act(T.lsb[:, C:480], T.r2[:].indirect(T.lst[:, 54:66]), AF.Copy, ["r2.%d" % q for q in range(4)] + ["lst.e"], ["lsb.b"], scale=0.5)
        else:
            act(T.lsb[:, 0:C], T.cm[:].indirect(T.lo[:, 72:90]), AF.Copy, ["cm", "lo.s"], ["lsb.a"])
            dmas("a", "stl", [(T.ls[:], T.lsb[0:128:16, :])], ["lsb.a", "lsb.b"], [])

    def y_a(_):
        act(T.yb[:, 0:H], bank(0, 0, H), AF.Copy, ["P:0"], ["yb.0"])
        dmas("a", "stz", [(T.y[:, 0:H], T.yb[:, 0:H])], ["yb.0"], [])

    renew.update({"X": closing, "l": listed, "o": lists_out, "y": y_a})
    for w in LAST.split():
        renew[w[0]](w[1:])

    mx(bank(1, 0, C - H), T.qv[:], T.sv[:], T.qx[:, H:C], T.sx[:, H:C], True, True, ["qv", "qx.b"], ["P:1"])
    dmas("s", "sto", [(T.oc[:, 4 * H:], T.qx[:, H:C].bitcast(dt.uint8))] + [(T.osc[4 * k:4 * k + 4, :], T.sx[32 * k:32 * k + 4, :]) for k in range(4)],
         ["qx.a", "qx.b"], [])
    cp(T.yb[:, H:C], bank(1, 0, C - H), ["P:1"], ["yb.1"])
    dmas("s", "sty", [(T.y[:, H:C], T.yb[:, H:C])], ["yb.1"], [])
    stores = ("stl", "stp", "sto", "stz", "sty")
    for s in SEMAPHORES:
        if count.get(s, 0) > waited.get(s, 0) and s not in stores:
            g.wait_ge(T.sem[s], count[s])
    for s in stores:
        g.wait_ge(T.sem[s], count[s])
